import numpy as np
import ml_dtypes


def mxq(x, axis, fmt="e4m3"):
    dtype, down = {"e4m3": (ml_dtypes.float8_e4m3fn, 7), "e5m2": (ml_dtypes.float8_e5m2, 14)}[fmt]
    v = np.moveaxis(np.asarray(x, np.float32).astype(ml_dtypes.bfloat16).astype(np.float64), axis, -1)
    blocks = v.reshape(v.shape[:-1] + (-1, 32))
    amax = np.abs(blocks).max(-1, keepdims=True)
    byte = np.maximum(np.where(amax > 0, np.frexp(amax)[1] - 1 + 127, 0) - down, 1)
    scale = np.exp2(byte - 127.0)
    codes = (blocks / scale).astype(np.float32).astype(dtype).astype(np.float64)
    return np.moveaxis((codes * scale).reshape(v.shape), -1, axis)


WIDE = False


def mx_kscale(k):
    if not WIDE:
        return np.ones(k)
    levels = np.array([10, -10, 5, -5, 0])
    if k % 512:
        return np.exp2(np.random.permutation(np.resize(levels, k // 32))).repeat(32)
    a = np.empty((k // 512, 16))
    for p in range(k // 512):
        a[p, :8] = np.random.permutation(np.resize(levels, 8))
        for g in range(8):
            far = levels[np.abs(levels - a[p, g]) >= 10]
            a[p, g + 8] = far[np.random.randint(len(far))]
    return np.exp2(a.ravel()).repeat(32)


def f64(x):
    return np.asarray(x).astype(np.float64)


def striped(idx):
    return np.tile(idx.reshape(-1, 16).T, (8, 1)).astype(np.uint16)


def unstriped(offs):
    return offs[:16].T.reshape(-1).astype(np.int64)


E2M1 = np.array([0.0, 0.5, 1.0, 1.5, 2.0, 3.0, 4.0, 6.0, -0.0, -0.5, -1.0, -1.5, -2.0, -3.0, -4.0, -6.0])


def pack_weight(w, fmt):
    k, n = w.shape
    w = f64(np.asarray(w, np.float32).astype(ml_dtypes.bfloat16)).reshape(k // 32, 32, n)
    amax = np.abs(w).max(1)
    if fmt == "e4m3":
        byte = np.frexp(amax)[1] - 1 + 127 - 7
    else:
        mant, ex = np.frexp(amax / 6.0)
        byte = np.where(mant > 0.5, ex, ex - 1) + 127
    byte = np.clip(np.where(amax > 0, byte, 1), 1, 254)
    scaled = (w * np.exp2(127.0 - byte)[:, None, :]).reshape(k, n).astype(np.float32)
    by_word = np.ascontiguousarray(scaled.reshape(k // 512, 128, 4, n).transpose(0, 1, 3, 2))
    if fmt == "e4m3":
        words = by_word.astype(ml_dtypes.float8_e4m3fn).view(np.uint8)
    else:
        c = by_word.astype(ml_dtypes.float4_e2m1fn).view(np.uint8) & 0xF
        words = (c[..., 0::2] | (c[..., 1::2] << 4)).reshape(k // 512, 128, 2 * n)
    return np.ascontiguousarray(words), np.ascontiguousarray(byte.astype(np.uint8).reshape(k // 512, 16, n))


def unpack_weight(words, scales, fmt):
    g, _, n = scales.shape
    words = np.ascontiguousarray(words).reshape(g, 128, n, -1)
    if fmt == "e4m3":
        vals = words.view(ml_dtypes.float8_e4m3fn).astype(np.float64)
    else:
        nib = np.empty((g, 128, n, 4), np.uint8)
        nib[..., 0::2] = words & 0xF
        nib[..., 1::2] = words >> 4
        vals = E2M1[nib]
    vals = vals * np.repeat(np.exp2(scales.astype(np.float64) - 127.0), 8, axis=1)[..., None]
    return vals.transpose(0, 1, 3, 2).reshape(g * 512, n)


def gelu(v):
    return 0.5 * v * (1.0 + np.tanh(np.sqrt(2.0 / np.pi) * (v + 0.044715 * v**3)))


K, T, S, P, H, N = 1024, 4096, 1024, 512, 1024, 768

def setup_inputs():
    n = np.random.standard_normal
    s = mx_kscale(K)[:, None]
    u = mx_kscale(H)[:, None]
    tab_words, tab_scales = pack_weight(n((K, T)) * s, "e4m3")
    w1 = n((K, H)) / np.sqrt(K) / s * (u ** 3).T
    w2_words, w2_scales = pack_weight(n((K, H)) / np.sqrt(K) / s * u.T, "e2m1")
    w3_words, w3_scales = pack_weight((n((H, N)) + 0.06) / np.sqrt(H) / u, "e4m3")
    return {
        "tab_words": tab_words, "tab_scales": tab_scales,
        "offs": striped(np.random.permutation(T)[:S]),
        "pos1": striped(np.random.permutation(S)[:P]),
        "pos2": striped(np.random.permutation(S)[:P]),
        "pos3": striped(np.random.permutation(S)[:P]),
        "w1": w1.astype(np.float32),
        "w2_words": w2_words, "w2_scales": w2_scales,
        "half": (np.exp(0.2 * n(H)) * u[:, 0] ** 2).astype(np.float32),
        "w3_words": w3_words, "w3_scales": w3_scales,
        "ded": (0.5 * np.exp(0.3 * n(N))).astype(np.float32),
    }

def reference(tab_words, tab_scales, offs, pos1, pos2, pos3, w1, w2_words, w2_scales,
              half, w3_words, w3_scales, ded):
    v = unpack_weight(tab_words, tab_scales, "e4m3")[:, unstriped(offs)]
    hail = mxq(f64(w1), 0, "e4m3").T @ v
    back = unpack_weight(w2_words, w2_scales, "e2m1").T @ v
    field = np.abs(hail[:, unstriped(pos1)])
    near = np.square(back[:, unstriped(pos2)])
    base = back[:, unstriped(pos3)]
    z = field / (f64(half)[:, None] + near) - base
    loss = unpack_weight(w3_words, w3_scales, "e4m3").T @ mxq(z, 0, "e4m3")
    return np.maximum(loss, f64(ded)[:, None])

@@ -1,0 +1,298 @@
+from contextlib import ExitStack
+
+import concourse.mybir as mybir
+
+K, T, S, M, H, N = 1024, 4096, 1024, 512, 1024, 768
+FLOPS = 2 * K * H * S * 2 + 2 * H * N * M
+
+F32 = mybir.dt.float32
+BF16 = mybir.dt.bfloat16
+I32 = mybir.dt.int32
+U32 = mybir.dt.uint32
+U16 = mybir.dt.uint16
+U8 = mybir.dt.uint8
+FP8X4 = mybir.dt.float8_e4m3fn_x4
+FP4X4 = mybir.dt.float4_e2m1fn_x4
+ACT = mybir.ActivationFunctionType
+ALU = mybir.AluOpType
+
+P = 128
+PACK = 4
+KP = P * PACK
+BANK = 512
+PASSES = K // KP
+GROUPS = H // KP
+SLICES = GROUPS * PACK
+NT = N // P
+HALF_M = M // 2
+
+
+def tile_list_hail_indemnity_kernel(tc, tab_words, tab_scales, offs, pos1, pos2, pos3, w1,
+                                              w2_words, w2_scales, half, w3_words, w3_scales, ded, out):
+    nc = tc.nc
+    with ExitStack() as ctx:
+        keep = ctx.enter_context(tc.tile_pool(name="keep", bufs=1))
+        work = ctx.enter_context(tc.tile_pool(name="work", bufs=3))
+        psum = ctx.enter_context(tc.psum_pool(name="psum", bufs=8))
+
+        offs_t = keep.tile([P, S // 16], U16, name="offs_t")
+        nc.sync.dma_start(offs_t[:], offs)
+
+        warm = keep.tile([P, 8], F32, name="warm")
+        nc.vector.memset(warm[:], 1.0)
+        tab_rows = keep.tile([P, T // 4], I32, name="tab_rows", align_bytes=64)
+        nc.vector.memset(tab_rows[:], 0)
+        nc.scalar.dma_start(tab_rows[0:P:4, :], tab_scales.rearrange("a q t -> (a q) t").bitcast(I32))
+        w2s_raw = keep.tile([P, PASSES * H // 4], I32, name="w2s_raw", tag="early", align_bytes=64)
+        nc.vector.memset(w2s_raw[:], 0)
+        for q in range(4):
+            nc.scalar.dma_start(
+                w2s_raw[32 * q:32 * q + 4, :].rearrange("r (a c) -> r a c", a=PASSES),
+                w2_scales.bitcast(I32)[:, 4 * q:4 * q + 4, :].rearrange("a r c -> r a c"))
+        warm2 = keep.tile([P, 8], F32, name="warm2")
+        nc.scalar.activation(warm2[:], warm[:], ACT.Abs_reciprocal_sqrt)
+        v_planes = [keep.tile([P, S // 4], I32, name="v_plane%d" % a, align_bytes=64) for a in range(PASSES)]
+        for a in range(PASSES):
+            nc.vector.memset(v_planes[a][:], 0)
+        w3s = keep.tile([P, PASSES * N // 4], I32, name="w3s", align_bytes=64)
+        nc.vector.memset(w3s[:], 0)
+
+        tab_w = [keep.tile([P, T], I32, name="tab_w%d" % a, align_bytes=64) for a in range(PASSES)]
+        nc.sync.dma_start(tab_w[0][:], tab_words[0].rearrange("p t i -> p (t i)").bitcast(I32))
+        w2_raw = keep.tile([P, PASSES, H // 2], I32, name="w2_raw", align_bytes=64)
+        nc.sync.dma_start(w2_raw[:], w2_words.bitcast(I32).rearrange("a p c -> p a c"))
+        nc.sync.dma_start(tab_w[1][:], tab_words[1].rearrange("p t i -> p (t i)").bitcast(I32))
+
+        w1_raw = {}
+
+        def load_w1(b):
+            for a in range(PASSES):
+                w1_raw[a, b] = keep.tile([P, PACK, KP], F32, name="w1_raw%d%d" % (a, b),
+                                         tag="early" if (a, b) == (0, 0) else "w1_raw%d%d" % (a, b), align_bytes=64)
+                nc.sync.dma_start(
+                    w1_raw[a, b][:],
+                    w1[a * KP:(a + 1) * KP, b * KP:(b + 1) * KP].rearrange("(p j) c -> p j c", j=PACK))
+
+        pos_t = []
+        for name, src in (("pos2_t", pos2), ("pos1_t", pos1), ("pos3_t", pos3)):
+            t_ = keep.tile([P, M // 16], U16, name=name)
+            pos_t.append((t_, src))
+        nc.sync.dma_start(pos_t[0][0][:], pos_t[0][1])
+        v_rows = keep.tile([P, S // 4], I32, name="v_rows", align_bytes=64)
+        nc.vector.tensor_copy(v_rows[:].bitcast(U8), tab_rows[:].bitcast(U8).indirect(offs_t[:]))
+        for a in range(PASSES):
+            for q in range(4):
+                first = 64 * a + 16 * q
+                nc.scalar.dma_start(v_planes[a][32 * q:32 * q + 4, :], v_rows[first:first + 16:4, :])
+
+        w2s = keep.tile([P, PASSES * H], U8, name="w2s", align_bytes=64)
+        nc.vector.tensor_copy(
+            w2s[:].rearrange("p (g t m) -> p g t m", t=PACK, m=P),
+            w2s_raw[:].bitcast(U8).rearrange("p (g m t) -> p g t m", t=PACK, m=P))
+
+        load_w1(0)
+        half_t = keep.tile([P, GROUPS, PACK], F32, name="half_t")
+        nc.sync.dma_start(half_t[:], half.rearrange("(b p t) -> p b t", b=GROUPS, t=PACK))
+        nc.sync.dma_start(pos_t[1][0][:], pos_t[1][1])
+        nc.sync.dma_start(pos_t[2][0][:], pos_t[2][1])
+        load_w1(1)
+        near_list, field_list, base_list = pos_t[0][0], pos_t[1][0], pos_t[2][0]
+        w3_w = keep.tile([P, PASSES, N], I32, name="w3_w", align_bytes=64)
+        nc.sync.dma_start(w3_w[:], w3_words.rearrange("a p c i -> p a (c i)").bitcast(I32))
+        for q in range(4):
+            nc.sync.dma_start(
+                w3s[32 * q:32 * q + 4, :].rearrange("r (a c) -> r a c", a=PASSES),
+                w3_scales.bitcast(I32)[:, 4 * q:4 * q + 4, :].rearrange("a r c -> r a c"))
+        ded_t = keep.tile([P, NT], F32, name="ded_t")
+        with nc.allow_non_contiguous_dma(reason="one deductible a partition"):
+            nc.sync.dma_start(ded_t[:], ded.rearrange("(c p) -> p c", p=P))
+
+        v_words = {}
+        whole = keep.tile([P, S], I32, name="v_words0", align_bytes=64)
+        nc.vector.tensor_copy(whole[:].bitcast(U32), tab_w[0][:].bitcast(U32).indirect(offs_t[:]))
+        for h in range(2):
+            v_words[0, h] = whole[:, h * BANK:(h + 1) * BANK]
+
+        w2c = keep.tile([P, PASSES * H * 2], U8, name="w2c", align_bytes=64)
+        nc.vector.tensor_copy(
+            w2c[:].bitcast(U16).rearrange("p (g t m) -> p g t m", t=PACK, m=P),
+            w2_raw[:].rearrange("p a c -> p (a c)").bitcast(U16).rearrange("p (g m t) -> p g t m", t=PACK, m=P))
+
+        for h in range(2):
+            part = keep.tile([P, BANK], I32, name="v_words1%d" % h, align_bytes=64)
+            nc.vector.tensor_copy(part[:].bitcast(U32),
+                                  tab_w[1][:].bitcast(U32).indirect(offs_t[:, h * 32:(h + 1) * 32]))
+            v_words[1, h] = part[:]
+
+        w1_bf, w1_codes, w1_scales = {}, {}, {}
+
+        def cast_w1(a, b):
+            w1_bf[a, b] = work.tile([P, PACK, P, PACK], BF16, name="w1_bf", tag="w1_bf", bufs=2, align_bytes=64)
+            nc.vector.tensor_copy(w1_bf[a, b][:].rearrange("p t m j -> p m j t"),
+                                  w1_raw[a, b][:].rearrange("p j (m t) -> p m j t", t=PACK))
+
+        def quant_w1(a, b):
+            w1_codes[a, b] = keep.tile([P, KP], U32, name="w1_codes%d%d" % (a, b), align_bytes=64)
+            w1_scales[a, b] = keep.tile([P, KP], U8, name="w1_scales%d%d" % (a, b), align_bytes=64)
+            nc.vector.quantize_mx(out=w1_codes[a, b][:].bitcast(FP8X4), scales=w1_scales[a, b][:],
+                                  in_=w1_bf[a, b][:].rearrange("p t m j -> p (t m j)"))
+
+        def first_pass(kind, s, h, a, acc):
+            b, t = divmod(s, PACK)
+            if kind == "back":
+                c0 = a * H + s * P
+                lhs = w2c[:, 2 * c0:2 * (c0 + P)].bitcast(FP4X4)
+                lhs_s = w2s[:, c0:c0 + P]
+            else:
+                lhs = w1_codes[a, b][:, t * P:(t + 1) * P].bitcast(FP8X4)
+                lhs_s = w1_scales[a, b][:, t * P:(t + 1) * P]
+            nc.tensor.matmul_mx(out=acc[:], lhsT=lhs, lhsT_scale=lhs_s, rhs=v_words[a, h].bitcast(FP8X4),
+                                rhs_scale=v_planes[a][:].bitcast(U8)[:, h * BANK:(h + 1) * BANK],
+                                start=(a == 0), stop=(a == PASSES - 1))
+
+        windows = {}
+        opened = {}
+
+        def open_rows(kind, s):
+            for h in range(2):
+                opened[kind, s, h] = psum.tile([P, BANK], F32, name="acc", tag="acc")
+                first_pass(kind, s, h, 0, opened[kind, s, h])
+
+        def close_rows(kind, s, halves=(0, 1)):
+            if (kind, s) not in windows:
+                windows[kind, s] = work.tile([P, S], F32, name=kind, tag=kind, bufs=6 if kind == "back" else 4, align_bytes=64)
+            for h in halves:
+                acc = opened[kind, s, h]
+                first_pass(kind, s, h, 1, acc)
+                nc.scalar.activation(windows[kind, s][:, h * BANK:(h + 1) * BANK], acc[:],
+                                     ACT.Copy if kind == "back" else ACT.Abs)
+
+        def rows(kind, s):
+            open_rows(kind, s)
+            close_rows(kind, s)
+
+        near, damp = {}, {}
+
+        def pick_near(s):
+            near[s] = work.tile([P, M], F32, name="near", tag="near", bufs=3)
+            nc.vector.tensor_copy(near[s][:], windows["back", s][:].indirect(near_list[:]))
+
+        def make_damp(s):
+            b, t = divmod(s, PACK)
+            sq = work.tile([P, M], F32, name="sq", tag="sq", bufs=2)
+            nc.scalar.activation(sq[:], near[s][:], ACT.Square)
+            rs = work.tile([P, M], F32, name="rs", tag="rs", bufs=2)
+            nc.scalar.activation(rs[:], sq[:], ACT.Abs_reciprocal_sqrt, bias=half_t[:, b, t:t + 1])
+            damp[s] = work.tile([P, M], F32, name="damp", tag="damp", bufs=4)
+            nc.scalar.activation(damp[s][:], rs[:], ACT.Square)
+
+        negz = {}
+        ratio = {}
+
+        def pick_field(s, m0, m1):
+            ratio[s, m0] = work.tile([P, m1 - m0], F32, name="ratio", tag="ratio", bufs=3)
+            nc.vector.tensor_tensor(ratio[s, m0][:], windows["hail", s][:].indirect(field_list[:, m0 // 16:m1 // 16]),
+                                    damp[s][:, m0:m1], ALU.mult)
+
+        def pick_base(s, m0, m1):
+            b, t = divmod(s, PACK)
+            if b not in negz:
+                negz[b] = keep.tile([P, PACK, M], F32, name="negz%d" % b, align_bytes=64)
+            nc.vector.tensor_tensor(negz[b][:, t, m0:m1], windows["back", s][:].indirect(base_list[:, m0 // 16:m1 // 16]),
+                                    ratio[s, m0][:], ALU.subtract)
+
+        z_bf, z_codes, z_scales = {}, {}, {}
+
+        def round_z(b, m0, m1, on_vector):
+            z_bf[b, m0] = keep.tile([P, m1 - m0, PACK], BF16, name="z_bf%d_%d" % (b, m0), align_bytes=64)
+            dst = z_bf[b, m0][:].rearrange("p (c i) t -> p c t i", i=4)
+            src = negz[b][:, :, m0:m1].rearrange("p t (c i) -> p c t i", i=4)
+            if on_vector:
+                nc.vector.tensor_scalar(dst, src, -1.0, None, ALU.mult)
+            else:
+                nc.scalar.activation(dst, src, ACT.Copy, scale=-1.0)
+
+        def quant_z(b, m0, m1):
+            z_codes[b, m0] = keep.tile([P, m1 - m0], U32, name="z_codes%d_%d" % (b, m0), align_bytes=64)
+            z_scales[b, m0] = keep.tile([P, m1 - m0], U8, name="z_scales%d_%d" % (b, m0), align_bytes=64)
+            nc.vector.quantize_mx(out=z_codes[b, m0][:].bitcast(FP8X4), scales=z_scales[b, m0][:],
+                                  in_=z_bf[b, m0][:].rearrange("p m t -> p (m t)"))
+
+        loss = {}
+
+        def last_pass(b, hm):
+            for c in range(NT):
+                if b == 0:
+                    loss[hm, c] = psum.tile([P, BANK], F32, name="acc", tag="acc")
+                    rhs = z_codes[0, 0][:, hm * HALF_M:(hm + 1) * HALF_M]
+                    rhs_s = z_scales[0, 0][:, hm * HALF_M:(hm + 1) * HALF_M]
+                else:
+                    rhs = z_codes[1, hm * HALF_M][:]
+                    rhs_s = z_scales[1, hm * HALF_M][:]
+                nc.tensor.matmul_mx(out=loss[hm, c][:, 0:HALF_M],
+                                    lhsT=w3_w[:, b, c * P:(c + 1) * P].bitcast(FP8X4),
+                                    lhsT_scale=w3s[:].bitcast(U8)[:, b * N + c * P:b * N + (c + 1) * P],
+                                    rhs=rhs.bitcast(FP8X4), rhs_scale=rhs_s, start=(b == 0), stop=(b == 1))
+
+        def finish(hm):
+            for c2 in range(NT // 2):
+                res = keep.tile([P, 2, HALF_M], F32, name="res%d_%d" % (hm, c2), align_bytes=64)
+                for u in range(2):
+                    c = 2 * c2 + u
+                    nc.vector.tensor_scalar(res[:, u, :], loss[hm, c][:, 0:HALF_M], ded_t[:, c:c + 1], None, ALU.max)
+                nc.sync.dma_start(
+                    out[c2 * 2 * P:(c2 + 1) * 2 * P, hm * HALF_M:(hm + 1) * HALF_M].rearrange("(u p) m -> p u m", p=P),
+                    res[:])
+
+        for s in range(4):
+            open_rows("back", s)
+        for s in range(2):
+            close_rows("back", s, (0,))
+        for s in range(2):
+            close_rows("back", s, (1,))
+        cast_w1(0, 0)
+        pick_near(0)
+        quant_w1(0, 0)
+        close_rows("back", 2)
+        cast_w1(1, 0)
+        pick_near(1)
+        quant_w1(1, 0)
+        make_damp(0)
+        close_rows("back", 3)
+        pick_near(2)
+        rows("hail", 0)
+        make_damp(1)
+        for s in range(SLICES - 2):
+            rows("hail", s + 1)
+            if s < 2:
+                cast_w1(s, 1)
+            pick_field(s, 0, M)
+            if s + 3 < SLICES:
+                pick_near(s + 3)
+            if s < 2:
+                quant_w1(s, 1)
+            pick_base(s, 0, M)
+            make_damp(s + 2)
+            if s + 4 < SLICES:
+                rows("back", s + 4)
+            if s == PACK - 1:
+                round_z(0, 0, M, False)
+            if s == PACK:
+                quant_z(0, 0, M)
+        rows("hail", SLICES - 1)
+        last_pass(0, 0)
+        for hm in range(2):
+            m0, m1 = hm * HALF_M, (hm + 1) * HALF_M
+            pick_field(SLICES - 2, m0, m1)
+            pick_field(SLICES - 1, m0, m1)
+            if hm == 1:
+                quant_z(1, 0, HALF_M)
+                last_pass(1, 0)
+            pick_base(SLICES - 2, m0, m1)
+            pick_base(SLICES - 1, m0, m1)
+            round_z(1, m0, m1, hm == 1)
+        finish(0)
+        last_pass(0, 1)
+        quant_z(1, HALF_M, M)
+        last_pass(1, 1)
+        finish(1)

@@ -25,6 +25,7 @@ GROUPS = H // KP
 SLICES = GROUPS * PACK
 NT = N // P
 HALF_M = M // 2
+SLOTS = (4096, 24576, 26624)
 
 
 def tile_list_hail_indemnity_kernel(tc, tab_words, tab_scales, offs, pos1, pos2, pos3, w1,
@@ -32,6 +33,7 @@ def tile_list_hail_indemnity_kernel(tc, tab_words, tab_scales, offs, pos1, pos2,
     nc = tc.nc
     with ExitStack() as ctx:
         keep = ctx.enter_context(tc.tile_pool(name="keep", bufs=1))
+        turns = ctx.enter_context(tc.tile_pool(name="turns", bufs=1))
         work = ctx.enter_context(tc.tile_pool(name="work", bufs=3))
         psum = ctx.enter_context(tc.psum_pool(name="psum", bufs=8))
 
@@ -40,10 +42,10 @@ def tile_list_hail_indemnity_kernel(tc, tab_words, tab_scales, offs, pos1, pos2,
 
         warm = keep.tile([P, 8], F32, name="warm")
         nc.vector.memset(warm[:], 1.0)
-        tab_rows = keep.tile([P, T // 4], I32, name="tab_rows", align_bytes=64)
+        tab_rows = turns.tile([P, T // 4], I32, name="tab_rows", offset=0, align_bytes=64)
         nc.vector.memset(tab_rows[:], 0)
         nc.scalar.dma_start(tab_rows[0:P:4, :], tab_scales.rearrange("a q t -> (a q) t").bitcast(I32))
-        w2s_raw = keep.tile([P, PASSES * H // 4], I32, name="w2s_raw", tag="early", align_bytes=64)
+        w2s_raw = turns.tile([P, PASSES * H // 4], I32, name="w2s_raw", offset=4096 + 8192 - 1024, align_bytes=64)
         nc.vector.memset(w2s_raw[:], 0)
         for q in range(4):
             nc.scalar.dma_start(
@@ -57,18 +59,18 @@ def tile_list_hail_indemnity_kernel(tc, tab_words, tab_scales, offs, pos1, pos2,
         w3s = keep.tile([P, PASSES * N // 4], I32, name="w3s", align_bytes=64)
         nc.vector.memset(w3s[:], 0)
 
-        tab_w = [keep.tile([P, T], I32, name="tab_w%d" % a, align_bytes=64) for a in range(PASSES)]
-        nc.sync.dma_start(tab_w[0][:], tab_words[0].rearrange("p t i -> p (t i)").bitcast(I32))
+        tab_w = [keep.tile([P, T], I32, name="tab_w0", align_bytes=64),
+                 turns.tile([P, T], I32, name="tab_w1", offset=32768, align_bytes=64)]
         w2_raw = keep.tile([P, PASSES, H // 2], I32, name="w2_raw", align_bytes=64)
         nc.sync.dma_start(w2_raw[:], w2_words.bitcast(I32).rearrange("a p c -> p a c"))
+        nc.sync.dma_start(tab_w[0][:], tab_words[0].rearrange("p t i -> p (t i)").bitcast(I32))
         nc.sync.dma_start(tab_w[1][:], tab_words[1].rearrange("p t i -> p (t i)").bitcast(I32))
 
         w1_raw = {}
 
         def load_w1(b):
             for a in range(PASSES):
-                w1_raw[a, b] = keep.tile([P, PACK, KP], F32, name="w1_raw%d%d" % (a, b),
-                                         tag="early" if (a, b) == (0, 0) else "w1_raw%d%d" % (a, b), align_bytes=64)
+                w1_raw[a, b] = turns.tile([P, PACK, KP], F32, name="w1_raw%d%d" % (a, b), offset=(4096 if b == 0 else 32768) + 8192 * a)
                 nc.sync.dma_start(
                     w1_raw[a, b][:],
                     w1[a * KP:(a + 1) * KP, b * KP:(b + 1) * KP].rearrange("(p j) c -> p j c", j=PACK))
@@ -78,6 +80,11 @@ def tile_list_hail_indemnity_kernel(tc, tab_words, tab_scales, offs, pos1, pos2,
             t_ = keep.tile([P, M // 16], U16, name=name)
             pos_t.append((t_, src))
         nc.sync.dma_start(pos_t[0][0][:], pos_t[0][1])
+        w2c = keep.tile([P, PASSES * H * 2], U8, name="w2c", align_bytes=64)
+        nc.vector.tensor_copy(
+            w2c[:].bitcast(U16).rearrange("p (g t m) -> p g t m", t=PACK, m=P),
+            w2_raw[:].rearrange("p a c -> p (a c)").bitcast(U16).rearrange("p (g m t) -> p g t m", t=PACK, m=P))
+
         v_rows = keep.tile([P, S // 4], I32, name="v_rows", align_bytes=64)
         nc.vector.tensor_copy(v_rows[:].bitcast(U8), tab_rows[:].bitcast(U8).indirect(offs_t[:]))
         for a in range(PASSES):
@@ -95,10 +102,7 @@ def tile_list_hail_indemnity_kernel(tc, tab_words, tab_scales, offs, pos1, pos2,
         nc.sync.dma_start(half_t[:], half.rearrange("(b p t) -> p b t", b=GROUPS, t=PACK))
         nc.sync.dma_start(pos_t[1][0][:], pos_t[1][1])
         nc.sync.dma_start(pos_t[2][0][:], pos_t[2][1])
-        load_w1(1)
         near_list, field_list, base_list = pos_t[0][0], pos_t[1][0], pos_t[2][0]
-        w3_w = keep.tile([P, PASSES, N], I32, name="w3_w", align_bytes=64)
-        nc.sync.dma_start(w3_w[:], w3_words.rearrange("a p c i -> p a (c i)").bitcast(I32))
         for q in range(4):
             nc.sync.dma_start(
                 w3s[32 * q:32 * q + 4, :].rearrange("r (a c) -> r a c", a=PASSES),
@@ -107,16 +111,13 @@ def tile_list_hail_indemnity_kernel(tc, tab_words, tab_scales, offs, pos1, pos2,
         with nc.allow_non_contiguous_dma(reason="one deductible a partition"):
             nc.sync.dma_start(ded_t[:], ded.rearrange("(c p) -> p c", p=P))
 
+        neg_ded = keep.tile([P, NT], F32, name="neg_ded")
+        nc.scalar.activation(neg_ded[:], ded_t[:], ACT.Copy, scale=-1.0)
         v_words = {}
-        whole = keep.tile([P, S], I32, name="v_words0", align_bytes=64)
+        whole = turns.tile([P, S], I32, name="v_words0", offset=0, align_bytes=64)
         nc.vector.tensor_copy(whole[:].bitcast(U32), tab_w[0][:].bitcast(U32).indirect(offs_t[:]))
         for h in range(2):
             v_words[0, h] = whole[:, h * BANK:(h + 1) * BANK]
-
-        w2c = keep.tile([P, PASSES * H * 2], U8, name="w2c", align_bytes=64)
-        nc.vector.tensor_copy(
-            w2c[:].bitcast(U16).rearrange("p (g t m) -> p g t m", t=PACK, m=P),
-            w2_raw[:].rearrange("p a c -> p (a c)").bitcast(U16).rearrange("p (g m t) -> p g t m", t=PACK, m=P))
 
         for h in range(2):
             part = keep.tile([P, BANK], I32, name="v_words1%d" % h, align_bytes=64)
@@ -126,10 +127,11 @@ def tile_list_hail_indemnity_kernel(tc, tab_words, tab_scales, offs, pos1, pos2,
 
         w1_bf, w1_codes, w1_scales = {}, {}, {}
 
-        def cast_w1(a, b):
-            w1_bf[a, b] = work.tile([P, PACK, P, PACK], BF16, name="w1_bf", tag="w1_bf", bufs=2, align_bytes=64)
-            nc.vector.tensor_copy(w1_bf[a, b][:].rearrange("p t m j -> p m j t"),
-                                  w1_raw[a, b][:].rearrange("p j (m t) -> p m j t", t=PACK))
+        def cast_w1(a, b, on_scalar=False):
+            w1_bf[a, b] = turns.tile([P, PACK, P, PACK], BF16, name="w1_bf%d%d" % (a, b), align_bytes=64,
+                                     offset={(0, 0): 20480, (1, 0): 24576, (0, 1): 20480, (1, 1): 6144}[a, b])
+            (nc.scalar.copy if on_scalar else nc.vector.tensor_copy)(w1_bf[a, b][:].rearrange("p t m j -> p m t j"),
+                                  w1_raw[a, b][:].rearrange("p j (m t) -> p m t j", t=PACK))
 
         def quant_w1(a, b):
             w1_codes[a, b] = keep.tile([P, KP], U32, name="w1_codes%d%d" % (a, b), align_bytes=64)
@@ -174,7 +176,7 @@ def tile_list_hail_indemnity_kernel(tc, tab_words, tab_scales, offs, pos1, pos2,
         near, damp = {}, {}
 
         def pick_near(s):
-            near[s] = work.tile([P, M], F32, name="near", tag="near", bufs=3)
+            near[s] = turns.tile([P, M], F32, name="near", tag="slot%d" % (s % 3), offset=SLOTS[s % 3])
             nc.vector.tensor_copy(near[s][:], windows["back", s][:].indirect(near_list[:]))
 
         def make_damp(s):
@@ -183,14 +185,18 @@ def tile_list_hail_indemnity_kernel(tc, tab_words, tab_scales, offs, pos1, pos2,
             nc.scalar.activation(sq[:], near[s][:], ACT.Square)
             rs = work.tile([P, M], F32, name="rs", tag="rs", bufs=2)
             nc.scalar.activation(rs[:], sq[:], ACT.Abs_reciprocal_sqrt, bias=half_t[:, b, t:t + 1])
-            damp[s] = work.tile([P, M], F32, name="damp", tag="damp", bufs=4)
+            damp[s] = turns.tile([P, M], F32, name="damp", tag="slot%d" % (s % 3), offset=SLOTS[s % 3])
             nc.scalar.activation(damp[s][:], rs[:], ACT.Square)
 
         negz = {}
         ratio = {}
 
         def pick_field(s, m0, m1):
-            ratio[s, m0] = work.tile([P, m1 - m0], F32, name="ratio", tag="ratio", bufs=3)
+            if m0 == 0:
+                ratio[s, m0] = work.tile([P, m1 - m0], F32, name="ratio", tag="ratio", bufs=3)
+            else:
+                ratio[s, m0] = turns.tile([P, m1 - m0], F32, name="ratio%d" % s,
+                                          offset=32768 if s == SLICES - 2 else 36864)
             nc.vector.tensor_tensor(ratio[s, m0][:], windows["hail", s][:].indirect(field_list[:, m0 // 16:m1 // 16]),
                                     damp[s][:, m0:m1], ALU.mult)
 
@@ -204,7 +210,8 @@ def tile_list_hail_indemnity_kernel(tc, tab_words, tab_scales, offs, pos1, pos2,
         z_bf, z_codes, z_scales = {}, {}, {}
 
         def round_z(b, m0, m1, on_vector):
-            z_bf[b, m0] = keep.tile([P, m1 - m0, PACK], BF16, name="z_bf%d_%d" % (b, m0), align_bytes=64)
+            z_bf[b, m0] = turns.tile([P, m1 - m0, PACK], BF16, name="z_bf%d_%d" % (b, m0), align_bytes=64,
+                                     offset={(0, 0): 32768, (1, 0): 36864, (1, HALF_M): 38912}[b, m0])
             dst = z_bf[b, m0][:].rearrange("p (c i) t -> p c t i", i=4)
             src = negz[b][:, :, m0:m1].rearrange("p t (c i) -> p c t i", i=4)
             if on_vector:
@@ -235,11 +242,19 @@ def tile_list_hail_indemnity_kernel(tc, tab_words, tab_scales, offs, pos1, pos2,
                                     rhs=rhs.bitcast(FP8X4), rhs_scale=rhs_s, start=(b == 0), stop=(b == 1))
 
         def finish(hm):
+            over = {}
+            if hm == 0:
+                for c in range(NT):
+                    over[c] = work.tile([P, HALF_M], F32, name="over", tag="over", bufs=NT)
+                    nc.scalar.activation(over[c][:], loss[hm, c][:, 0:HALF_M], ACT.Relu, bias=neg_ded[:, c:c + 1])
             for c2 in range(NT // 2):
                 res = keep.tile([P, 2, HALF_M], F32, name="res%d_%d" % (hm, c2), align_bytes=64)
                 for u in range(2):
                     c = 2 * c2 + u
-                    nc.vector.tensor_scalar(res[:, u, :], loss[hm, c][:, 0:HALF_M], ded_t[:, c:c + 1], None, ALU.max)
+                    if hm == 0:
+                        nc.scalar.activation(res[:, u, :], over[c][:], ACT.Identity, bias=ded_t[:, c:c + 1])
+                    else:
+                        nc.vector.tensor_scalar(res[:, u, :], loss[hm, c][:, 0:HALF_M], ded_t[:, c:c + 1], None, ALU.max)
                 nc.sync.dma_start(
                     out[c2 * 2 * P:(c2 + 1) * 2 * P, hm * HALF_M:(hm + 1) * HALF_M].rearrange("(u p) m -> p u m", p=P),
                     res[:])
@@ -252,45 +267,50 @@ def tile_list_hail_indemnity_kernel(tc, tab_words, tab_scales, offs, pos1, pos2,
             close_rows("back", s, (1,))
         cast_w1(0, 0)
         pick_near(0)
-        quant_w1(0, 0)
-        close_rows("back", 2)
         cast_w1(1, 0)
-        pick_near(1)
+        quant_w1(0, 0)
         quant_w1(1, 0)
+        load_w1(1)
+        close_rows("back", 2)
         make_damp(0)
         close_rows("back", 3)
+        pick_near(1)
         pick_near(2)
         rows("hail", 0)
         make_damp(1)
         for s in range(SLICES - 2):
             rows("hail", s + 1)
-            if s < 2:
-                cast_w1(s, 1)
+            if s == 0:
+                cast_w1(0, 1)
+            if s == 1:
+                cast_w1(1, 1)
             pick_field(s, 0, M)
             if s + 3 < SLICES:
                 pick_near(s + 3)
             if s < 2:
                 quant_w1(s, 1)
             pick_base(s, 0, M)
-            make_damp(s + 2)
             if s + 4 < SLICES:
                 rows("back", s + 4)
-            if s == PACK - 1:
-                round_z(0, 0, M, False)
-            if s == PACK:
-                quant_z(0, 0, M)
+            make_damp(s + 2)
+        w3_w = turns.tile([P, PASSES, N], I32, name="w3_w", offset=12288, align_bytes=64)
+        nc.sync.dma_start(w3_w[:], w3_words.rearrange("a p c i -> p a (c i)").bitcast(I32))
         rows("hail", SLICES - 1)
+        round_z(0, 0, M, False)
+        pick_field(SLICES - 2, 0, HALF_M)
+        pick_field(SLICES - 1, 0, HALF_M)
+        pick_base(SLICES - 2, 0, HALF_M)
+        pick_base(SLICES - 1, 0, HALF_M)
+        round_z(1, 0, HALF_M, False)
+        quant_z(0, 0, M)
         last_pass(0, 0)
-        for hm in range(2):
-            m0, m1 = hm * HALF_M, (hm + 1) * HALF_M
-            pick_field(SLICES - 2, m0, m1)
-            pick_field(SLICES - 1, m0, m1)
-            if hm == 1:
-                quant_z(1, 0, HALF_M)
-                last_pass(1, 0)
-            pick_base(SLICES - 2, m0, m1)
-            pick_base(SLICES - 1, m0, m1)
-            round_z(1, m0, m1, hm == 1)
+        pick_field(SLICES - 2, HALF_M, M)
+        pick_base(SLICES - 2, HALF_M, M)
+        quant_z(1, 0, HALF_M)
+        last_pass(1, 0)
+        pick_field(SLICES - 1, HALF_M, M)
+        pick_base(SLICES - 1, HALF_M, M)
+        round_z(1, HALF_M, M, True)
         finish(0)
         last_pass(0, 1)
         quant_z(1, HALF_M, M)

@@ -25,7 +25,10 @@ GROUPS = H // KP
 SLICES = GROUPS * PACK
 NT = N // P
 HALF_M = M // 2
-SLOTS = (4096, 24576, 26624)
+TAB1 = 8064
+TAB0 = 32640
+RAW = TAB0 + 2048
+SLOTS = (RAW, 28544, 30592)
 
 
 def tile_list_hail_indemnity_kernel(tc, tab_words, tab_scales, offs, pos1, pos2, pos3, w1,
@@ -37,87 +40,70 @@ def tile_list_hail_indemnity_kernel(tc, tab_words, tab_scales, offs, pos1, pos2,
         work = ctx.enter_context(tc.tile_pool(name="work", bufs=3))
         psum = ctx.enter_context(tc.psum_pool(name="psum", bufs=8))
 
-        offs_t = keep.tile([P, S // 16], U16, name="offs_t")
-        nc.sync.dma_start(offs_t[:], offs)
-
-        warm = keep.tile([P, 8], F32, name="warm")
+        warm = turns.tile([P, 8], F32, name="warm", offset=TAB0)
         nc.vector.memset(warm[:], 1.0)
-        tab_rows = turns.tile([P, T // 4], I32, name="tab_rows", offset=0, align_bytes=64)
-        nc.vector.memset(tab_rows[:], 0)
-        nc.scalar.dma_start(tab_rows[0:P:4, :], tab_scales.rearrange("a q t -> (a q) t").bitcast(I32))
-        w2s_raw = turns.tile([P, PASSES * H // 4], I32, name="w2s_raw", offset=4096 + 8192 - 1024, align_bytes=64)
-        nc.vector.memset(w2s_raw[:], 0)
-        for q in range(4):
-            nc.scalar.dma_start(
-                w2s_raw[32 * q:32 * q + 4, :].rearrange("r (a c) -> r a c", a=PASSES),
-                w2_scales.bitcast(I32)[:, 4 * q:4 * q + 4, :].rearrange("a r c -> r a c"))
         warm2 = keep.tile([P, 8], F32, name="warm2")
         nc.scalar.activation(warm2[:], warm[:], ACT.Abs_reciprocal_sqrt)
-        v_planes = [keep.tile([P, S // 4], I32, name="v_plane%d" % a, align_bytes=64) for a in range(PASSES)]
-        for a in range(PASSES):
-            nc.vector.memset(v_planes[a][:], 0)
-        w3s = keep.tile([P, PASSES * N // 4], I32, name="w3s", align_bytes=64)
-        nc.vector.memset(w3s[:], 0)
-
-        tab_w = [keep.tile([P, T], I32, name="tab_w0", align_bytes=64),
-                 turns.tile([P, T], I32, name="tab_w1", offset=32768, align_bytes=64)]
+        lists = {}
+        for name, src in (("offs", offs), ("pos2", pos2), ("pos1", pos1), ("pos3", pos3)):
+            lists[name] = keep.tile([P, src.shape[1]], U16, name=name + "_t")
+            nc.sync.dma_start(lists[name][:], src)
+        offs_t, near_list, field_list, base_list = lists["offs"], lists["pos2"], lists["pos1"], lists["pos3"]
         w2_raw = keep.tile([P, PASSES, H // 2], I32, name="w2_raw", align_bytes=64)
         nc.sync.dma_start(w2_raw[:], w2_words.bitcast(I32).rearrange("a p c -> p a c"))
+        tab_w = [turns.tile([P, T], I32, name="tab_w0", offset=TAB0, align_bytes=64),
+                 turns.tile([P, T], I32, name="tab_w1", offset=TAB1, align_bytes=64)]
+
+        tab_rows = turns.tile([P, T // 4], I32, name="tab_rows", offset=4032, align_bytes=64)
+        nc.vector.memset(tab_rows[:], 0)
+        nc.sync.dma_start(tab_rows[0:P:4, :], tab_scales.rearrange("a q t -> (a q) t").bitcast(I32))
+        w2s_raw = keep.tile([P, PASSES * H // 4], I32, name="w2s_raw", align_bytes=64)
+        nc.gpsimd.memset(w2s_raw[:], 0)
+        for q in range(4):
+            nc.gpsimd.dma_start(
+                w2s_raw[32 * q:32 * q + 4, :].rearrange("r (a c) -> r a c", a=PASSES),
+                w2_scales.bitcast(I32)[:, 4 * q:4 * q + 4, :].rearrange("a r c -> r a c"))
         nc.sync.dma_start(tab_w[0][:], tab_words[0].rearrange("p t i -> p (t i)").bitcast(I32))
-        nc.sync.dma_start(tab_w[1][:], tab_words[1].rearrange("p t i -> p (t i)").bitcast(I32))
+        planes = keep.tile([P, PASSES * S // 4], I32, name="planes", align_bytes=64)
+        nc.vector.memset(planes[:], 0)
+        v_planes = [planes[:, a * (S // 4):(a + 1) * (S // 4)] for a in range(PASSES)]
 
         w1_raw = {}
 
         def load_w1(b):
             for a in range(PASSES):
-                w1_raw[a, b] = turns.tile([P, PACK, KP], F32, name="w1_raw%d%d" % (a, b), offset=(4096 if b == 0 else 32768) + 8192 * a)
+                w1_raw[a, b] = turns.tile([P, PACK, KP], F32, name="w1_raw%d%d" % (a, b), offset=(RAW if b == 0 else TAB1) + 8192 * a)
                 nc.sync.dma_start(
                     w1_raw[a, b][:],
                     w1[a * KP:(a + 1) * KP, b * KP:(b + 1) * KP].rearrange("(p j) c -> p j c", j=PACK))
-
-        pos_t = []
-        for name, src in (("pos2_t", pos2), ("pos1_t", pos1), ("pos3_t", pos3)):
-            t_ = keep.tile([P, M // 16], U16, name=name)
-            pos_t.append((t_, src))
-        nc.sync.dma_start(pos_t[0][0][:], pos_t[0][1])
-        w2c = keep.tile([P, PASSES * H * 2], U8, name="w2c", align_bytes=64)
-        nc.vector.tensor_copy(
-            w2c[:].bitcast(U16).rearrange("p (g t m) -> p g t m", t=PACK, m=P),
-            w2_raw[:].rearrange("p a c -> p (a c)").bitcast(U16).rearrange("p (g m t) -> p g t m", t=PACK, m=P))
 
         v_rows = keep.tile([P, S // 4], I32, name="v_rows", align_bytes=64)
         nc.vector.tensor_copy(v_rows[:].bitcast(U8), tab_rows[:].bitcast(U8).indirect(offs_t[:]))
         for a in range(PASSES):
             for q in range(4):
                 first = 64 * a + 16 * q
-                nc.scalar.dma_start(v_planes[a][32 * q:32 * q + 4, :], v_rows[first:first + 16:4, :])
-
-        w2s = keep.tile([P, PASSES * H], U8, name="w2s", align_bytes=64)
+                queue = nc.scalar if q % 2 else nc.sync
+                queue.dma_start(v_planes[a][32 * q:32 * q + 4, :], v_rows[first:first + 16:4, :])
+        nc.sync.dma_start(tab_w[1][:], tab_words[1].rearrange("p t i -> p (t i)").bitcast(I32))
+        w2c = turns.tile([P, PASSES * H * 2], U8, name="w2c", offset=0, align_bytes=64)
         nc.vector.tensor_copy(
-            w2s[:].rearrange("p (g t m) -> p g t m", t=PACK, m=P),
-            w2s_raw[:].bitcast(U8).rearrange("p (g m t) -> p g t m", t=PACK, m=P))
+            w2c[:].bitcast(U16).rearrange("p (g t m) -> p g t m", t=PACK, m=P),
+            w2_raw[:].rearrange("p a c -> p (a c)").bitcast(U16).rearrange("p (g m t) -> p g t m", t=PACK, m=P))
 
-        load_w1(0)
-        half_t = keep.tile([P, GROUPS, PACK], F32, name="half_t")
-        nc.sync.dma_start(half_t[:], half.rearrange("(b p t) -> p b t", b=GROUPS, t=PACK))
-        nc.sync.dma_start(pos_t[1][0][:], pos_t[1][1])
-        nc.sync.dma_start(pos_t[2][0][:], pos_t[2][1])
-        near_list, field_list, base_list = pos_t[0][0], pos_t[1][0], pos_t[2][0]
-        for q in range(4):
-            nc.sync.dma_start(
-                w3s[32 * q:32 * q + 4, :].rearrange("r (a c) -> r a c", a=PASSES),
-                w3_scales.bitcast(I32)[:, 4 * q:4 * q + 4, :].rearrange("a r c -> r a c"))
-        ded_t = keep.tile([P, NT], F32, name="ded_t")
-        with nc.allow_non_contiguous_dma(reason="one deductible a partition"):
-            nc.sync.dma_start(ded_t[:], ded.rearrange("(c p) -> p c", p=P))
+        half_t = turns.tile([P, GROUPS, PACK], F32, name="half_t", offset=4096)
+        nc.scalar.dma_start(half_t[:], half.rearrange("(b p t) -> p b t", b=GROUPS, t=PACK))
 
-        neg_ded = keep.tile([P, NT], F32, name="neg_ded")
-        nc.scalar.activation(neg_ded[:], ded_t[:], ACT.Copy, scale=-1.0)
         v_words = {}
-        whole = turns.tile([P, S], I32, name="v_words0", offset=0, align_bytes=64)
+        whole = keep.tile([P, S], I32, name="v_words0", align_bytes=64)
         nc.vector.tensor_copy(whole[:].bitcast(U32), tab_w[0][:].bitcast(U32).indirect(offs_t[:]))
         for h in range(2):
             v_words[0, h] = whole[:, h * BANK:(h + 1) * BANK]
+
+        w2s = turns.tile([P, PASSES * H], U8, name="w2s", offset=TAB0, align_bytes=64)
+        nc.vector.tensor_copy(
+            w2s[:].rearrange("p (g t m) -> p g t m", t=PACK, m=P),
+            w2s_raw[:].bitcast(U8).rearrange("p (g m t) -> p g t m", t=PACK, m=P))
+        load_w1(0)
 
         for h in range(2):
             part = keep.tile([P, BANK], I32, name="v_words1%d" % h, align_bytes=64)
@@ -129,9 +115,9 @@ def tile_list_hail_indemnity_kernel(tc, tab_words, tab_scales, offs, pos1, pos2,
 
         def cast_w1(a, b, on_scalar=False):
             w1_bf[a, b] = turns.tile([P, PACK, P, PACK], BF16, name="w1_bf%d%d" % (a, b), align_bytes=64,
-                                     offset={(0, 0): 20480, (1, 0): 24576, (0, 1): 20480, (1, 1): 6144}[a, b])
-            (nc.scalar.copy if on_scalar else nc.vector.tensor_copy)(w1_bf[a, b][:].rearrange("p t m j -> p m t j"),
-                                  w1_raw[a, b][:].rearrange("p j (m t) -> p m t j", t=PACK))
+                                     offset={(0, 0): 24448, (1, 0): 28544, (0, 1): 24448, (1, 1): RAW + 2048}[a, b])
+            (nc.scalar.copy if on_scalar else nc.vector.tensor_copy)(w1_bf[a, b][:].rearrange("p t m j -> p m j t"),
+                                  w1_raw[a, b][:].rearrange("p j (m t) -> p m j t", t=PACK))
 
         def quant_w1(a, b):
             w1_codes[a, b] = keep.tile([P, KP], U32, name="w1_codes%d%d" % (a, b), align_bytes=64)
@@ -149,7 +135,7 @@ def tile_list_hail_indemnity_kernel(tc, tab_words, tab_scales, offs, pos1, pos2,
                 lhs = w1_codes[a, b][:, t * P:(t + 1) * P].bitcast(FP8X4)
                 lhs_s = w1_scales[a, b][:, t * P:(t + 1) * P]
             nc.tensor.matmul_mx(out=acc[:], lhsT=lhs, lhsT_scale=lhs_s, rhs=v_words[a, h].bitcast(FP8X4),
-                                rhs_scale=v_planes[a][:].bitcast(U8)[:, h * BANK:(h + 1) * BANK],
+                                rhs_scale=v_planes[a].bitcast(U8)[:, h * BANK:(h + 1) * BANK],
                                 start=(a == 0), stop=(a == PASSES - 1))
 
         windows = {}
@@ -196,7 +182,7 @@ def tile_list_hail_indemnity_kernel(tc, tab_words, tab_scales, offs, pos1, pos2,
                 ratio[s, m0] = work.tile([P, m1 - m0], F32, name="ratio", tag="ratio", bufs=3)
             else:
                 ratio[s, m0] = turns.tile([P, m1 - m0], F32, name="ratio%d" % s,
-                                          offset=32768 if s == SLICES - 2 else 36864)
+                                          offset=TAB1 if s == SLICES - 2 else TAB1 + 4096)
             nc.vector.tensor_tensor(ratio[s, m0][:], windows["hail", s][:].indirect(field_list[:, m0 // 16:m1 // 16]),
                                     damp[s][:, m0:m1], ALU.mult)
 
@@ -211,9 +197,9 @@ def tile_list_hail_indemnity_kernel(tc, tab_words, tab_scales, offs, pos1, pos2,
 
         def round_z(b, m0, m1, on_vector):
             z_bf[b, m0] = turns.tile([P, m1 - m0, PACK], BF16, name="z_bf%d_%d" % (b, m0), align_bytes=64,
-                                     offset={(0, 0): 32768, (1, 0): 36864, (1, HALF_M): 38912}[b, m0])
-            dst = z_bf[b, m0][:].rearrange("p (c i) t -> p c t i", i=4)
-            src = negz[b][:, :, m0:m1].rearrange("p t (c i) -> p c t i", i=4)
+                                     offset={(0, 0): TAB1, (1, 0): TAB1 + 4096, (1, HALF_M): TAB1 + 6144}[b, m0])
+            dst = z_bf[b, m0][:]
+            src = negz[b][:, :, m0:m1].rearrange("p t m -> p m t")
             if on_vector:
                 nc.vector.tensor_scalar(dst, src, -1.0, None, ALU.mult)
             else:
@@ -259,7 +245,7 @@ def tile_list_hail_indemnity_kernel(tc, tab_words, tab_scales, offs, pos1, pos2,
                     out[c2 * 2 * P:(c2 + 1) * 2 * P, hm * HALF_M:(hm + 1) * HALF_M].rearrange("(u p) m -> p u m", p=P),
                     res[:])
 
-        for s in range(4):
+        for s in range(2):
             open_rows("back", s)
         for s in range(2):
             close_rows("back", s, (0,))
@@ -271,9 +257,9 @@ def tile_list_hail_indemnity_kernel(tc, tab_words, tab_scales, offs, pos1, pos2,
         quant_w1(0, 0)
         quant_w1(1, 0)
         load_w1(1)
-        close_rows("back", 2)
+        rows("back", 2)
         make_damp(0)
-        close_rows("back", 3)
+        rows("back", 3)
         pick_near(1)
         pick_near(2)
         rows("hail", 0)
@@ -283,7 +269,7 @@ def tile_list_hail_indemnity_kernel(tc, tab_words, tab_scales, offs, pos1, pos2,
             if s == 0:
                 cast_w1(0, 1)
             if s == 1:
-                cast_w1(1, 1)
+                cast_w1(1, 1, True)
             pick_field(s, 0, M)
             if s + 3 < SLICES:
                 pick_near(s + 3)
@@ -293,7 +279,18 @@ def tile_list_hail_indemnity_kernel(tc, tab_words, tab_scales, offs, pos1, pos2,
             if s + 4 < SLICES:
                 rows("back", s + 4)
             make_damp(s + 2)
-        w3_w = turns.tile([P, PASSES, N], I32, name="w3_w", offset=12288, align_bytes=64)
+        ded_t = turns.tile([P, NT], F32, name="ded_t", offset=RAW + 7680)
+        with nc.allow_non_contiguous_dma(reason="one deductible a partition"):
+            nc.sync.dma_start(ded_t[:], ded.rearrange("(c p) -> p c", p=P))
+        neg_ded = turns.tile([P, NT], F32, name="neg_ded", offset=RAW + 2048)
+        nc.scalar.activation(neg_ded[:], ded_t[:], ACT.Copy, scale=-1.0)
+        w3s = turns.tile([P, PASSES * N // 4], I32, name="w3s", offset=RAW + 6144, align_bytes=64)
+        nc.gpsimd.memset(w3s[:], 0)
+        for q in range(4):
+            nc.sync.dma_start(
+                w3s[32 * q:32 * q + 4, :].rearrange("r (a c) -> r a c", a=PASSES),
+                w3_scales.bitcast(I32)[:, 4 * q:4 * q + 4, :].rearrange("a r c -> r a c"))
+        w3_w = turns.tile([P, PASSES, N], I32, name="w3_w", offset=RAW + 8192, align_bytes=64)
         nc.sync.dma_start(w3_w[:], w3_words.rearrange("a p c i -> p a (c i)").bitcast(I32))
         rows("hail", SLICES - 1)
         round_z(0, 0, M, False)

@@ -24,99 +24,108 @@ PASSES = K // KP
 GROUPS = H // KP
 SLICES = GROUPS * PACK
 NT = N // P
-HALF_M = M // 2
-TAB1 = 8064
-TAB0 = 32640
-RAW = TAB0 + 2048
-SLOTS = (RAW, 28544, 30592)
+HM = M // 2
+TAB_BYTES = 4 * T
+RAW_BYTES = 4 * PACK * KP
+V_ROWS = TAB_BYTES
+RAW0 = V_ROWS + S // 2 - RAW_BYTES
+W2_RAW = V_ROWS + S
+W2S_RAW = W2_RAW + PASSES * 2 * H
+TAB1 = RAW0 + 2 * RAW_BYTES
+TAB_ROWS = TAB1 + TAB_BYTES
 
 
 def tile_list_hail_indemnity_kernel(tc, tab_words, tab_scales, offs, pos1, pos2, pos3, w1,
-                                              w2_words, w2_scales, half, w3_words, w3_scales, ded, out):
+                                                 w2_words, w2_scales, half, w3_words, w3_scales, ded, out):
     nc = tc.nc
     with ExitStack() as ctx:
         keep = ctx.enter_context(tc.tile_pool(name="keep", bufs=1))
         turns = ctx.enter_context(tc.tile_pool(name="turns", bufs=1))
-        work = ctx.enter_context(tc.tile_pool(name="work", bufs=3))
+        work = ctx.enter_context(tc.tile_pool(name="work", bufs=2))
         psum = ctx.enter_context(tc.psum_pool(name="psum", bufs=8))
 
-        warm = turns.tile([P, 8], F32, name="warm", offset=TAB0)
-        nc.vector.memset(warm[:], 1.0)
-        warm2 = keep.tile([P, 8], F32, name="warm2")
-        nc.scalar.activation(warm2[:], warm[:], ACT.Abs_reciprocal_sqrt)
-        lists = {}
-        for name, src in (("offs", offs), ("pos2", pos2), ("pos1", pos1), ("pos3", pos3)):
-            lists[name] = keep.tile([P, src.shape[1]], U16, name=name + "_t")
-            nc.sync.dma_start(lists[name][:], src)
-        offs_t, near_list, field_list, base_list = lists["offs"], lists["pos2"], lists["pos1"], lists["pos3"]
-        w2_raw = keep.tile([P, PASSES, H // 2], I32, name="w2_raw", align_bytes=64)
-        nc.sync.dma_start(w2_raw[:], w2_words.bitcast(I32).rearrange("a p c -> p a c"))
-        tab_w = [turns.tile([P, T], I32, name="tab_w0", offset=TAB0, align_bytes=64),
-                 turns.tile([P, T], I32, name="tab_w1", offset=TAB1, align_bytes=64)]
-
-        tab_rows = turns.tile([P, T // 4], I32, name="tab_rows", offset=4032, align_bytes=64)
+        tab_rows = turns.tile([P, T // 4], I32, name="tab_rows", offset=TAB_ROWS, align_bytes=64)
         nc.vector.memset(tab_rows[:], 0)
-        nc.sync.dma_start(tab_rows[0:P:4, :], tab_scales.rearrange("a q t -> (a q) t").bitcast(I32))
-        w2s_raw = keep.tile([P, PASSES * H // 4], I32, name="w2s_raw", align_bytes=64)
+        w2s_raw = turns.tile([P, PASSES * H // 4], I32, name="w2s_raw", offset=W2S_RAW, align_bytes=64)
         nc.gpsimd.memset(w2s_raw[:], 0)
-        for q in range(4):
-            nc.gpsimd.dma_start(
-                w2s_raw[32 * q:32 * q + 4, :].rearrange("r (a c) -> r a c", a=PASSES),
-                w2_scales.bitcast(I32)[:, 4 * q:4 * q + 4, :].rearrange("a r c -> r a c"))
-        nc.sync.dma_start(tab_w[0][:], tab_words[0].rearrange("p t i -> p (t i)").bitcast(I32))
         planes = keep.tile([P, PASSES * S // 4], I32, name="planes", align_bytes=64)
         nc.vector.memset(planes[:], 0)
+
+        lists = {}
+
+        def load_list(name, src):
+            lists[name] = keep.tile([P, src.shape[1]], U16, name=name + "_t")
+            nc.sync.dma_start(lists[name][:], src)
+
+        load_list("offs", offs)
+        half_t = turns.tile([P, GROUPS, PACK], F32, name="half_t", offset=TAB1)
+        nc.sync.dma_start(half_t[:], half.rearrange("(b p t) -> p b t", b=GROUPS, t=PACK))
+        inv_root = keep.tile([P, SLICES], F32, name="inv_root")
+        nc.scalar.activation(inv_root[:], half_t[:].rearrange("p b t -> p (b t)"), ACT.Abs_reciprocal_sqrt)
+        w2_raw = turns.tile([P, PASSES, H // 2], I32, name="w2_raw", offset=W2_RAW, align_bytes=64)
+        nc.sync.dma_start(w2_raw[:], w2_words.bitcast(I32).rearrange("a p c -> p a c"))
+        load_list("pos2", pos2)
+        load_list("pos1", pos1)
+        load_list("pos3", pos3)
+        offs_t, near_list, field_list, base_list = lists["offs"], lists["pos2"], lists["pos1"], lists["pos3"]
+        tab_w = []
+        for a in range(PASSES):
+            tab_w.append(turns.tile([P, T], I32, name="tab_w%d" % a, offset=a * TAB1, align_bytes=64))
+            nc.sync.dma_start(tab_w[a][:], tab_words[a].rearrange("p t i -> p (t i)").bitcast(I32))
+            if a == 0:
+                for q in range(4):
+                    nc.scalar.dma_start(
+                        w2s_raw[32 * q:32 * q + 4, :].rearrange("r (a c) -> r a c", a=PASSES),
+                        w2_scales.bitcast(I32)[:, 4 * q:4 * q + 4, :].rearrange("a r c -> r a c"))
+                nc.sync.dma_start(tab_rows[0:P:4, :], tab_scales.rearrange("a q t -> (a q) t").bitcast(I32))
+
+        w2c = keep.tile([P, PASSES * H * 2], U8, name="w2c", align_bytes=64)
+        nc.vector.tensor_copy(
+            w2c[:].bitcast(U16).rearrange("p (g t m n) -> p g m t n", t=PACK, m=P // 8, n=8),
+            w2_raw[:].rearrange("p a c -> p (a c)").bitcast(U16).rearrange("p (g m n t) -> p g m t n", t=PACK, m=P // 8, n=8))
+
+        w2s = keep.tile([P, PASSES * H], U8, name="w2s", align_bytes=64)
+        nc.vector.tensor_copy(
+            w2s[:].rearrange("p (g t m n) -> p g m t n", t=PACK, m=P // 16, n=16),
+            w2s_raw[:].bitcast(U8).rearrange("p (g m n t) -> p g m t n", t=PACK, m=P // 16, n=16))
+
+        v_rows = turns.tile([P, S // 4], I32, name="v_rows", offset=V_ROWS, align_bytes=64)
+        nc.vector.tensor_copy(v_rows[:].bitcast(U8), tab_rows[:].bitcast(U8).indirect(offs_t[:]))
         v_planes = [planes[:, a * (S // 4):(a + 1) * (S // 4)] for a in range(PASSES)]
+        for a in range(PASSES):
+            for q in range(4):
+                first = 64 * a + 16 * q
+                queue = nc.gpsimd if 4 * a + q == 7 else nc.scalar
+                queue.dma_start(v_planes[a][32 * q:32 * q + 4, :], v_rows[first:first + 16:4, :])
+        v_words = {}
+        whole = turns.tile([P, S], I32, name="v_words0", offset=TAB_ROWS, align_bytes=64)
+        nc.vector.tensor_copy(whole[:].bitcast(U32), tab_w[0][:].bitcast(U32).indirect(offs_t[:]))
+        for h in range(2):
+            v_words[0, h] = whole[:, h * BANK:(h + 1) * BANK]
 
         w1_raw = {}
 
         def load_w1(b):
             for a in range(PASSES):
-                w1_raw[a, b] = turns.tile([P, PACK, KP], F32, name="w1_raw%d%d" % (a, b), offset=(RAW if b == 0 else TAB1) + 8192 * a)
+                w1_raw[a, b] = turns.tile([P, PACK, KP], F32, name="w1_raw%d%d" % (a, b),
+                                          offset=(TAB1 if b else RAW0) + a * RAW_BYTES)
                 nc.sync.dma_start(
                     w1_raw[a, b][:],
                     w1[a * KP:(a + 1) * KP, b * KP:(b + 1) * KP].rearrange("(p j) c -> p j c", j=PACK))
 
-        v_rows = keep.tile([P, S // 4], I32, name="v_rows", align_bytes=64)
-        nc.vector.tensor_copy(v_rows[:].bitcast(U8), tab_rows[:].bitcast(U8).indirect(offs_t[:]))
-        for a in range(PASSES):
-            for q in range(4):
-                first = 64 * a + 16 * q
-                queue = nc.scalar if q % 2 else nc.sync
-                queue.dma_start(v_planes[a][32 * q:32 * q + 4, :], v_rows[first:first + 16:4, :])
-        nc.sync.dma_start(tab_w[1][:], tab_words[1].rearrange("p t i -> p (t i)").bitcast(I32))
-        w2c = turns.tile([P, PASSES * H * 2], U8, name="w2c", offset=0, align_bytes=64)
-        nc.vector.tensor_copy(
-            w2c[:].bitcast(U16).rearrange("p (g t m) -> p g t m", t=PACK, m=P),
-            w2_raw[:].rearrange("p a c -> p (a c)").bitcast(U16).rearrange("p (g m t) -> p g t m", t=PACK, m=P))
-
-        half_t = turns.tile([P, GROUPS, PACK], F32, name="half_t", offset=4096)
-        nc.scalar.dma_start(half_t[:], half.rearrange("(b p t) -> p b t", b=GROUPS, t=PACK))
-
-        v_words = {}
-        whole = keep.tile([P, S], I32, name="v_words0", align_bytes=64)
-        nc.vector.tensor_copy(whole[:].bitcast(U32), tab_w[0][:].bitcast(U32).indirect(offs_t[:]))
-        for h in range(2):
-            v_words[0, h] = whole[:, h * BANK:(h + 1) * BANK]
-
-        w2s = turns.tile([P, PASSES * H], U8, name="w2s", offset=TAB0, align_bytes=64)
-        nc.vector.tensor_copy(
-            w2s[:].rearrange("p (g t m) -> p g t m", t=PACK, m=P),
-            w2s_raw[:].bitcast(U8).rearrange("p (g m t) -> p g t m", t=PACK, m=P))
         load_w1(0)
-
         for h in range(2):
             part = keep.tile([P, BANK], I32, name="v_words1%d" % h, align_bytes=64)
             nc.vector.tensor_copy(part[:].bitcast(U32),
                                   tab_w[1][:].bitcast(U32).indirect(offs_t[:, h * 32:(h + 1) * 32]))
             v_words[1, h] = part[:]
+        load_w1(1)
 
         w1_bf, w1_codes, w1_scales = {}, {}, {}
 
-        def cast_w1(a, b, on_scalar=False):
-            w1_bf[a, b] = turns.tile([P, PACK, P, PACK], BF16, name="w1_bf%d%d" % (a, b), align_bytes=64,
-                                     offset={(0, 0): 24448, (1, 0): 28544, (0, 1): 24448, (1, 1): RAW + 2048}[a, b])
-            (nc.scalar.copy if on_scalar else nc.vector.tensor_copy)(w1_bf[a, b][:].rearrange("p t m j -> p m j t"),
+        def cast_w1(a, b):
+            w1_bf[a, b] = work.tile([P, PACK, P, PACK], BF16, name="w1_bf", tag="w1_bf", bufs=2, align_bytes=64)
+            nc.vector.tensor_copy(w1_bf[a, b][:].rearrange("p t m j -> p m j t"),
                                   w1_raw[a, b][:].rearrange("p j (m t) -> p m j t", t=PACK))
 
         def quant_w1(a, b):
@@ -125,8 +134,12 @@ def tile_list_hail_indemnity_kernel(tc, tab_words, tab_scales, offs, pos1, pos2,
             nc.vector.quantize_mx(out=w1_codes[a, b][:].bitcast(FP8X4), scales=w1_scales[a, b][:],
                                   in_=w1_bf[a, b][:].rearrange("p t m j -> p (t m j)"))
 
-        def first_pass(kind, s, h, a, acc):
+        banks = {}
+
+        def first_pass(kind, s, h, a):
             b, t = divmod(s, PACK)
+            if a == 0:
+                banks[kind, s, h] = psum.tile([P, BANK], F32, name="acc", tag="acc")
             if kind == "back":
                 c0 = a * H + s * P
                 lhs = w2c[:, 2 * c0:2 * (c0 + P)].bitcast(FP4X4)
@@ -134,72 +147,72 @@ def tile_list_hail_indemnity_kernel(tc, tab_words, tab_scales, offs, pos1, pos2,
             else:
                 lhs = w1_codes[a, b][:, t * P:(t + 1) * P].bitcast(FP8X4)
                 lhs_s = w1_scales[a, b][:, t * P:(t + 1) * P]
-            nc.tensor.matmul_mx(out=acc[:], lhsT=lhs, lhsT_scale=lhs_s, rhs=v_words[a, h].bitcast(FP8X4),
+            nc.tensor.matmul_mx(out=banks[kind, s, h][:], lhsT=lhs, lhsT_scale=lhs_s,
+                                rhs=v_words[a, h].bitcast(FP8X4),
                                 rhs_scale=v_planes[a].bitcast(U8)[:, h * BANK:(h + 1) * BANK],
                                 start=(a == 0), stop=(a == PASSES - 1))
 
         windows = {}
-        opened = {}
 
-        def open_rows(kind, s):
-            for h in range(2):
-                opened[kind, s, h] = psum.tile([P, BANK], F32, name="acc", tag="acc")
-                first_pass(kind, s, h, 0, opened[kind, s, h])
-
-        def close_rows(kind, s, halves=(0, 1)):
+        def empty_bank(kind, s, h):
             if (kind, s) not in windows:
-                windows[kind, s] = work.tile([P, S], F32, name=kind, tag=kind, bufs=6 if kind == "back" else 4, align_bytes=64)
-            for h in halves:
-                acc = opened[kind, s, h]
-                first_pass(kind, s, h, 1, acc)
-                nc.scalar.activation(windows[kind, s][:, h * BANK:(h + 1) * BANK], acc[:],
-                                     ACT.Copy if kind == "back" else ACT.Abs)
+                windows[kind, s] = work.tile([P, S], F32, name=kind, tag=kind,
+                                             bufs=SLICES if kind == "back" else 4, align_bytes=64)
+            nc.scalar.activation(windows[kind, s][:, h * BANK:(h + 1) * BANK], banks[kind, s, h][:],
+                                 ACT.Copy if kind == "back" else ACT.Abs)
 
-        def rows(kind, s):
-            open_rows(kind, s)
-            close_rows(kind, s)
+        def half_rows(kind, s, h):
+            for a in range(PASSES):
+                first_pass(kind, s, h, a)
+            empty_bank(kind, s, h)
 
-        near, damp = {}, {}
+        negz = [keep.tile([P, PACK, M], F32, name="negz%d" % b, align_bytes=64) for b in range(GROUPS)]
+        root0 = keep.tile([P, M], F32, name="root0")
+        near, square, damp, ratio = {}, {}, {}, {}
+
+        def z_slot(s):
+            return negz[s // PACK][:, s % PACK, :]
+
+        def root_cols(s, m0, m1):
+            if s == 0:
+                return root0[:, m0:m1]
+            if s == SLICES - 2 and m0 >= HM:
+                return z_slot(SLICES - 1)[:, m0:m1]
+            return z_slot(s - 1)[:, m0:m1]
 
         def pick_near(s):
-            near[s] = turns.tile([P, M], F32, name="near", tag="slot%d" % (s % 3), offset=SLOTS[s % 3])
+            near[s] = work.tile([P, M], F32, name="near", tag="near", bufs=4)
             nc.vector.tensor_copy(near[s][:], windows["back", s][:].indirect(near_list[:]))
 
-        def make_damp(s):
-            b, t = divmod(s, PACK)
-            sq = work.tile([P, M], F32, name="sq", tag="sq", bufs=2)
-            nc.scalar.activation(sq[:], near[s][:], ACT.Square)
-            rs = work.tile([P, M], F32, name="rs", tag="rs", bufs=2)
-            nc.scalar.activation(rs[:], sq[:], ACT.Abs_reciprocal_sqrt, bias=half_t[:, b, t:t + 1])
-            damp[s] = turns.tile([P, M], F32, name="damp", tag="slot%d" % (s % 3), offset=SLOTS[s % 3])
-            nc.scalar.activation(damp[s][:], rs[:], ACT.Square)
+        def square_near(s):
+            square[s] = work.tile([P, M], F32, name="square", tag="square", bufs=2)
+            nc.scalar.activation(square[s][:], near[s][:], ACT.Square, scale=inv_root[:, s:s + 1])
 
-        negz = {}
-        ratio = {}
+        def root(s, m0=0, m1=M):
+            nc.scalar.activation(root_cols(s, m0, m1), square[s][:, m0:m1], ACT.Abs_reciprocal_sqrt, bias=1.0)
 
-        def pick_field(s, m0, m1):
-            if m0 == 0:
-                ratio[s, m0] = work.tile([P, m1 - m0], F32, name="ratio", tag="ratio", bufs=3)
-            else:
-                ratio[s, m0] = turns.tile([P, m1 - m0], F32, name="ratio%d" % s,
-                                          offset=TAB1 if s == SLICES - 2 else TAB1 + 4096)
-            nc.vector.tensor_tensor(ratio[s, m0][:], windows["hail", s][:].indirect(field_list[:, m0 // 16:m1 // 16]),
+        def make_damp(s, m0=0, m1=M):
+            if s not in damp:
+                damp[s] = work.tile([P, M], F32, name="damp", tag="damp", bufs=4)
+            nc.scalar.activation(damp[s][:, m0:m1], root_cols(s, m0, m1), ACT.Square, scale=inv_root[:, s:s + 1])
+
+        def pick_field(s, m0=0, m1=M):
+            if s not in ratio:
+                ratio[s] = work.tile([P, M], F32, name="ratio", tag="ratio", bufs=3)
+            nc.vector.tensor_tensor(ratio[s][:, m0:m1], windows["hail", s][:].indirect(field_list[:, m0 // 16:m1 // 16]),
                                     damp[s][:, m0:m1], ALU.mult)
 
-        def pick_base(s, m0, m1):
-            b, t = divmod(s, PACK)
-            if b not in negz:
-                negz[b] = keep.tile([P, PACK, M], F32, name="negz%d" % b, align_bytes=64)
-            nc.vector.tensor_tensor(negz[b][:, t, m0:m1], windows["back", s][:].indirect(base_list[:, m0 // 16:m1 // 16]),
-                                    ratio[s, m0][:], ALU.subtract)
+        def pick_base(s, m0=0, m1=M):
+            nc.vector.tensor_tensor(z_slot(s)[:, m0:m1], windows["back", s][:].indirect(base_list[:, m0 // 16:m1 // 16]),
+                                    ratio[s][:, m0:m1], ALU.subtract)
 
         z_bf, z_codes, z_scales = {}, {}, {}
 
         def round_z(b, m0, m1, on_vector):
             z_bf[b, m0] = turns.tile([P, m1 - m0, PACK], BF16, name="z_bf%d_%d" % (b, m0), align_bytes=64,
-                                     offset={(0, 0): TAB1, (1, 0): TAB1 + 4096, (1, HALF_M): TAB1 + 6144}[b, m0])
-            dst = z_bf[b, m0][:]
-            src = negz[b][:, :, m0:m1].rearrange("p t m -> p m t")
+                                     offset=2 * PACK * (b * M + m0))
+            dst = z_bf[b, m0][:].rearrange("p (c i) t -> p c t i", i=4)
+            src = negz[b][:, :, m0:m1].rearrange("p t (c i) -> p c t i", i=4)
             if on_vector:
                 nc.vector.tensor_scalar(dst, src, -1.0, None, ALU.mult)
             else:
@@ -212,104 +225,118 @@ def tile_list_hail_indemnity_kernel(tc, tab_words, tab_scales, offs, pos1, pos2,
                                   in_=z_bf[b, m0][:].rearrange("p m t -> p (m t)"))
 
         loss = {}
+        late = {}
+
+        def load_last():
+            late["ded"] = turns.tile([P, NT], F32, name="ded_t", offset=RAW0 + 7680)
+            with nc.allow_non_contiguous_dma(reason="one deductible a partition"):
+                nc.sync.dma_start(late["ded"][:], ded.rearrange("(c p) -> p c", p=P))
+            late["w3s"] = turns.tile([P, PASSES * N // 4], I32, name="w3s", offset=RAW0 + 6144, align_bytes=64)
+            nc.gpsimd.memset(late["w3s"][:], 0)
+            late["w3w"] = turns.tile([P, PASSES, N], I32, name="w3_w", offset=RAW0, align_bytes=64)
+            nc.sync.dma_start(late["w3w"][:], w3_words.rearrange("a p c i -> p a (c i)").bitcast(I32))
+            for q in range(4):
+                nc.sync.dma_start(
+                    late["w3s"][32 * q:32 * q + 4, :].rearrange("r (a c) -> r a c", a=PASSES),
+                    w3_scales.bitcast(I32)[:, 4 * q:4 * q + 4, :].rearrange("a r c -> r a c"))
 
         def last_pass(b, hm):
             for c in range(NT):
+                c2, u = divmod(c, 2)
                 if b == 0:
-                    loss[hm, c] = psum.tile([P, BANK], F32, name="acc", tag="acc")
-                    rhs = z_codes[0, 0][:, hm * HALF_M:(hm + 1) * HALF_M]
-                    rhs_s = z_scales[0, 0][:, hm * HALF_M:(hm + 1) * HALF_M]
+                    if u == 0:
+                        loss[hm, c2] = psum.tile([P, 2, HM], F32, name="acc", tag="acc")
+                    rhs = z_codes[0, 0][:, hm * HM:(hm + 1) * HM]
+                    rhs_s = z_scales[0, 0][:, hm * HM:(hm + 1) * HM]
                 else:
-                    rhs = z_codes[1, hm * HALF_M][:]
-                    rhs_s = z_scales[1, hm * HALF_M][:]
-                nc.tensor.matmul_mx(out=loss[hm, c][:, 0:HALF_M],
-                                    lhsT=w3_w[:, b, c * P:(c + 1) * P].bitcast(FP8X4),
-                                    lhsT_scale=w3s[:].bitcast(U8)[:, b * N + c * P:b * N + (c + 1) * P],
-                                    rhs=rhs.bitcast(FP8X4), rhs_scale=rhs_s, start=(b == 0), stop=(b == 1))
+                    rhs = z_codes[1, hm * HM][:]
+                    rhs_s = z_scales[1, hm * HM][:]
+                nc.tensor.matmul_mx(out=loss[hm, c2][:, u, :],
+                                    lhsT=late["w3w"][:, b, c * P:(c + 1) * P].bitcast(FP8X4),
+                                    lhsT_scale=late["w3s"][:].bitcast(U8)[:, b * N + c * P:b * N + (c + 1) * P],
+                                    rhs=rhs.bitcast(FP8X4), rhs_scale=rhs_s,
+                                    start=(b == 0 and u == 0), stop=(b == 1 and u == 1))
 
-        def finish(hm):
+        def finish(hm, c2, on_vector):
+            res = keep.tile([P, 2, HM], F32, name="res%d_%d" % (hm, c2), align_bytes=64)
             over = {}
-            if hm == 0:
-                for c in range(NT):
-                    over[c] = work.tile([P, HALF_M], F32, name="over", tag="over", bufs=NT)
-                    nc.scalar.activation(over[c][:], loss[hm, c][:, 0:HALF_M], ACT.Relu, bias=neg_ded[:, c:c + 1])
-            for c2 in range(NT // 2):
-                res = keep.tile([P, 2, HALF_M], F32, name="res%d_%d" % (hm, c2), align_bytes=64)
+            for u in range(2):
+                c = 2 * c2 + u
+                if on_vector:
+                    nc.vector.tensor_scalar(res[:, u, :], loss[hm, c2][:, u, :], late["ded"][:, c:c + 1], None, ALU.max)
+                else:
+                    over[u] = work.tile([P, HM], F32, name="over", tag="over", bufs=4)
+                    nc.scalar.activation(over[u][:], loss[hm, c2][:, u, :], ACT.Relu, bias=late["neg"][:, c:c + 1])
+            if not on_vector:
                 for u in range(2):
                     c = 2 * c2 + u
-                    if hm == 0:
-                        nc.scalar.activation(res[:, u, :], over[c][:], ACT.Identity, bias=ded_t[:, c:c + 1])
-                    else:
-                        nc.vector.tensor_scalar(res[:, u, :], loss[hm, c][:, 0:HALF_M], ded_t[:, c:c + 1], None, ALU.max)
-                nc.sync.dma_start(
-                    out[c2 * 2 * P:(c2 + 1) * 2 * P, hm * HALF_M:(hm + 1) * HALF_M].rearrange("(u p) m -> p u m", p=P),
-                    res[:])
-
-        for s in range(2):
-            open_rows("back", s)
-        for s in range(2):
-            close_rows("back", s, (0,))
-        for s in range(2):
-            close_rows("back", s, (1,))
-        cast_w1(0, 0)
-        pick_near(0)
-        cast_w1(1, 0)
-        quant_w1(0, 0)
-        quant_w1(1, 0)
-        load_w1(1)
-        rows("back", 2)
-        make_damp(0)
-        rows("back", 3)
-        pick_near(1)
-        pick_near(2)
-        rows("hail", 0)
-        make_damp(1)
-        for s in range(SLICES - 2):
-            rows("hail", s + 1)
-            if s == 0:
-                cast_w1(0, 1)
-            if s == 1:
-                cast_w1(1, 1, True)
-            pick_field(s, 0, M)
-            if s + 3 < SLICES:
-                pick_near(s + 3)
-            if s < 2:
-                quant_w1(s, 1)
-            pick_base(s, 0, M)
-            if s + 4 < SLICES:
-                rows("back", s + 4)
-            make_damp(s + 2)
-        ded_t = turns.tile([P, NT], F32, name="ded_t", offset=RAW + 7680)
-        with nc.allow_non_contiguous_dma(reason="one deductible a partition"):
-            nc.sync.dma_start(ded_t[:], ded.rearrange("(c p) -> p c", p=P))
-        neg_ded = turns.tile([P, NT], F32, name="neg_ded", offset=RAW + 2048)
-        nc.scalar.activation(neg_ded[:], ded_t[:], ACT.Copy, scale=-1.0)
-        w3s = turns.tile([P, PASSES * N // 4], I32, name="w3s", offset=RAW + 6144, align_bytes=64)
-        nc.gpsimd.memset(w3s[:], 0)
-        for q in range(4):
+                    nc.scalar.activation(res[:, u, :], over[u][:], ACT.Identity, bias=late["ded"][:, c:c + 1])
             nc.sync.dma_start(
-                w3s[32 * q:32 * q + 4, :].rearrange("r (a c) -> r a c", a=PASSES),
-                w3_scales.bitcast(I32)[:, 4 * q:4 * q + 4, :].rearrange("a r c -> r a c"))
-        w3_w = turns.tile([P, PASSES, N], I32, name="w3_w", offset=RAW + 8192, align_bytes=64)
-        nc.sync.dma_start(w3_w[:], w3_words.rearrange("a p c i -> p a (c i)").bitcast(I32))
-        rows("hail", SLICES - 1)
+                out[c2 * 2 * P:(c2 + 1) * 2 * P, hm * HM:(hm + 1) * HM].rearrange("(u p) m -> p u m", p=P), res[:])
+
+        for s, h in ((0, 0), (1, 0), (0, 1), (1, 1), (2, 0), (2, 1), (3, 0), (3, 1)):
+            half_rows("back", s, h)
+        for a in range(PASSES):
+            cast_w1(a, 0)
+            quant_w1(a, 0)
+            pick_near(2 * a)
+            pick_near(2 * a + 1)
+        load_last()
+        for s in range(2):
+            square_near(s)
+            half_rows("back", PACK + s, 0)
+            root(s)
+            half_rows("back", PACK + s, 1)
+            cast_w1(s, 1)
+            quant_w1(s, 1)
+            pick_near(PACK + s)
+        late["neg"] = keep.tile([P, NT], F32, name="neg_ded")
+        for s in range(SLICES - 2):
+            half_rows("hail", s, 0)
+            square_near(s + 2)
+            half_rows("hail", s, 1)
+            make_damp(s)
+            pick_field(s)
+            if s > 0:
+                pick_base(s - 1)
+            if s + 2 == SLICES - 2:
+                root(s + 2, 0, HM)
+                root(s + 2, HM, M)
+            else:
+                root(s + 2)
+            if s < 2:
+                for h in range(2):
+                    half_rows("back", SLICES - 2 + s, h)
+                pick_near(SLICES - 2 + s)
+        nc.scalar.activation(late["neg"][:], late["ded"][:], ACT.Copy, scale=-1.0)
+        s6, s7 = SLICES - 2, SLICES - 1
+        for s in (s6, s7):
+            for h in range(2):
+                half_rows("hail", s, h)
+        make_damp(s6, 0, HM)
+        pick_field(s6, 0, HM)
+        pick_base(s6 - 1)
+        make_damp(s7, 0, HM)
+        pick_field(s7, 0, HM)
+        pick_base(s6, 0, HM)
+        pick_base(s7, 0, HM)
         round_z(0, 0, M, False)
-        pick_field(SLICES - 2, 0, HALF_M)
-        pick_field(SLICES - 1, 0, HALF_M)
-        pick_base(SLICES - 2, 0, HALF_M)
-        pick_base(SLICES - 1, 0, HALF_M)
-        round_z(1, 0, HALF_M, False)
         quant_z(0, 0, M)
         last_pass(0, 0)
-        pick_field(SLICES - 2, HALF_M, M)
-        pick_base(SLICES - 2, HALF_M, M)
-        quant_z(1, 0, HALF_M)
-        last_pass(1, 0)
-        pick_field(SLICES - 1, HALF_M, M)
-        pick_base(SLICES - 1, HALF_M, M)
-        round_z(1, HALF_M, M, True)
-        finish(0)
         last_pass(0, 1)
-        quant_z(1, HALF_M, M)
+        make_damp(s6, HM, M)
+        pick_field(s6, HM, M)
+        round_z(1, 0, HM, False)
+        quant_z(1, 0, HM)
+        last_pass(1, 0)
+        make_damp(s7, HM, M)
+        pick_field(s7, HM, M)
+        pick_base(s6, HM, M)
+        pick_base(s7, HM, M)
+        round_z(1, HM, M, True)
+        for c2 in range(NT // 2):
+            finish(0, c2, False)
+        quant_z(1, HM, M)
         last_pass(1, 1)
-        finish(1)
+        for c2 in range(NT // 2):
+            finish(1, c2, True)

@@ -27,12 +27,9 @@ NT = N // P
 HM = M // 2
 TAB_BYTES = 4 * T
 RAW_BYTES = 4 * PACK * KP
-V_ROWS = TAB_BYTES
-RAW0 = V_ROWS + S // 2 - RAW_BYTES
-W2_RAW = V_ROWS + S
-W2S_RAW = W2_RAW + PASSES * 2 * H
-TAB1 = RAW0 + 2 * RAW_BYTES
-TAB_ROWS = TAB1 + TAB_BYTES
+TAB1 = TAB_BYTES
+TAB_ROWS = 2 * TAB_BYTES
+RAW0 = 0
 
 
 def tile_list_hail_indemnity_kernel(tc, tab_words, tab_scales, offs, pos1, pos2, pos3, w1,
@@ -46,7 +43,7 @@ def tile_list_hail_indemnity_kernel(tc, tab_words, tab_scales, offs, pos1, pos2,
 
         tab_rows = turns.tile([P, T // 4], I32, name="tab_rows", offset=TAB_ROWS, align_bytes=64)
         nc.vector.memset(tab_rows[:], 0)
-        w2s_raw = turns.tile([P, PASSES * H // 4], I32, name="w2s_raw", offset=W2S_RAW, align_bytes=64)
+        w2s_raw = keep.tile([P, PASSES * H // 4], I32, name="w2s_raw", align_bytes=64)
         nc.gpsimd.memset(w2s_raw[:], 0)
         planes = keep.tile([P, PASSES * S // 4], I32, name="planes", align_bytes=64)
         nc.vector.memset(planes[:], 0)
@@ -62,7 +59,7 @@ def tile_list_hail_indemnity_kernel(tc, tab_words, tab_scales, offs, pos1, pos2,
         nc.sync.dma_start(half_t[:], half.rearrange("(b p t) -> p b t", b=GROUPS, t=PACK))
         inv_root = keep.tile([P, SLICES], F32, name="inv_root")
         nc.scalar.activation(inv_root[:], half_t[:].rearrange("p b t -> p (b t)"), ACT.Abs_reciprocal_sqrt)
-        w2_raw = turns.tile([P, PASSES, H // 2], I32, name="w2_raw", offset=W2_RAW, align_bytes=64)
+        w2_raw = keep.tile([P, PASSES, H // 2], I32, name="w2_raw", align_bytes=64)
         nc.sync.dma_start(w2_raw[:], w2_words.bitcast(I32).rearrange("a p c -> p a c"))
         load_list("pos2", pos2)
         load_list("pos1", pos1)
@@ -77,7 +74,7 @@ def tile_list_hail_indemnity_kernel(tc, tab_words, tab_scales, offs, pos1, pos2,
                     nc.scalar.dma_start(
                         w2s_raw[32 * q:32 * q + 4, :].rearrange("r (a c) -> r a c", a=PASSES),
                         w2_scales.bitcast(I32)[:, 4 * q:4 * q + 4, :].rearrange("a r c -> r a c"))
-                nc.sync.dma_start(tab_rows[0:P:4, :], tab_scales.rearrange("a q t -> (a q) t").bitcast(I32))
+                nc.scalar.dma_start(tab_rows[0:P:4, :], tab_scales.rearrange("a q t -> (a q) t").bitcast(I32))
 
         w2c = keep.tile([P, PASSES * H * 2], U8, name="w2c", align_bytes=64)
         nc.vector.tensor_copy(
@@ -89,13 +86,13 @@ def tile_list_hail_indemnity_kernel(tc, tab_words, tab_scales, offs, pos1, pos2,
             w2s[:].rearrange("p (g t m n) -> p g m t n", t=PACK, m=P // 16, n=16),
             w2s_raw[:].bitcast(U8).rearrange("p (g m n t) -> p g m t n", t=PACK, m=P // 16, n=16))
 
-        v_rows = turns.tile([P, S // 4], I32, name="v_rows", offset=V_ROWS, align_bytes=64)
+        v_rows = keep.tile([P, S // 4], I32, name="v_rows", align_bytes=64)
         nc.vector.tensor_copy(v_rows[:].bitcast(U8), tab_rows[:].bitcast(U8).indirect(offs_t[:]))
         v_planes = [planes[:, a * (S // 4):(a + 1) * (S // 4)] for a in range(PASSES)]
         for a in range(PASSES):
             for q in range(4):
                 first = 64 * a + 16 * q
-                queue = nc.gpsimd if 4 * a + q == 7 else nc.scalar
+                queue = nc.gpsimd if 4 * a + q >= 6 else nc.scalar
                 queue.dma_start(v_planes[a][32 * q:32 * q + 4, :], v_rows[first:first + 16:4, :])
         v_words = {}
         whole = turns.tile([P, S], I32, name="v_words0", offset=TAB_ROWS, align_bytes=64)
@@ -138,7 +135,7 @@ def tile_list_hail_indemnity_kernel(tc, tab_words, tab_scales, offs, pos1, pos2,
 
         def first_pass(kind, s, h, a):
             b, t = divmod(s, PACK)
-            if a == 0:
+            if a == PASSES - 1:
                 banks[kind, s, h] = psum.tile([P, BANK], F32, name="acc", tag="acc")
             if kind == "back":
                 c0 = a * H + s * P
@@ -150,21 +147,26 @@ def tile_list_hail_indemnity_kernel(tc, tab_words, tab_scales, offs, pos1, pos2,
             nc.tensor.matmul_mx(out=banks[kind, s, h][:], lhsT=lhs, lhsT_scale=lhs_s,
                                 rhs=v_words[a, h].bitcast(FP8X4),
                                 rhs_scale=v_planes[a].bitcast(U8)[:, h * BANK:(h + 1) * BANK],
-                                start=(a == 0), stop=(a == PASSES - 1))
+                                start=(a == PASSES - 1), stop=(a == 0))
 
         windows = {}
 
-        def empty_bank(kind, s, h):
+        def empty_bank(kind, s, h, on_vector=False):
             if (kind, s) not in windows:
                 windows[kind, s] = work.tile([P, S], F32, name=kind, tag=kind,
                                              bufs=SLICES if kind == "back" else 4, align_bytes=64)
-            nc.scalar.activation(windows[kind, s][:, h * BANK:(h + 1) * BANK], banks[kind, s, h][:],
-                                 ACT.Copy if kind == "back" else ACT.Abs)
+            dst = windows[kind, s][:, h * BANK:(h + 1) * BANK]
+            if on_vector:
+                nc.vector.tensor_copy(dst, banks[kind, s, h][:])
+            elif kind == "back":
+                nc.scalar.copy(dst, banks[kind, s, h][:])
+            else:
+                nc.scalar.activation(dst, banks[kind, s, h][:], ACT.Abs)
 
-        def half_rows(kind, s, h):
-            for a in range(PASSES):
+        def half_rows(kind, s, h, on_vector=False):
+            for a in reversed(range(PASSES)):
                 first_pass(kind, s, h, a)
-            empty_bank(kind, s, h)
+            empty_bank(kind, s, h, on_vector)
 
         negz = [keep.tile([P, PACK, M], F32, name="negz%d" % b, align_bytes=64) for b in range(GROUPS)]
         root0 = keep.tile([P, M], F32, name="root0")
@@ -181,7 +183,12 @@ def tile_list_hail_indemnity_kernel(tc, tab_words, tab_scales, offs, pos1, pos2,
             return z_slot(s - 1)[:, m0:m1]
 
         def pick_near(s):
-            near[s] = work.tile([P, M], F32, name="near", tag="near", bufs=4)
+            if s < 2:
+                near[s] = turns.tile([P, M], F32, name="near%d" % s, offset=4 * M * s)
+            elif s < 2 + PACK:
+                near[s] = turns.tile([P, M], F32, name="near%d" % s, offset=RAW_BYTES + 4 * M * (s - 2))
+            else:
+                near[s] = work.tile([P, M], F32, name="near", tag="near", bufs=2)
             nc.vector.tensor_copy(near[s][:], windows["back", s][:].indirect(near_list[:]))
 
         def square_near(s):
@@ -210,7 +217,7 @@ def tile_list_hail_indemnity_kernel(tc, tab_words, tab_scales, offs, pos1, pos2,
 
         def round_z(b, m0, m1, on_vector):
             z_bf[b, m0] = turns.tile([P, m1 - m0, PACK], BF16, name="z_bf%d_%d" % (b, m0), align_bytes=64,
-                                     offset=2 * PACK * (b * M + m0))
+                                     offset=RAW_BYTES + 2 * PACK * (b * M + m0))
             dst = z_bf[b, m0][:].rearrange("p (c i) t -> p c t i", i=4)
             src = negz[b][:, :, m0:m1].rearrange("p t (c i) -> p c t i", i=4)
             if on_vector:
@@ -240,48 +247,49 @@ def tile_list_hail_indemnity_kernel(tc, tab_words, tab_scales, offs, pos1, pos2,
                     late["w3s"][32 * q:32 * q + 4, :].rearrange("r (a c) -> r a c", a=PASSES),
                     w3_scales.bitcast(I32)[:, 4 * q:4 * q + 4, :].rearrange("a r c -> r a c"))
 
-        def last_pass(b, hm):
-            for c in range(NT):
-                c2, u = divmod(c, 2)
-                if b == 0:
-                    if u == 0:
-                        loss[hm, c2] = psum.tile([P, 2, HM], F32, name="acc", tag="acc")
-                    rhs = z_codes[0, 0][:, hm * HM:(hm + 1) * HM]
-                    rhs_s = z_scales[0, 0][:, hm * HM:(hm + 1) * HM]
-                else:
-                    rhs = z_codes[1, hm * HM][:]
-                    rhs_s = z_scales[1, hm * HM][:]
-                nc.tensor.matmul_mx(out=loss[hm, c2][:, u, :],
-                                    lhsT=late["w3w"][:, b, c * P:(c + 1) * P].bitcast(FP8X4),
-                                    lhsT_scale=late["w3s"][:].bitcast(U8)[:, b * N + c * P:b * N + (c + 1) * P],
-                                    rhs=rhs.bitcast(FP8X4), rhs_scale=rhs_s,
-                                    start=(b == 0 and u == 0), stop=(b == 1 and u == 1))
+        def bank_groups(m0, m1):
+            per_bank = BANK // (m1 - m0)
+            return [range(c0, min(c0 + per_bank, NT)) for c0 in range(0, NT, per_bank)]
 
-        def finish(hm, c2, on_vector):
-            res = keep.tile([P, 2, HM], F32, name="res%d_%d" % (hm, c2), align_bytes=64)
-            over = {}
-            for u in range(2):
-                c = 2 * c2 + u
-                if on_vector:
-                    nc.vector.tensor_scalar(res[:, u, :], loss[hm, c2][:, u, :], late["ded"][:, c:c + 1], None, ALU.max)
+        def last_pass(b, m0, m1):
+            for group in bank_groups(m0, m1):
+                if b == 0:
+                    loss[m0, group[0]] = psum.tile([P, len(group), m1 - m0], F32, name="acc", tag="acc")
+                    rhs, rhs_s = z_codes[0, 0][:, m0:m1], z_scales[0, 0][:, m0:m1]
                 else:
-                    over[u] = work.tile([P, HM], F32, name="over", tag="over", bufs=4)
-                    nc.scalar.activation(over[u][:], loss[hm, c2][:, u, :], ACT.Relu, bias=late["neg"][:, c:c + 1])
-            if not on_vector:
-                for u in range(2):
-                    c = 2 * c2 + u
-                    nc.scalar.activation(res[:, u, :], over[u][:], ACT.Identity, bias=late["ded"][:, c:c + 1])
-            nc.sync.dma_start(
-                out[c2 * 2 * P:(c2 + 1) * 2 * P, hm * HM:(hm + 1) * HM].rearrange("(u p) m -> p u m", p=P), res[:])
+                    rhs, rhs_s = z_codes[1, m0][:], z_scales[1, m0][:]
+                for u, c in enumerate(group):
+                    nc.tensor.matmul_mx(out=loss[m0, group[0]][:, u, :],
+                                        lhsT=late["w3w"][:, b, c * P:(c + 1) * P].bitcast(FP8X4),
+                                        lhsT_scale=late["w3s"][:].bitcast(U8)[:, b * N + c * P:b * N + (c + 1) * P],
+                                        rhs=rhs.bitcast(FP8X4), rhs_scale=rhs_s,
+                                        start=(b == 0 and u == 0), stop=(b == 1 and u == len(group) - 1))
+
+        def finish(m0, m1, group, on_vector):
+            n, c0 = len(group), group[0]
+            acc = loss[m0, c0]
+            res = keep.tile([P, n, m1 - m0], F32, name="res%d_%d" % (m0, c0), align_bytes=64)
+            if on_vector:
+                nc.vector.tensor_tensor(res[:], acc[:],
+                                        late["ded"][:, c0:c0 + n].unsqueeze(2).to_broadcast([P, n, m1 - m0]), ALU.max)
+            else:
+                over = work.tile([P, n, m1 - m0], F32, name="over", tag="over", bufs=2)
+                for u, c in enumerate(group):
+                    nc.scalar.activation(over[:, u, :], acc[:, u, :], ACT.Relu, bias=late["neg"][:, c:c + 1])
+                for u, c in enumerate(group):
+                    nc.scalar.activation(res[:, u, :], over[:, u, :], ACT.Identity, bias=late["ded"][:, c:c + 1])
+            nc.sync.dma_start(out[c0 * P:(c0 + n) * P, m0:m1].rearrange("(u p) m -> p u m", p=P), res[:])
 
         for s, h in ((0, 0), (1, 0), (0, 1), (1, 1), (2, 0), (2, 1), (3, 0), (3, 1)):
             half_rows("back", s, h)
-        for a in range(PASSES):
-            cast_w1(a, 0)
-            quant_w1(a, 0)
-            pick_near(2 * a)
-            pick_near(2 * a + 1)
-        load_last()
+        cast_w1(0, 0)
+        quant_w1(0, 0)
+        pick_near(0)
+        pick_near(1)
+        cast_w1(1, 0)
+        pick_near(2)
+        quant_w1(1, 0)
+        pick_near(3)
         for s in range(2):
             square_near(s)
             half_rows("back", PACK + s, 0)
@@ -290,6 +298,7 @@ def tile_list_hail_indemnity_kernel(tc, tab_words, tab_scales, offs, pos1, pos2,
             cast_w1(s, 1)
             quant_w1(s, 1)
             pick_near(PACK + s)
+        load_last()
         late["neg"] = keep.tile([P, NT], F32, name="neg_ded")
         for s in range(SLICES - 2):
             half_rows("hail", s, 0)
@@ -313,30 +322,31 @@ def tile_list_hail_indemnity_kernel(tc, tab_words, tab_scales, offs, pos1, pos2,
         for s in (s6, s7):
             for h in range(2):
                 half_rows("hail", s, h)
-        make_damp(s6, 0, HM)
-        pick_field(s6, 0, HM)
-        pick_base(s6 - 1)
-        make_damp(s7, 0, HM)
-        pick_field(s7, 0, HM)
-        pick_base(s6, 0, HM)
-        pick_base(s7, 0, HM)
-        round_z(0, 0, M, False)
-        quant_z(0, 0, M)
-        last_pass(0, 0)
-        last_pass(0, 1)
-        make_damp(s6, HM, M)
-        pick_field(s6, HM, M)
-        round_z(1, 0, HM, False)
-        quant_z(1, 0, HM)
-        last_pass(1, 0)
-        make_damp(s7, HM, M)
-        pick_field(s7, HM, M)
-        pick_base(s6, HM, M)
-        pick_base(s7, HM, M)
-        round_z(1, HM, M, True)
-        for c2 in range(NT // 2):
-            finish(0, c2, False)
-        quant_z(1, HM, M)
-        last_pass(1, 1)
-        for c2 in range(NT // 2):
-            finish(1, c2, True)
+        cuts = (0, HM, HM + HM // 2, M)
+        chunks = list(zip(cuts[:-1], cuts[1:]))
+        for i, (m0, m1) in enumerate(chunks):
+            make_damp(s6, m0, m1)
+            pick_field(s6, m0, m1)
+            if i == 0:
+                pick_base(s6 - 1)
+            else:
+                round_z(1, *chunks[i - 1], False)
+                quant_z(1, *chunks[i - 1])
+                last_pass(1, *chunks[i - 1])
+            make_damp(s7, m0, m1)
+            pick_field(s7, m0, m1)
+            pick_base(s6, m0, m1)
+            pick_base(s7, m0, m1)
+            if i == 0:
+                round_z(0, 0, M, False)
+                quant_z(0, 0, M)
+                for c in chunks:
+                    last_pass(0, *c)
+        round_z(1, *chunks[-1], True)
+        quant_z(1, *chunks[-1])
+        last_pass(1, *chunks[-1])
+        for group in bank_groups(*chunks[0]):
+            finish(*chunks[0], group, False)
+        for c in chunks[1:]:
+            for group in bank_groups(*c):
+                finish(*c, group, True)

@@ -30,6 +30,7 @@ RAW_BYTES = 4 * PACK * KP
 TAB1 = TAB_BYTES
 TAB_ROWS = 2 * TAB_BYTES
 RAW0 = 0
+W1_BF = TAB_ROWS + T
 
 
 def tile_list_hail_indemnity_kernel(tc, tab_words, tab_scales, offs, pos1, pos2, pos3, w1,
@@ -121,9 +122,16 @@ def tile_list_hail_indemnity_kernel(tc, tab_words, tab_scales, offs, pos1, pos2,
         w1_bf, w1_codes, w1_scales = {}, {}, {}
 
         def cast_w1(a, b):
-            w1_bf[a, b] = work.tile([P, PACK, P, PACK], BF16, name="w1_bf", tag="w1_bf", bufs=2, align_bytes=64)
-            nc.vector.tensor_copy(w1_bf[a, b][:].rearrange("p t m j -> p m j t"),
-                                  w1_raw[a, b][:].rearrange("p j (m t) -> p m j t", t=PACK))
+            w1_bf[a, b] = turns.tile([P, PACK, P, PACK], BF16, name="w1_bf%d%d" % (a, b), align_bytes=64,
+                                     offset=W1_BF + 4 * S * (2 * b + a))
+            if (a, b) == (0, 0):
+                nc.vector.tensor_copy(w1_bf[a, b][:].rearrange("p t m j -> p m j t"),
+                                      w1_raw[a, b][:].rearrange("p j (m t) -> p m j t", t=PACK))
+                return
+            dst = w1_bf[a, b][:].rearrange("p t m j -> p m t j")
+            src = w1_raw[a, b][:].rearrange("p j (m t) -> p m t j", t=PACK)
+            for m0 in range(0, P, P // 4):
+                nc.gpsimd.tensor_scalar(dst[:, m0:m0 + P // 4], src[:, m0:m0 + P // 4], 1.0, 0.0, ALU.mult, ALU.add)
 
         def quant_w1(a, b):
             w1_codes[a, b] = keep.tile([P, KP], U32, name="w1_codes%d%d" % (a, b), align_bytes=64)
@@ -135,7 +143,8 @@ def tile_list_hail_indemnity_kernel(tc, tab_words, tab_scales, offs, pos1, pos2,
 
         def first_pass(kind, s, h, a):
             b, t = divmod(s, PACK)
-            if a == PASSES - 1:
+            opens = (kind, s, h) not in banks
+            if opens:
                 banks[kind, s, h] = psum.tile([P, BANK], F32, name="acc", tag="acc")
             if kind == "back":
                 c0 = a * H + s * P
@@ -147,14 +156,18 @@ def tile_list_hail_indemnity_kernel(tc, tab_words, tab_scales, offs, pos1, pos2,
             nc.tensor.matmul_mx(out=banks[kind, s, h][:], lhsT=lhs, lhsT_scale=lhs_s,
                                 rhs=v_words[a, h].bitcast(FP8X4),
                                 rhs_scale=v_planes[a].bitcast(U8)[:, h * BANK:(h + 1) * BANK],
-                                start=(a == PASSES - 1), stop=(a == 0))
+                                start=opens, stop=not opens)
 
         windows = {}
 
         def empty_bank(kind, s, h, on_vector=False):
             if (kind, s) not in windows:
-                windows[kind, s] = work.tile([P, S], F32, name=kind, tag=kind,
-                                             bufs=SLICES if kind == "back" else 4, align_bytes=64)
+                if kind == "back" and s >= SLICES - 2:
+                    windows[kind, s] = turns.tile([P, S], F32, name="back%d" % s, align_bytes=64,
+                                                  offset=W1_BF + 4 * S * (s - PACK))
+                else:
+                    windows[kind, s] = work.tile([P, S], F32, name=kind, tag=kind,
+                                                 bufs=SLICES - 2 if kind == "back" else 4, align_bytes=64)
             dst = windows[kind, s][:, h * BANK:(h + 1) * BANK]
             if on_vector:
                 nc.vector.tensor_copy(dst, banks[kind, s, h][:])
@@ -164,7 +177,8 @@ def tile_list_hail_indemnity_kernel(tc, tab_words, tab_scales, offs, pos1, pos2,
                 nc.scalar.activation(dst, banks[kind, s, h][:], ACT.Abs)
 
         def half_rows(kind, s, h, on_vector=False):
-            for a in reversed(range(PASSES)):
+            order = range(PASSES) if kind == "back" and s < 2 else reversed(range(PASSES))
+            for a in order:
                 first_pass(kind, s, h, a)
             empty_bank(kind, s, h, on_vector)
 
@@ -185,14 +199,17 @@ def tile_list_hail_indemnity_kernel(tc, tab_words, tab_scales, offs, pos1, pos2,
         def pick_near(s):
             if s < 2:
                 near[s] = turns.tile([P, M], F32, name="near%d" % s, offset=4 * M * s)
-            elif s < 2 + PACK:
-                near[s] = turns.tile([P, M], F32, name="near%d" % s, offset=RAW_BYTES + 4 * M * (s - 2))
+            elif s in (PACK, PACK + 1):
+                near[s] = turns.tile([P, M], F32, name="near%d" % s, offset=RAW_BYTES + 4 * M * (s - PACK))
             else:
                 near[s] = work.tile([P, M], F32, name="near", tag="near", bufs=2)
             nc.vector.tensor_copy(near[s][:], windows["back", s][:].indirect(near_list[:]))
 
         def square_near(s):
-            square[s] = work.tile([P, M], F32, name="square", tag="square", bufs=2)
+            if s in (2, 3):
+                square[s] = turns.tile([P, M], F32, name="square%d" % s, offset=W1_BF + 4 * S + 4 * M * (s - 2))
+            else:
+                square[s] = work.tile([P, M], F32, name="square", tag="square", bufs=2)
             nc.scalar.activation(square[s][:], near[s][:], ACT.Square, scale=inv_root[:, s:s + 1])
 
         def root(s, m0=0, m1=M):
@@ -288,8 +305,8 @@ def tile_list_hail_indemnity_kernel(tc, tab_words, tab_scales, offs, pos1, pos2,
         pick_near(1)
         cast_w1(1, 0)
         pick_near(2)
-        quant_w1(1, 0)
         pick_near(3)
+        quant_w1(1, 0)
         for s in range(2):
             square_near(s)
             half_rows("back", PACK + s, 0)
@@ -315,7 +332,7 @@ def tile_list_hail_indemnity_kernel(tc, tab_words, tab_scales, offs, pos1, pos2,
                 root(s + 2)
             if s < 2:
                 for h in range(2):
-                    half_rows("back", SLICES - 2 + s, h)
+                    half_rows("back", SLICES - 2 + s, h, s == 1)
                 pick_near(SLICES - 2 + s)
         nc.scalar.activation(late["neg"][:], late["ded"][:], ACT.Copy, scale=-1.0)
         s6, s7 = SLICES - 2, SLICES - 1
@@ -329,10 +346,6 @@ def tile_list_hail_indemnity_kernel(tc, tab_words, tab_scales, offs, pos1, pos2,
             pick_field(s6, m0, m1)
             if i == 0:
                 pick_base(s6 - 1)
-            else:
-                round_z(1, *chunks[i - 1], False)
-                quant_z(1, *chunks[i - 1])
-                last_pass(1, *chunks[i - 1])
             make_damp(s7, m0, m1)
             pick_field(s7, m0, m1)
             pick_base(s6, m0, m1)
@@ -342,6 +355,10 @@ def tile_list_hail_indemnity_kernel(tc, tab_words, tab_scales, offs, pos1, pos2,
                 quant_z(0, 0, M)
                 for c in chunks:
                     last_pass(0, *c)
+            else:
+                round_z(1, *chunks[i - 1], False)
+                quant_z(1, *chunks[i - 1])
+                last_pass(1, *chunks[i - 1])
         round_z(1, *chunks[-1], True)
         quant_z(1, *chunks[-1])
         last_pass(1, *chunks[-1])

@@ -40,7 +40,7 @@ def tile_list_hail_indemnity_kernel(tc, tab_words, tab_scales, offs, pos1, pos2,
         keep = ctx.enter_context(tc.tile_pool(name="keep", bufs=1))
         turns = ctx.enter_context(tc.tile_pool(name="turns", bufs=1))
         work = ctx.enter_context(tc.tile_pool(name="work", bufs=2))
-        psum = ctx.enter_context(tc.psum_pool(name="psum", bufs=8))
+        psum = ctx.enter_context(tc.psum_pool(name="psum", bufs=4))
 
         tab_rows = turns.tile([P, T // 4], I32, name="tab_rows", offset=TAB_ROWS, align_bytes=64)
         nc.vector.memset(tab_rows[:], 0)
@@ -60,6 +60,8 @@ def tile_list_hail_indemnity_kernel(tc, tab_words, tab_scales, offs, pos1, pos2,
         nc.sync.dma_start(half_t[:], half.rearrange("(b p t) -> p b t", b=GROUPS, t=PACK))
         inv_root = keep.tile([P, SLICES], F32, name="inv_root")
         nc.scalar.activation(inv_root[:], half_t[:].rearrange("p b t -> p (b t)"), ACT.Abs_reciprocal_sqrt)
+        half_k = keep.tile([P, SLICES], F32, name="half_k")
+        nc.scalar.activation(half_k[:], half_t[:].rearrange("p b t -> p (b t)"), ACT.Identity)
         w2_raw = keep.tile([P, PASSES, H // 2], I32, name="w2_raw", align_bytes=64)
         nc.sync.dma_start(w2_raw[:], w2_words.bitcast(I32).rearrange("a p c -> p a c"))
         load_list("pos2", pos2)
@@ -123,7 +125,7 @@ def tile_list_hail_indemnity_kernel(tc, tab_words, tab_scales, offs, pos1, pos2,
 
         def cast_w1(a, b):
             w1_bf[a, b] = turns.tile([P, PACK, P, PACK], BF16, name="w1_bf%d%d" % (a, b), align_bytes=64,
-                                     offset=W1_BF + 4 * S * (2 * b + a))
+                                     offset=W1_BF + 4 * S * min(2 * b + a, 1))
             if (a, b) == (0, 0):
                 nc.vector.tensor_copy(w1_bf[a, b][:].rearrange("p t m j -> p m j t"),
                                       w1_raw[a, b][:].rearrange("p j (m t) -> p m j t", t=PACK))
@@ -139,102 +141,102 @@ def tile_list_hail_indemnity_kernel(tc, tab_words, tab_scales, offs, pos1, pos2,
             nc.vector.quantize_mx(out=w1_codes[a, b][:].bitcast(FP8X4), scales=w1_scales[a, b][:],
                                   in_=w1_bf[a, b][:].rearrange("p t m j -> p (t m j)"))
 
-        banks = {}
-
-        def first_pass(kind, s, h, a):
-            b, t = divmod(s, PACK)
-            opens = (kind, s, h) not in banks
-            if opens:
-                banks[kind, s, h] = psum.tile([P, BANK], F32, name="acc", tag="acc")
-            if kind == "back":
-                c0 = a * H + s * P
-                lhs = w2c[:, 2 * c0:2 * (c0 + P)].bitcast(FP4X4)
-                lhs_s = w2s[:, c0:c0 + P]
-            else:
-                lhs = w1_codes[a, b][:, t * P:(t + 1) * P].bitcast(FP8X4)
-                lhs_s = w1_scales[a, b][:, t * P:(t + 1) * P]
-            nc.tensor.matmul_mx(out=banks[kind, s, h][:], lhsT=lhs, lhsT_scale=lhs_s,
-                                rhs=v_words[a, h].bitcast(FP8X4),
-                                rhs_scale=v_planes[a].bitcast(U8)[:, h * BANK:(h + 1) * BANK],
-                                start=opens, stop=not opens)
-
         windows = {}
 
-        def empty_bank(kind, s, h, on_vector=False):
+        def rows(kind, s, h):
+            b, t = divmod(s, PACK)
+            bank = psum.tile([P, BANK], F32, name=kind + "_acc", tag=kind, bufs=4)
+            order = range(PASSES) if kind == "back" and s < 2 else reversed(range(PASSES))
+            for i, a in enumerate(order):
+                if kind == "back":
+                    c0 = a * H + s * P
+                    lhs = w2c[:, 2 * c0:2 * (c0 + P)].bitcast(FP4X4)
+                    lhs_s = w2s[:, c0:c0 + P]
+                else:
+                    lhs = w1_codes[a, b][:, t * P:(t + 1) * P].bitcast(FP8X4)
+                    lhs_s = w1_scales[a, b][:, t * P:(t + 1) * P]
+                nc.tensor.matmul_mx(out=bank[:], lhsT=lhs, lhsT_scale=lhs_s,
+                                    rhs=v_words[a, h].bitcast(FP8X4),
+                                    rhs_scale=v_planes[a].bitcast(U8)[:, h * BANK:(h + 1) * BANK],
+                                    start=(i == 0), stop=(i == PASSES - 1))
             if (kind, s) not in windows:
-                if kind == "back" and s >= SLICES - 2:
-                    windows[kind, s] = turns.tile([P, S], F32, name="back%d" % s, align_bytes=64,
-                                                  offset=W1_BF + 4 * S * (s - PACK))
+                if kind == "back" and s == SLICES - 1:
+                    windows[kind, s] = turns.tile([P, S], F32, name="back%d" % s, align_bytes=64, offset=TAB1 + 4 * S)
                 else:
                     windows[kind, s] = work.tile([P, S], F32, name=kind, tag=kind,
-                                                 bufs=SLICES - 2 if kind == "back" else 4, align_bytes=64)
+                                                 bufs=SLICES - 1 if kind == "back" else 4, align_bytes=64)
             dst = windows[kind, s][:, h * BANK:(h + 1) * BANK]
-            if on_vector:
-                nc.vector.tensor_copy(dst, banks[kind, s, h][:])
+            if kind == "back" and s == SLICES - 1:
+                nc.vector.tensor_copy(dst, bank[:])
             elif kind == "back":
-                nc.scalar.copy(dst, banks[kind, s, h][:])
+                nc.scalar.copy(dst, bank[:])
             else:
-                nc.scalar.activation(dst, banks[kind, s, h][:], ACT.Abs)
+                nc.scalar.activation(dst, bank[:], ACT.Abs)
 
-        def half_rows(kind, s, h, on_vector=False):
-            order = range(PASSES) if kind == "back" and s < 2 else reversed(range(PASSES))
-            for a in order:
-                first_pass(kind, s, h, a)
-            empty_bank(kind, s, h, on_vector)
+        def window(kind, s):
+            for h in range(2):
+                rows(kind, s, h)
 
         negz = [keep.tile([P, PACK, M], F32, name="negz%d" % b, align_bytes=64) for b in range(GROUPS)]
-        root0 = keep.tile([P, M], F32, name="root0")
-        near, square, damp, ratio = {}, {}, {}, {}
+        near, square, root, damp, ratio = {}, {}, {}, {}, {}
 
-        def z_slot(s):
-            return negz[s // PACK][:, s % PACK, :]
-
-        def root_cols(s, m0, m1):
-            if s == 0:
-                return root0[:, m0:m1]
-            if s == SLICES - 2 and m0 >= HM:
-                return z_slot(SLICES - 1)[:, m0:m1]
-            return z_slot(s - 1)[:, m0:m1]
+        def pair_tile(store, name, s, bufs):
+            if s // 2 not in store:
+                store[s // 2] = work.tile([P, 2, M], F32, name=name, tag=name, bufs=bufs)
+            return store[s // 2]
 
         def pick_near(s):
+            if s == 3:
+                dst = turns.tile([P, M], F32, name="near3", offset=RAW_BYTES)[:]
+            elif s < 3:
+                dst = work.tile([P, M], F32, name="near_one", tag="near_one", bufs=3)[:]
+            else:
+                if s // 2 not in near:
+                    if s == SLICES - 2:
+                        near[s // 2] = turns.tile([P, 2, M], F32, name="near67", offset=TAB1)
+                    else:
+                        near[s // 2] = turns.tile([P, 2, M], F32, name="near45", offset=RAW_BYTES + 4 * M)
+                dst = near[s // 2][:, s % 2, :]
+            near["one", s] = dst
+            nc.vector.tensor_copy(dst, windows["back", s][:].indirect(near_list[:]))
+
+        def square_one(s):
+            dst = pair_tile(square, "square", s, 2)[:, s % 2, :]
             if s < 2:
-                near[s] = turns.tile([P, M], F32, name="near%d" % s, offset=4 * M * s)
-            elif s in (PACK, PACK + 1):
-                near[s] = turns.tile([P, M], F32, name="near%d" % s, offset=RAW_BYTES + 4 * M * (s - PACK))
+                nc.scalar.activation(dst, near["one", s], ACT.Square, scale=inv_root[:, s:s + 1])
             else:
-                near[s] = work.tile([P, M], F32, name="near", tag="near", bufs=2)
-            nc.vector.tensor_copy(near[s][:], windows["back", s][:].indirect(near_list[:]))
+                nc.scalar.activation(dst, near["one", s], ACT.Square)
 
-        def square_near(s):
-            if s in (2, 3):
-                square[s] = turns.tile([P, M], F32, name="square%d" % s, offset=W1_BF + 4 * S + 4 * M * (s - 2))
-            else:
-                square[s] = work.tile([P, M], F32, name="square", tag="square", bufs=2)
-            nc.scalar.activation(square[s][:], near[s][:], ACT.Square, scale=inv_root[:, s:s + 1])
+        def square_pair(s):
+            nc.scalar.activation(pair_tile(square, "square", s, 2)[:], near[s // 2][:], ACT.Square)
 
-        def root(s, m0=0, m1=M):
-            nc.scalar.activation(root_cols(s, m0, m1), square[s][:, m0:m1], ACT.Abs_reciprocal_sqrt, bias=1.0)
+        def make_root(s):
+            nc.scalar.activation(pair_tile(root, "root", s, 2)[:, s % 2, :], square[s // 2][:, s % 2, :],
+                                 ACT.Abs_reciprocal_sqrt, bias=1.0 if s < 2 else half_k[:, s:s + 1])
 
-        def make_damp(s, m0=0, m1=M):
-            if s not in damp:
-                damp[s] = work.tile([P, M], F32, name="damp", tag="damp", bufs=4)
-            nc.scalar.activation(damp[s][:, m0:m1], root_cols(s, m0, m1), ACT.Square, scale=inv_root[:, s:s + 1])
+        def damp_one(s):
+            nc.scalar.activation(pair_tile(damp, "damp", s, 2)[:, s % 2, :], root[s // 2][:, s % 2, :],
+                                 ACT.Square, scale=inv_root[:, s:s + 1])
+
+        def damp_pair(s, m0=0, m1=M):
+            nc.scalar.activation(pair_tile(damp, "damp", s, 2)[:, :, m0:m1], root[s // 2][:, :, m0:m1], ACT.Square)
 
         def pick_field(s, m0=0, m1=M):
-            if s not in ratio:
-                ratio[s] = work.tile([P, M], F32, name="ratio", tag="ratio", bufs=3)
-            nc.vector.tensor_tensor(ratio[s][:, m0:m1], windows["hail", s][:].indirect(field_list[:, m0 // 16:m1 // 16]),
-                                    damp[s][:, m0:m1], ALU.mult)
+            if s == 0:
+                ratio[0] = turns.tile([P, 2, M], F32, name="ratio01", offset=TAB1 + RAW_BYTES)
+            nc.vector.tensor_tensor(pair_tile(ratio, "ratio", s, 2)[:, s % 2, m0:m1],
+                                    windows["hail", s][:].indirect(field_list[:, m0 // 16:m1 // 16]),
+                                    damp[s // 2][:, s % 2, m0:m1], ALU.mult)
 
         def pick_base(s, m0=0, m1=M):
-            nc.vector.tensor_tensor(z_slot(s)[:, m0:m1], windows["back", s][:].indirect(base_list[:, m0 // 16:m1 // 16]),
-                                    ratio[s][:, m0:m1], ALU.subtract)
+            nc.vector.tensor_tensor(negz[s // PACK][:, s % PACK, m0:m1],
+                                    windows["back", s][:].indirect(base_list[:, m0 // 16:m1 // 16]),
+                                    ratio[s // 2][:, s % 2, m0:m1], ALU.subtract)
 
         z_bf, z_codes, z_scales = {}, {}, {}
 
         def round_z(b, m0, m1, on_vector):
-            z_bf[b, m0] = turns.tile([P, m1 - m0, PACK], BF16, name="z_bf%d_%d" % (b, m0), align_bytes=64,
-                                     offset=RAW_BYTES + 2 * PACK * (b * M + m0))
+            z_bf[b, m0] = keep.tile([P, m1 - m0, PACK], BF16, name="z_bf%d_%d" % (b, m0), align_bytes=64)
             dst = z_bf[b, m0][:].rearrange("p (c i) t -> p c t i", i=4)
             src = negz[b][:, :, m0:m1].rearrange("p t (c i) -> p c t i", i=4)
             if on_vector:
@@ -271,7 +273,8 @@ def tile_list_hail_indemnity_kernel(tc, tab_words, tab_scales, offs, pos1, pos2,
         def last_pass(b, m0, m1):
             for group in bank_groups(m0, m1):
                 if b == 0:
-                    loss[m0, group[0]] = psum.tile([P, len(group), m1 - m0], F32, name="acc", tag="acc")
+                    tag = "back" if len(loss) < 4 else "hail"
+                    loss[m0, group[0]] = psum.tile([P, len(group), m1 - m0], F32, name="loss", tag=tag, bufs=4)
                     rhs, rhs_s = z_codes[0, 0][:, m0:m1], z_scales[0, 0][:, m0:m1]
                 else:
                     rhs, rhs_s = z_codes[1, m0][:], z_scales[1, m0][:]
@@ -297,56 +300,67 @@ def tile_list_hail_indemnity_kernel(tc, tab_words, tab_scales, offs, pos1, pos2,
                     nc.scalar.activation(res[:, u, :], over[:, u, :], ACT.Identity, bias=late["ded"][:, c:c + 1])
             nc.sync.dma_start(out[c0 * P:(c0 + n) * P, m0:m1].rearrange("(u p) m -> p u m", p=P), res[:])
 
-        for s, h in ((0, 0), (1, 0), (0, 1), (1, 1), (2, 0), (2, 1), (3, 0), (3, 1)):
-            half_rows("back", s, h)
+        for s, h in ((0, 0), (1, 0), (0, 1), (1, 1)):
+            rows("back", s, h)
         cast_w1(0, 0)
         quant_w1(0, 0)
         pick_near(0)
         pick_near(1)
-        cast_w1(1, 0)
+        window("back", 2)
         pick_near(2)
-        pick_near(3)
+        cast_w1(1, 0)
         quant_w1(1, 0)
-        for s in range(2):
-            square_near(s)
-            half_rows("back", PACK + s, 0)
-            root(s)
-            half_rows("back", PACK + s, 1)
-            cast_w1(s, 1)
-            quant_w1(s, 1)
-            pick_near(PACK + s)
         load_last()
-        late["neg"] = keep.tile([P, NT], F32, name="neg_ded")
-        for s in range(SLICES - 2):
-            half_rows("hail", s, 0)
-            square_near(s + 2)
-            half_rows("hail", s, 1)
-            make_damp(s)
+        cast_w1(0, 1)
+        quant_w1(0, 1)
+        cast_w1(1, 1)
+        quant_w1(1, 1)
+        for s in range(3, 6):
+            window("back", s)
+            pick_near(s)
+        square_one(0)
+        rows("back", 6, 0)
+        make_root(0)
+        rows("back", 6, 1)
+        pick_near(6)
+        window("back", 7)
+        pick_near(7)
+        square_one(1)
+        damp_one(0)
+        make_root(1)
+        rows("hail", 0, 0)
+        damp_one(1)
+        rows("hail", 0, 1)
+        window("hail", 1)
+        for s in (0, 1):
             pick_field(s)
-            if s > 0:
-                pick_base(s - 1)
-            if s + 2 == SLICES - 2:
-                root(s + 2, 0, HM)
-                root(s + 2, HM, M)
-            else:
-                root(s + 2)
-            if s < 2:
-                for h in range(2):
-                    half_rows("back", SLICES - 2 + s, h, s == 1)
-                pick_near(SLICES - 2 + s)
-        nc.scalar.activation(late["neg"][:], late["ded"][:], ACT.Copy, scale=-1.0)
-        s6, s7 = SLICES - 2, SLICES - 1
-        for s in (s6, s7):
-            for h in range(2):
-                half_rows("hail", s, h)
+        for s in (0, 1):
+            pick_base(s)
         cuts = (0, HM, HM + HM // 2, M)
         chunks = list(zip(cuts[:-1], cuts[1:]))
+        for s in range(2, SLICES, 2):
+            if s == 2:
+                square_one(s)
+                square_one(s + 1)
+            else:
+                square_pair(s)
+            rows("hail", s, 0)
+            make_root(s)
+            make_root(s + 1)
+            rows("hail", s, 1)
+            window("hail", s + 1)
+            if s + 2 < SLICES:
+                damp_pair(s)
+                for u in (s, s + 1):
+                    pick_field(u)
+                for u in (s, s + 1):
+                    pick_base(u)
+        late["neg"] = keep.tile([P, NT], F32, name="neg_ded")
+        nc.scalar.activation(late["neg"][:], late["ded"][:], ACT.Copy, scale=-1.0)
+        s6, s7 = SLICES - 2, SLICES - 1
         for i, (m0, m1) in enumerate(chunks):
-            make_damp(s6, m0, m1)
+            damp_pair(s6, m0, m1)
             pick_field(s6, m0, m1)
-            if i == 0:
-                pick_base(s6 - 1)
-            make_damp(s7, m0, m1)
             pick_field(s7, m0, m1)
             pick_base(s6, m0, m1)
             pick_base(s7, m0, m1)
@@ -363,7 +377,7 @@ def tile_list_hail_indemnity_kernel(tc, tab_words, tab_scales, offs, pos1, pos2,
         quant_z(1, *chunks[-1])
         last_pass(1, *chunks[-1])
         for group in bank_groups(*chunks[0]):
-            finish(*chunks[0], group, False)
+            finish(*chunks[0], group, group[-1] == NT - 1)
         for c in chunks[1:]:
             for group in bank_groups(*c):
                 finish(*c, group, True)

@@ -45,7 +45,7 @@ def tile_list_hail_indemnity_kernel(tc, tab_words, tab_scales, offs, pos1, pos2,
         tab_rows = turns.tile([P, T // 4], I32, name="tab_rows", offset=TAB_ROWS, align_bytes=64)
         nc.vector.memset(tab_rows[:], 0)
         w2s_raw = keep.tile([P, PASSES * H // 4], I32, name="w2s_raw", align_bytes=64)
-        nc.gpsimd.memset(w2s_raw[:], 0)
+        nc.vector.memset(w2s_raw[:], 0)
         planes = keep.tile([P, PASSES * S // 4], I32, name="planes", align_bytes=64)
         nc.vector.memset(planes[:], 0)
 
@@ -58,26 +58,25 @@ def tile_list_hail_indemnity_kernel(tc, tab_words, tab_scales, offs, pos1, pos2,
         load_list("offs", offs)
         half_t = turns.tile([P, GROUPS, PACK], F32, name="half_t", offset=TAB1)
         nc.sync.dma_start(half_t[:], half.rearrange("(b p t) -> p b t", b=GROUPS, t=PACK))
+        load_list("pos2", pos2)
+        load_list("pos1", pos1)
+        w2_raw = keep.tile([P, PASSES, H // 2], I32, name="w2_raw", align_bytes=64)
+        nc.sync.dma_start(w2_raw[:], w2_words.bitcast(I32).rearrange("a p c -> p a c"))
+        load_list("pos3", pos3)
+        offs_t, near_list, field_list, base_list = lists["offs"], lists["pos2"], lists["pos1"], lists["pos3"]
+        tab_w = [turns.tile([P, T], I32, name="tab_w0", offset=0, align_bytes=64)]
+        nc.sync.dma_start(tab_w[0][:], tab_words[0].rearrange("p t i -> p (t i)").bitcast(I32))
+        nc.scalar.dma_start(tab_rows[0:P:4, :], tab_scales.rearrange("a q t -> (a q) t").bitcast(I32))
+        for q in range(4):
+            nc.scalar.dma_start(
+                w2s_raw[32 * q:32 * q + 4, :].rearrange("r (a c) -> r a c", a=PASSES),
+                w2_scales.bitcast(I32)[:, 4 * q:4 * q + 4, :].rearrange("a r c -> r a c"))
         inv_root = keep.tile([P, SLICES], F32, name="inv_root")
         nc.scalar.activation(inv_root[:], half_t[:].rearrange("p b t -> p (b t)"), ACT.Abs_reciprocal_sqrt)
         half_k = keep.tile([P, SLICES], F32, name="half_k")
         nc.scalar.activation(half_k[:], half_t[:].rearrange("p b t -> p (b t)"), ACT.Identity)
-        w2_raw = keep.tile([P, PASSES, H // 2], I32, name="w2_raw", align_bytes=64)
-        nc.sync.dma_start(w2_raw[:], w2_words.bitcast(I32).rearrange("a p c -> p a c"))
-        load_list("pos2", pos2)
-        load_list("pos1", pos1)
-        load_list("pos3", pos3)
-        offs_t, near_list, field_list, base_list = lists["offs"], lists["pos2"], lists["pos1"], lists["pos3"]
-        tab_w = []
-        for a in range(PASSES):
-            tab_w.append(turns.tile([P, T], I32, name="tab_w%d" % a, offset=a * TAB1, align_bytes=64))
-            nc.sync.dma_start(tab_w[a][:], tab_words[a].rearrange("p t i -> p (t i)").bitcast(I32))
-            if a == 0:
-                for q in range(4):
-                    nc.scalar.dma_start(
-                        w2s_raw[32 * q:32 * q + 4, :].rearrange("r (a c) -> r a c", a=PASSES),
-                        w2_scales.bitcast(I32)[:, 4 * q:4 * q + 4, :].rearrange("a r c -> r a c"))
-                nc.scalar.dma_start(tab_rows[0:P:4, :], tab_scales.rearrange("a q t -> (a q) t").bitcast(I32))
+        tab_w.append(turns.tile([P, T], I32, name="tab_w1", offset=TAB1, align_bytes=64))
+        nc.sync.dma_start(tab_w[1][:], tab_words[1].rearrange("p t i -> p (t i)").bitcast(I32))
 
         w2c = keep.tile([P, PASSES * H * 2], U8, name="w2c", align_bytes=64)
         nc.vector.tensor_copy(

@@ -30,7 +30,7 @@ RAW_BYTES = 4 * PACK * KP
 TAB1 = TAB_BYTES
 TAB_ROWS = 2 * TAB_BYTES
 RAW0 = 0
-W1_BF = TAB_ROWS + T
+FIRST_RAW = TAB_ROWS + T
 
 
 def tile_list_hail_indemnity_kernel(tc, tab_words, tab_scales, offs, pos1, pos2, pos3, w1,
@@ -40,11 +40,11 @@ def tile_list_hail_indemnity_kernel(tc, tab_words, tab_scales, offs, pos1, pos2,
         keep = ctx.enter_context(tc.tile_pool(name="keep", bufs=1))
         turns = ctx.enter_context(tc.tile_pool(name="turns", bufs=1))
         work = ctx.enter_context(tc.tile_pool(name="work", bufs=2))
-        psum = ctx.enter_context(tc.psum_pool(name="psum", bufs=4))
+        psum = ctx.enter_context(tc.psum_pool(name="psum", bufs=8))
 
         tab_rows = turns.tile([P, T // 4], I32, name="tab_rows", offset=TAB_ROWS, align_bytes=64)
         nc.vector.memset(tab_rows[:], 0)
-        w2s_raw = keep.tile([P, PASSES * H // 4], I32, name="w2s_raw", align_bytes=64)
+        w2s_raw = turns.tile([P, PASSES * H // 4], I32, name="w2s_raw", offset=FIRST_RAW + RAW_BYTES - H, align_bytes=64)
         nc.vector.memset(w2s_raw[:], 0)
         planes = keep.tile([P, PASSES * S // 4], I32, name="planes", align_bytes=64)
         nc.vector.memset(planes[:], 0)
@@ -97,7 +97,7 @@ def tile_list_hail_indemnity_kernel(tc, tab_words, tab_scales, offs, pos1, pos2,
                 queue = nc.gpsimd if 4 * a + q >= 6 else nc.scalar
                 queue.dma_start(v_planes[a][32 * q:32 * q + 4, :], v_rows[first:first + 16:4, :])
         v_words = {}
-        whole = turns.tile([P, S], I32, name="v_words0", offset=TAB_ROWS, align_bytes=64)
+        whole = turns.tile([P, S], I32, name="v_words0", offset=FIRST_RAW + RAW_BYTES, align_bytes=64)
         nc.vector.tensor_copy(whole[:].bitcast(U32), tab_w[0][:].bitcast(U32).indirect(offs_t[:]))
         for h in range(2):
             v_words[0, h] = whole[:, h * BANK:(h + 1) * BANK]
@@ -107,7 +107,7 @@ def tile_list_hail_indemnity_kernel(tc, tab_words, tab_scales, offs, pos1, pos2,
         def load_w1(b):
             for a in range(PASSES):
                 w1_raw[a, b] = turns.tile([P, PACK, KP], F32, name="w1_raw%d%d" % (a, b),
-                                          offset=(TAB1 if b else RAW0) + a * RAW_BYTES)
+                                          offset=(TAB1 if b else RAW0) + a * RAW_BYTES if a or b else FIRST_RAW)
                 nc.sync.dma_start(
                     w1_raw[a, b][:],
                     w1[a * KP:(a + 1) * KP, b * KP:(b + 1) * KP].rearrange("(p j) c -> p j c", j=PACK))
@@ -123,16 +123,14 @@ def tile_list_hail_indemnity_kernel(tc, tab_words, tab_scales, offs, pos1, pos2,
         w1_bf, w1_codes, w1_scales = {}, {}, {}
 
         def cast_w1(a, b):
-            w1_bf[a, b] = turns.tile([P, PACK, P, PACK], BF16, name="w1_bf%d%d" % (a, b), align_bytes=64,
-                                     offset=W1_BF + 4 * S * min(2 * b + a, 1))
+            w1_bf[a, b] = work.tile([P, PACK, P, PACK], BF16, name="w1_bf", tag="w1_bf", bufs=1, align_bytes=64)
             if (a, b) == (0, 0):
                 nc.vector.tensor_copy(w1_bf[a, b][:].rearrange("p t m j -> p m j t"),
                                       w1_raw[a, b][:].rearrange("p j (m t) -> p m j t", t=PACK))
                 return
             dst = w1_bf[a, b][:].rearrange("p t m j -> p m t j")
             src = w1_raw[a, b][:].rearrange("p j (m t) -> p m t j", t=PACK)
-            for m0 in range(0, P, P // 4):
-                nc.gpsimd.tensor_scalar(dst[:, m0:m0 + P // 4], src[:, m0:m0 + P // 4], 1.0, 0.0, ALU.mult, ALU.add)
+            nc.gpsimd.tensor_scalar(dst, src, 1.0, 0.0, ALU.mult, ALU.add)
 
         def quant_w1(a, b):
             w1_codes[a, b] = keep.tile([P, KP], U32, name="w1_codes%d%d" % (a, b), align_bytes=64)
@@ -144,8 +142,8 @@ def tile_list_hail_indemnity_kernel(tc, tab_words, tab_scales, offs, pos1, pos2,
 
         def rows(kind, s, h):
             b, t = divmod(s, PACK)
-            bank = psum.tile([P, BANK], F32, name=kind + "_acc", tag=kind, bufs=4)
-            order = range(PASSES) if kind == "back" and s < 2 else reversed(range(PASSES))
+            bank = psum.tile([P, BANK], F32, name="acc", tag="acc")
+            order = range(PASSES) if kind == "back" and s < 3 else reversed(range(PASSES))
             for i, a in enumerate(order):
                 if kind == "back":
                     c0 = a * H + s * P
@@ -188,7 +186,7 @@ def tile_list_hail_indemnity_kernel(tc, tab_words, tab_scales, offs, pos1, pos2,
             if s == 3:
                 dst = turns.tile([P, M], F32, name="near3", offset=RAW_BYTES)[:]
             elif s < 3:
-                dst = work.tile([P, M], F32, name="near_one", tag="near_one", bufs=3)[:]
+                dst = turns.tile([P, M], F32, name="near%d" % s, offset=FIRST_RAW + 4 * M * s)[:]
             else:
                 if s // 2 not in near:
                     if s == SLICES - 2:
@@ -253,12 +251,12 @@ def tile_list_hail_indemnity_kernel(tc, tab_words, tab_scales, offs, pos1, pos2,
         late = {}
 
         def load_last():
-            late["ded"] = turns.tile([P, NT], F32, name="ded_t", offset=RAW0 + 7680)
+            late["ded"] = turns.tile([P, NT], F32, name="ded_t", offset=FIRST_RAW + 7680)
             with nc.allow_non_contiguous_dma(reason="one deductible a partition"):
                 nc.sync.dma_start(late["ded"][:], ded.rearrange("(c p) -> p c", p=P))
-            late["w3s"] = turns.tile([P, PASSES * N // 4], I32, name="w3s", offset=RAW0 + 6144, align_bytes=64)
+            late["w3s"] = turns.tile([P, PASSES * N // 4], I32, name="w3s", offset=FIRST_RAW + 6144, align_bytes=64)
             nc.gpsimd.memset(late["w3s"][:], 0)
-            late["w3w"] = turns.tile([P, PASSES, N], I32, name="w3_w", offset=RAW0, align_bytes=64)
+            late["w3w"] = turns.tile([P, PASSES, N], I32, name="w3_w", offset=FIRST_RAW, align_bytes=64)
             nc.sync.dma_start(late["w3w"][:], w3_words.rearrange("a p c i -> p a (c i)").bitcast(I32))
             for q in range(4):
                 nc.sync.dma_start(
@@ -272,8 +270,7 @@ def tile_list_hail_indemnity_kernel(tc, tab_words, tab_scales, offs, pos1, pos2,
         def last_pass(b, m0, m1):
             for group in bank_groups(m0, m1):
                 if b == 0:
-                    tag = "back" if len(loss) < 4 else "hail"
-                    loss[m0, group[0]] = psum.tile([P, len(group), m1 - m0], F32, name="loss", tag=tag, bufs=4)
+                    loss[m0, group[0]] = psum.tile([P, len(group), m1 - m0], F32, name="acc", tag="acc")
                     rhs, rhs_s = z_codes[0, 0][:, m0:m1], z_scales[0, 0][:, m0:m1]
                 else:
                     rhs, rhs_s = z_codes[1, m0][:], z_scales[1, m0][:]
@@ -309,7 +306,6 @@ def tile_list_hail_indemnity_kernel(tc, tab_words, tab_scales, offs, pos1, pos2,
         pick_near(2)
         cast_w1(1, 0)
         quant_w1(1, 0)
-        load_last()
         cast_w1(0, 1)
         quant_w1(0, 1)
         cast_w1(1, 1)
@@ -335,7 +331,7 @@ def tile_list_hail_indemnity_kernel(tc, tab_words, tab_scales, offs, pos1, pos2,
             pick_field(s)
         for s in (0, 1):
             pick_base(s)
-        cuts = (0, HM, HM + HM // 2, M)
+        cuts = (0, HM, M)
         chunks = list(zip(cuts[:-1], cuts[1:]))
         for s in range(2, SLICES, 2):
             if s == 2:
@@ -354,6 +350,7 @@ def tile_list_hail_indemnity_kernel(tc, tab_words, tab_scales, offs, pos1, pos2,
                     pick_field(u)
                 for u in (s, s + 1):
                     pick_base(u)
+        load_last()
         late["neg"] = keep.tile([P, NT], F32, name="neg_ded")
         nc.scalar.activation(late["neg"][:], late["ded"][:], ACT.Copy, scale=-1.0)
         s6, s7 = SLICES - 2, SLICES - 1
@@ -377,6 +374,5 @@ def tile_list_hail_indemnity_kernel(tc, tab_words, tab_scales, offs, pos1, pos2,
         last_pass(1, *chunks[-1])
         for group in bank_groups(*chunks[0]):
             finish(*chunks[0], group, group[-1] == NT - 1)
-        for c in chunks[1:]:
-            for group in bank_groups(*c):
-                finish(*c, group, True)
+        for group in bank_groups(*chunks[1]):
+            finish(*chunks[1], group, True)

@@ -73,8 +73,8 @@ def tile_list_hail_indemnity_kernel(tc, tab_words, tab_scales, offs, pos1, pos2,
                 w2_scales.bitcast(I32)[:, 4 * q:4 * q + 4, :].rearrange("a r c -> r a c"))
         inv_root = keep.tile([P, SLICES], F32, name="inv_root")
         nc.scalar.activation(inv_root[:], half_t[:].rearrange("p b t -> p (b t)"), ACT.Abs_reciprocal_sqrt)
-        half_k = keep.tile([P, SLICES], F32, name="half_k")
-        nc.scalar.activation(half_k[:], half_t[:].rearrange("p b t -> p (b t)"), ACT.Identity)
+        inv_half = keep.tile([P, SLICES], F32, name="inv_half")
+        nc.scalar.activation(inv_half[:], inv_root[:], ACT.Square)
         tab_w.append(turns.tile([P, T], I32, name="tab_w1", offset=TAB1, align_bytes=64))
         nc.sync.dma_start(tab_w[1][:], tab_words[1].rearrange("p t i -> p (t i)").bitcast(I32))
 
@@ -140,9 +140,12 @@ def tile_list_hail_indemnity_kernel(tc, tab_words, tab_scales, offs, pos1, pos2,
 
         windows = {}
 
-        def rows(kind, s, h):
+        sums = {}
+
+        def multiply(kind, s, h):
             b, t = divmod(s, PACK)
             bank = psum.tile([P, BANK], F32, name="acc", tag="acc")
+            sums[kind, s, h] = bank
             order = range(PASSES) if kind == "back" and s < 3 else reversed(range(PASSES))
             for i, a in enumerate(order):
                 if kind == "back":
@@ -156,6 +159,9 @@ def tile_list_hail_indemnity_kernel(tc, tab_words, tab_scales, offs, pos1, pos2,
                                     rhs=v_words[a, h].bitcast(FP8X4),
                                     rhs_scale=v_planes[a].bitcast(U8)[:, h * BANK:(h + 1) * BANK],
                                     start=(i == 0), stop=(i == PASSES - 1))
+
+        def empty(kind, s, h):
+            bank = sums[kind, s, h]
             if (kind, s) not in windows:
                 if kind == "back" and s == SLICES - 1:
                     windows[kind, s] = turns.tile([P, S], F32, name="back%d" % s, align_bytes=64, offset=TAB1 + 4 * S)
@@ -168,14 +174,18 @@ def tile_list_hail_indemnity_kernel(tc, tab_words, tab_scales, offs, pos1, pos2,
             elif kind == "back":
                 nc.scalar.copy(dst, bank[:])
             else:
-                nc.scalar.activation(dst, bank[:], ACT.Abs)
+                nc.scalar.activation(dst, bank[:], ACT.Abs, scale=inv_half[:, s:s + 1])
+
+        def rows(kind, s, h):
+            multiply(kind, s, h)
+            empty(kind, s, h)
 
         def window(kind, s):
             for h in range(2):
                 rows(kind, s, h)
 
         negz = [keep.tile([P, PACK, M], F32, name="negz%d" % b, align_bytes=64) for b in range(GROUPS)]
-        near, square, root, damp, ratio = {}, {}, {}, {}, {}
+        near, damp, ratio = {}, {}, {}
 
         def pair_tile(store, name, s, bufs):
             if s // 2 not in store:
@@ -197,26 +207,21 @@ def tile_list_hail_indemnity_kernel(tc, tab_words, tab_scales, offs, pos1, pos2,
             near["one", s] = dst
             nc.vector.tensor_copy(dst, windows["back", s][:].indirect(near_list[:]))
 
-        def square_one(s):
-            dst = pair_tile(square, "square", s, 2)[:, s % 2, :]
-            if s < 2:
-                nc.scalar.activation(dst, near["one", s], ACT.Square, scale=inv_root[:, s:s + 1])
-            else:
-                nc.scalar.activation(dst, near["one", s], ACT.Square)
+        def square_near(s):
+            nc.scalar.activation(pair_tile(damp, "damp", s, 2)[:, s % 2, :], near["one", s], ACT.Square,
+                                 scale=inv_root[:, s:s + 1])
 
-        def square_pair(s):
-            nc.scalar.activation(pair_tile(square, "square", s, 2)[:], near[s // 2][:], ACT.Square)
+        def root_pair(s):
+            nc.scalar.activation(damp[s // 2][:], damp[s // 2][:], ACT.Abs_reciprocal_sqrt, bias=1.0)
 
-        def make_root(s):
-            nc.scalar.activation(pair_tile(root, "root", s, 2)[:, s % 2, :], square[s // 2][:, s % 2, :],
-                                 ACT.Abs_reciprocal_sqrt, bias=1.0 if s < 2 else half_k[:, s:s + 1])
+        def root_one(s):
+            nc.scalar.activation(damp[0][:, s, :], damp[0][:, s, :], ACT.Abs_reciprocal_sqrt, bias=1.0)
 
         def damp_one(s):
-            nc.scalar.activation(pair_tile(damp, "damp", s, 2)[:, s % 2, :], root[s // 2][:, s % 2, :],
-                                 ACT.Square, scale=inv_root[:, s:s + 1])
+            nc.scalar.activation(damp[0][:, s, :], damp[0][:, s, :], ACT.Square)
 
         def damp_pair(s, m0=0, m1=M):
-            nc.scalar.activation(pair_tile(damp, "damp", s, 2)[:, :, m0:m1], root[s // 2][:, :, m0:m1], ACT.Square)
+            nc.scalar.activation(damp[s // 2][:, :, m0:m1], damp[s // 2][:, :, m0:m1], ACT.Square)
 
         def pick_field(s, m0=0, m1=M):
             if s == 0:
@@ -313,16 +318,16 @@ def tile_list_hail_indemnity_kernel(tc, tab_words, tab_scales, offs, pos1, pos2,
         for s in range(3, 6):
             window("back", s)
             pick_near(s)
-        square_one(0)
+        square_near(0)
         rows("back", 6, 0)
-        make_root(0)
+        root_one(0)
         rows("back", 6, 1)
         pick_near(6)
         window("back", 7)
         pick_near(7)
-        square_one(1)
+        square_near(1)
         damp_one(0)
-        make_root(1)
+        root_one(1)
         rows("hail", 0, 0)
         damp_one(1)
         rows("hail", 0, 1)
@@ -334,16 +339,16 @@ def tile_list_hail_indemnity_kernel(tc, tab_words, tab_scales, offs, pos1, pos2,
         cuts = (0, HM, M)
         chunks = list(zip(cuts[:-1], cuts[1:]))
         for s in range(2, SLICES, 2):
-            if s == 2:
-                square_one(s)
-                square_one(s + 1)
-            else:
-                square_pair(s)
-            rows("hail", s, 0)
-            make_root(s)
-            make_root(s + 1)
-            rows("hail", s, 1)
-            window("hail", s + 1)
+            banks = [(u, h) for u in (s, s + 1) for h in range(2)]
+            for u, h in banks:
+                multiply("hail", u, h)
+            square_near(s)
+            square_near(s + 1)
+            for u, h in reversed(banks[2:]):
+                empty("hail", u, h)
+            root_pair(s)
+            for u, h in reversed(banks[:2]):
+                empty("hail", u, h)
             if s + 2 < SLICES:
                 damp_pair(s)
                 for u in (s, s + 1):

@@ -42,11 +42,15 @@ def tile_list_hail_indemnity_kernel(tc, tab_words, tab_scales, offs, pos1, pos2,
         work = ctx.enter_context(tc.tile_pool(name="work", bufs=2))
         psum = ctx.enter_context(tc.psum_pool(name="psum", bufs=8))
 
-        tab_rows = turns.tile([P, T // 4], I32, name="tab_rows", offset=TAB_ROWS, align_bytes=64)
-        nc.vector.memset(tab_rows[:], 0)
-        w2s_raw = turns.tile([P, PASSES * H // 4], I32, name="w2s_raw", offset=FIRST_RAW + RAW_BYTES - H, align_bytes=64)
-        nc.vector.memset(w2s_raw[:], 0)
-        planes = keep.tile([P, PASSES * S // 4], I32, name="planes", align_bytes=64)
+        tab_rows = turns.tile([P, T // 4], I32, name="tab_rows", offset=TAB1 + T, align_bytes=64)
+        nc.vector.memset(tab_rows[32:64, :], 0)
+        nc.vector.memset(tab_rows[64:P, :], 0)
+        half_t = keep.tile([P, GROUPS, PACK], F32, name="half_t")
+        nc.gpsimd.dma_start(half_t[:], half.rearrange("(b p t) -> p b t", b=GROUPS, t=PACK))
+        w2s_rows = turns.tile([P, H // 4], I32, name="w2s_rows", offset=TAB_ROWS - H // 2, align_bytes=64)
+        nc.gpsimd.memset(w2s_rows[32:64, :], 0)
+        nc.gpsimd.memset(w2s_rows[64:P, :], 0)
+        planes = keep.tile([P, PASSES, (S + H) // 4], I32, name="planes", align_bytes=64)
         nc.vector.memset(planes[:], 0)
 
         lists = {}
@@ -56,46 +60,40 @@ def tile_list_hail_indemnity_kernel(tc, tab_words, tab_scales, offs, pos1, pos2,
             nc.sync.dma_start(lists[name][:], src)
 
         load_list("offs", offs)
-        half_t = turns.tile([P, GROUPS, PACK], F32, name="half_t", offset=TAB1)
-        nc.sync.dma_start(half_t[:], half.rearrange("(b p t) -> p b t", b=GROUPS, t=PACK))
+        nc.sync.dma_start(tab_rows[0:32, :], tab_scales.bitcast(I32).rearrange("a q t -> q a t"))
+        nc.sync.dma_start(w2s_rows[0:32, :], w2_scales.bitcast(I32).rearrange("a q c -> q a c"))
+        w2_raw = turns.tile([P, PASSES, H // 2], I32, name="w2_raw", offset=FIRST_RAW, align_bytes=64)
+        nc.sync.dma_start(w2_raw[:], w2_words.bitcast(I32).rearrange("a p c -> p a c"))
         load_list("pos2", pos2)
         load_list("pos1", pos1)
-        w2_raw = keep.tile([P, PASSES, H // 2], I32, name="w2_raw", align_bytes=64)
-        nc.sync.dma_start(w2_raw[:], w2_words.bitcast(I32).rearrange("a p c -> p a c"))
         load_list("pos3", pos3)
         offs_t, near_list, field_list, base_list = lists["offs"], lists["pos2"], lists["pos1"], lists["pos3"]
         tab_w = [turns.tile([P, T], I32, name="tab_w0", offset=0, align_bytes=64)]
         nc.sync.dma_start(tab_w[0][:], tab_words[0].rearrange("p t i -> p (t i)").bitcast(I32))
-        nc.scalar.dma_start(tab_rows[0:P:4, :], tab_scales.rearrange("a q t -> (a q) t").bitcast(I32))
-        for q in range(4):
-            nc.scalar.dma_start(
-                w2s_raw[32 * q:32 * q + 4, :].rearrange("r (a c) -> r a c", a=PASSES),
-                w2_scales.bitcast(I32)[:, 4 * q:4 * q + 4, :].rearrange("a r c -> r a c"))
         inv_root = keep.tile([P, SLICES], F32, name="inv_root")
         nc.scalar.activation(inv_root[:], half_t[:].rearrange("p b t -> p (b t)"), ACT.Abs_reciprocal_sqrt)
         inv_half = keep.tile([P, SLICES], F32, name="inv_half")
         nc.scalar.activation(inv_half[:], inv_root[:], ACT.Square)
+
+        staged = keep.tile([P, (S + H) // 4], I32, name="staged", align_bytes=64)
+        nc.gpsimd.tensor_copy(
+            staged[:, S // 4:].bitcast(U8).rearrange("p (g t m n) -> p g m t n", t=PACK, m=P // 16, n=16),
+            w2s_rows[:].bitcast(U8).rearrange("p (g m n t) -> p g m t n", t=PACK, m=P // 16, n=16))
+        v_rows = turns.tile([P, S // 4], I32, name="v_rows", offset=TAB1, align_bytes=64)
+        nc.vector.tensor_copy(v_rows[:].bitcast(U8), tab_rows[:].bitcast(U8).indirect(offs_t[:]))
+        nc.vector.tensor_copy(staged[:, :S // 4], v_rows[:])
+        for q in range(4):
+            nc.sync.dma_start(planes[32 * q:32 * q + 4], staged[8 * q:8 * q + 8, :])
         tab_w.append(turns.tile([P, T], I32, name="tab_w1", offset=TAB1, align_bytes=64))
         nc.sync.dma_start(tab_w[1][:], tab_words[1].rearrange("p t i -> p (t i)").bitcast(I32))
+        v_planes = [planes[:, a, :S // 4] for a in range(PASSES)]
+        w2s = [planes[:, a, S // 4:].bitcast(U8) for a in range(PASSES)]
 
-        w2c = keep.tile([P, PASSES * H * 2], U8, name="w2c", align_bytes=64)
+        w2c = turns.tile([P, PASSES * H * 2], U8, name="w2c", offset=TAB_ROWS, align_bytes=64)
         nc.vector.tensor_copy(
             w2c[:].bitcast(U16).rearrange("p (g t m n) -> p g m t n", t=PACK, m=P // 8, n=8),
             w2_raw[:].rearrange("p a c -> p (a c)").bitcast(U16).rearrange("p (g m n t) -> p g m t n", t=PACK, m=P // 8, n=8))
 
-        w2s = keep.tile([P, PASSES * H], U8, name="w2s", align_bytes=64)
-        nc.vector.tensor_copy(
-            w2s[:].rearrange("p (g t m n) -> p g m t n", t=PACK, m=P // 16, n=16),
-            w2s_raw[:].bitcast(U8).rearrange("p (g m n t) -> p g m t n", t=PACK, m=P // 16, n=16))
-
-        v_rows = keep.tile([P, S // 4], I32, name="v_rows", align_bytes=64)
-        nc.vector.tensor_copy(v_rows[:].bitcast(U8), tab_rows[:].bitcast(U8).indirect(offs_t[:]))
-        v_planes = [planes[:, a * (S // 4):(a + 1) * (S // 4)] for a in range(PASSES)]
-        for a in range(PASSES):
-            for q in range(4):
-                first = 64 * a + 16 * q
-                queue = nc.gpsimd if 4 * a + q >= 6 else nc.scalar
-                queue.dma_start(v_planes[a][32 * q:32 * q + 4, :], v_rows[first:first + 16:4, :])
         v_words = {}
         whole = turns.tile([P, S], I32, name="v_words0", offset=FIRST_RAW + RAW_BYTES, align_bytes=64)
         nc.vector.tensor_copy(whole[:].bitcast(U32), tab_w[0][:].bitcast(U32).indirect(offs_t[:]))
@@ -107,7 +105,7 @@ def tile_list_hail_indemnity_kernel(tc, tab_words, tab_scales, offs, pos1, pos2,
         def load_w1(b):
             for a in range(PASSES):
                 w1_raw[a, b] = turns.tile([P, PACK, KP], F32, name="w1_raw%d%d" % (a, b),
-                                          offset=(TAB1 if b else RAW0) + a * RAW_BYTES if a or b else FIRST_RAW)
+                                          offset=((FIRST_RAW, RAW0), (RAW_BYTES, TAB1 + RAW_BYTES))[a][b])
                 nc.sync.dma_start(
                     w1_raw[a, b][:],
                     w1[a * KP:(a + 1) * KP, b * KP:(b + 1) * KP].rearrange("(p j) c -> p j c", j=PACK))
@@ -151,7 +149,7 @@ def tile_list_hail_indemnity_kernel(tc, tab_words, tab_scales, offs, pos1, pos2,
                 if kind == "back":
                     c0 = a * H + s * P
                     lhs = w2c[:, 2 * c0:2 * (c0 + P)].bitcast(FP4X4)
-                    lhs_s = w2s[:, c0:c0 + P]
+                    lhs_s = w2s[a][:, s * P:(s + 1) * P]
                 else:
                     lhs = w1_codes[a, b][:, t * P:(t + 1) * P].bitcast(FP8X4)
                     lhs_s = w1_scales[a, b][:, t * P:(t + 1) * P]
@@ -164,7 +162,7 @@ def tile_list_hail_indemnity_kernel(tc, tab_words, tab_scales, offs, pos1, pos2,
             bank = sums[kind, s, h]
             if (kind, s) not in windows:
                 if kind == "back" and s == SLICES - 1:
-                    windows[kind, s] = turns.tile([P, S], F32, name="back%d" % s, align_bytes=64, offset=TAB1 + 4 * S)
+                    windows[kind, s] = turns.tile([P, S], F32, name="back%d" % s, align_bytes=64, offset=RAW0 + 4 * S)
                 else:
                     windows[kind, s] = work.tile([P, S], F32, name=kind, tag=kind,
                                                  bufs=SLICES - 1 if kind == "back" else 4, align_bytes=64)
@@ -200,7 +198,7 @@ def tile_list_hail_indemnity_kernel(tc, tab_words, tab_scales, offs, pos1, pos2,
             else:
                 if s // 2 not in near:
                     if s == SLICES - 2:
-                        near[s // 2] = turns.tile([P, 2, M], F32, name="near67", offset=TAB1)
+                        near[s // 2] = turns.tile([P, 2, M], F32, name="near67", offset=RAW0)
                     else:
                         near[s // 2] = turns.tile([P, 2, M], F32, name="near45", offset=RAW_BYTES + 4 * M)
                 dst = near[s // 2][:, s % 2, :]

@@ -361,14 +361,19 @@ def tile_list_hail_indemnity_kernel(tc, tab_words, tab_scales, offs, pos1, pos2,
             damp_pair(s6, m0, m1)
             pick_field(s6, m0, m1)
             pick_field(s7, m0, m1)
-            pick_base(s6, m0, m1)
-            pick_base(s7, m0, m1)
             if i == 0:
+                pick_base(s6, m0, m1)
+                pick_base(s7, m0, m1)
                 round_z(0, 0, M, False)
                 quant_z(0, 0, M)
                 for c in chunks:
                     last_pass(0, *c)
             else:
+                base = turns.tile([P, 2, HM], F32, name="base_last", offset=RAW0)
+                for u in (s6, s7):
+                    nc.scalar.activation(base[:, u % 2, :], windows["back", u][:].indirect(base_list[:, HM // 16:]),
+                                         ACT.Copy)
+                nc.vector.tensor_tensor(negz[1][:, 2:, HM:], base[:], ratio[s6 // 2][:, :, HM:], ALU.subtract)
                 round_z(1, *chunks[i - 1], False)
                 quant_z(1, *chunks[i - 1])
                 last_pass(1, *chunks[i - 1])

@@ -121,8 +121,10 @@ def tile_list_hail_indemnity_kernel(tc, tab_words, tab_scales, offs, pos1, pos2,
         w1_bf, w1_codes, w1_scales = {}, {}, {}
 
         def cast_w1(a, b):
-            w1_bf[a, b] = work.tile([P, PACK, P, PACK], BF16, name="w1_bf", tag="w1_bf", bufs=1, align_bytes=64)
-            if (a, b) == (0, 0):
+            first = (a, b) == (0, 0)
+            w1_bf[a, b] = work.tile([P, PACK, P, PACK], BF16, name="w1_bf", tag="w1_first" if first else "w1_bf",
+                                    bufs=1, align_bytes=64)
+            if (a, b) == (1, 0):
                 nc.vector.tensor_copy(w1_bf[a, b][:].rearrange("p t m j -> p m j t"),
                                       w1_raw[a, b][:].rearrange("p j (m t) -> p m j t", t=PACK))
                 return
@@ -136,38 +138,35 @@ def tile_list_hail_indemnity_kernel(tc, tab_words, tab_scales, offs, pos1, pos2,
             nc.vector.quantize_mx(out=w1_codes[a, b][:].bitcast(FP8X4), scales=w1_scales[a, b][:],
                                   in_=w1_bf[a, b][:].rearrange("p t m j -> p (t m j)"))
 
-        windows = {}
+        windows, sums = {}, {}
 
-        sums = {}
+        def one_pass(kind, s, h, a, first):
+            b, t = divmod(s, PACK)
+            if first:
+                sums[kind, s, h] = psum.tile([P, BANK], F32, name="acc", tag="acc")
+            if kind == "back":
+                c0 = a * H + s * P
+                lhs = w2c[:, 2 * c0:2 * (c0 + P)].bitcast(FP4X4)
+                lhs_s = w2s[a][:, s * P:(s + 1) * P]
+            else:
+                lhs = w1_codes[a, b][:, t * P:(t + 1) * P].bitcast(FP8X4)
+                lhs_s = w1_scales[a, b][:, t * P:(t + 1) * P]
+            nc.tensor.matmul_mx(out=sums[kind, s, h][:], lhsT=lhs, lhsT_scale=lhs_s,
+                                rhs=v_words[a, h].bitcast(FP8X4),
+                                rhs_scale=v_planes[a].bitcast(U8)[:, h * BANK:(h + 1) * BANK],
+                                start=first, stop=not first)
 
         def multiply(kind, s, h):
-            b, t = divmod(s, PACK)
-            bank = psum.tile([P, BANK], F32, name="acc", tag="acc")
-            sums[kind, s, h] = bank
-            order = range(PASSES) if kind == "back" and s < 3 else reversed(range(PASSES))
-            for i, a in enumerate(order):
-                if kind == "back":
-                    c0 = a * H + s * P
-                    lhs = w2c[:, 2 * c0:2 * (c0 + P)].bitcast(FP4X4)
-                    lhs_s = w2s[a][:, s * P:(s + 1) * P]
-                else:
-                    lhs = w1_codes[a, b][:, t * P:(t + 1) * P].bitcast(FP8X4)
-                    lhs_s = w1_scales[a, b][:, t * P:(t + 1) * P]
-                nc.tensor.matmul_mx(out=bank[:], lhsT=lhs, lhsT_scale=lhs_s,
-                                    rhs=v_words[a, h].bitcast(FP8X4),
-                                    rhs_scale=v_planes[a].bitcast(U8)[:, h * BANK:(h + 1) * BANK],
-                                    start=(i == 0), stop=(i == PASSES - 1))
+            for a in range(PASSES):
+                one_pass(kind, s, h, a, a == 0)
 
         def empty(kind, s, h):
             bank = sums[kind, s, h]
             if (kind, s) not in windows:
-                if kind == "back" and s == SLICES - 1:
-                    windows[kind, s] = turns.tile([P, S], F32, name="back%d" % s, align_bytes=64, offset=RAW0 + 4 * S)
-                else:
-                    windows[kind, s] = work.tile([P, S], F32, name=kind, tag=kind,
-                                                 bufs=SLICES - 1 if kind == "back" else 4, align_bytes=64)
+                windows[kind, s] = work.tile([P, S], F32, name=kind, tag=kind,
+                                             bufs=SLICES if kind == "back" else 4, align_bytes=64)
             dst = windows[kind, s][:, h * BANK:(h + 1) * BANK]
-            if kind == "back" and s == SLICES - 1:
+            if kind == "back" and s in (2, 3) and h == 0:
                 nc.vector.tensor_copy(dst, bank[:])
             elif kind == "back":
                 nc.scalar.copy(dst, bank[:])
@@ -191,32 +190,20 @@ def tile_list_hail_indemnity_kernel(tc, tab_words, tab_scales, offs, pos1, pos2,
             return store[s // 2]
 
         def pick_near(s):
-            if s == 3:
-                dst = turns.tile([P, M], F32, name="near3", offset=RAW_BYTES)[:]
-            elif s < 3:
-                dst = turns.tile([P, M], F32, name="near%d" % s, offset=FIRST_RAW + 4 * M * s)[:]
+            if s < 2:
+                near[s] = keep.tile([P, M], F32, name="near%d" % s)
+            elif s < 5:
+                near[s] = turns.tile([P, M], F32, name="near%d" % s, offset=RAW_BYTES + 4 * M * (s - 2))
             else:
-                if s // 2 not in near:
-                    if s == SLICES - 2:
-                        near[s // 2] = turns.tile([P, 2, M], F32, name="near67", offset=RAW0)
-                    else:
-                        near[s // 2] = turns.tile([P, 2, M], F32, name="near45", offset=RAW_BYTES + 4 * M)
-                dst = near[s // 2][:, s % 2, :]
-            near["one", s] = dst
-            nc.vector.tensor_copy(dst, windows["back", s][:].indirect(near_list[:]))
+                near[s] = turns.tile([P, M], F32, name="near%d" % s, offset=RAW0 + 4 * M * (s - 5))
+            nc.vector.tensor_copy(near[s][:], windows["back", s][:].indirect(near_list[:]))
 
         def square_near(s):
-            nc.scalar.activation(pair_tile(damp, "damp", s, 2)[:, s % 2, :], near["one", s], ACT.Square,
+            nc.scalar.activation(pair_tile(damp, "damp", s, 2)[:, s % 2, :], near[s][:], ACT.Square,
                                  scale=inv_root[:, s:s + 1])
 
         def root_pair(s):
             nc.scalar.activation(damp[s // 2][:], damp[s // 2][:], ACT.Abs_reciprocal_sqrt, bias=1.0)
-
-        def root_one(s):
-            nc.scalar.activation(damp[0][:, s, :], damp[0][:, s, :], ACT.Abs_reciprocal_sqrt, bias=1.0)
-
-        def damp_one(s):
-            nc.scalar.activation(damp[0][:, s, :], damp[0][:, s, :], ACT.Square)
 
         def damp_pair(s, m0=0, m1=M):
             nc.scalar.activation(damp[s // 2][:, :, m0:m1], damp[s // 2][:, :, m0:m1], ACT.Square)
@@ -233,22 +220,30 @@ def tile_list_hail_indemnity_kernel(tc, tab_words, tab_scales, offs, pos1, pos2,
                                     windows["back", s][:].indirect(base_list[:, m0 // 16:m1 // 16]),
                                     ratio[s // 2][:, s % 2, m0:m1], ALU.subtract)
 
+        z_sets = ((0, 1), (2,), (3,))
         z_bf, z_codes, z_scales = {}, {}, {}
+        for pieces in z_sets:
+            bf = keep.tile([P, len(pieces), HM, PACK], BF16, name="z_bf%d" % pieces[0], align_bytes=64)
+            codes = keep.tile([P, len(pieces), HM], U32, name="z_codes%d" % pieces[0], align_bytes=64)
+            scales = keep.tile([P, len(pieces), HM], U8, name="z_scales%d" % pieces[0], align_bytes=64)
+            z_bf[pieces], z_codes[pieces], z_scales[pieces] = bf, codes, scales
 
-        def round_z(b, m0, m1, on_vector):
-            z_bf[b, m0] = keep.tile([P, m1 - m0, PACK], BF16, name="z_bf%d_%d" % (b, m0), align_bytes=64)
-            dst = z_bf[b, m0][:].rearrange("p (c i) t -> p c t i", i=4)
-            src = negz[b][:, :, m0:m1].rearrange("p t (c i) -> p c t i", i=4)
+        def piece(store, b, c):
+            pieces = [q for q in z_sets if 2 * b + c in q][0]
+            return store[pieces][:, pieces.index(2 * b + c)]
+
+        def round_z(b, c, on_vector):
+            dst = piece(z_bf, b, c).rearrange("p (c i) t -> p c t i", i=4)
+            src = negz[b][:, :, c * HM:(c + 1) * HM].rearrange("p t (c i) -> p c t i", i=4)
             if on_vector:
                 nc.vector.tensor_scalar(dst, src, -1.0, None, ALU.mult)
             else:
                 nc.scalar.activation(dst, src, ACT.Copy, scale=-1.0)
 
-        def quant_z(b, m0, m1):
-            z_codes[b, m0] = keep.tile([P, m1 - m0], U32, name="z_codes%d_%d" % (b, m0), align_bytes=64)
-            z_scales[b, m0] = keep.tile([P, m1 - m0], U8, name="z_scales%d_%d" % (b, m0), align_bytes=64)
-            nc.vector.quantize_mx(out=z_codes[b, m0][:].bitcast(FP8X4), scales=z_scales[b, m0][:],
-                                  in_=z_bf[b, m0][:].rearrange("p m t -> p (m t)"))
+        def quant_z(pieces):
+            nc.vector.quantize_mx(out=z_codes[pieces][:].rearrange("p u m -> p (u m)").bitcast(FP8X4),
+                                  scales=z_scales[pieces][:].rearrange("p u m -> p (u m)"),
+                                  in_=z_bf[pieces][:].rearrange("p u m t -> p (u m t)"))
 
         loss = {}
         late = {}
@@ -257,7 +252,7 @@ def tile_list_hail_indemnity_kernel(tc, tab_words, tab_scales, offs, pos1, pos2,
             late["ded"] = turns.tile([P, NT], F32, name="ded_t", offset=FIRST_RAW + 7680)
             with nc.allow_non_contiguous_dma(reason="one deductible a partition"):
                 nc.sync.dma_start(late["ded"][:], ded.rearrange("(c p) -> p c", p=P))
-            late["w3s"] = turns.tile([P, PASSES * N // 4], I32, name="w3s", offset=FIRST_RAW + 6144, align_bytes=64)
+            late["w3s"] = turns.tile([P, PASSES * N // 4], I32, name="w3s", offset=TAB1, align_bytes=64)
             nc.gpsimd.memset(late["w3s"][:], 0)
             late["w3w"] = turns.tile([P, PASSES, N], I32, name="w3_w", offset=FIRST_RAW, align_bytes=64)
             nc.sync.dma_start(late["w3w"][:], w3_words.rearrange("a p c i -> p a (c i)").bitcast(I32))
@@ -266,86 +261,81 @@ def tile_list_hail_indemnity_kernel(tc, tab_words, tab_scales, offs, pos1, pos2,
                     late["w3s"][32 * q:32 * q + 4, :].rearrange("r (a c) -> r a c", a=PASSES),
                     w3_scales.bitcast(I32)[:, 4 * q:4 * q + 4, :].rearrange("a r c -> r a c"))
 
-        def bank_groups(m0, m1):
-            per_bank = BANK // (m1 - m0)
-            return [range(c0, min(c0 + per_bank, NT)) for c0 in range(0, NT, per_bank)]
+        groups = [range(c0, c0 + 2) for c0 in range(0, NT, 2)]
 
-        def last_pass(b, m0, m1):
-            for group in bank_groups(m0, m1):
+        def last_pass(b, c):
+            for group in groups:
                 if b == 0:
-                    loss[m0, group[0]] = psum.tile([P, len(group), m1 - m0], F32, name="acc", tag="acc")
-                    rhs, rhs_s = z_codes[0, 0][:, m0:m1], z_scales[0, 0][:, m0:m1]
-                else:
-                    rhs, rhs_s = z_codes[1, m0][:], z_scales[1, m0][:]
-                for u, c in enumerate(group):
-                    nc.tensor.matmul_mx(out=loss[m0, group[0]][:, u, :],
-                                        lhsT=late["w3w"][:, b, c * P:(c + 1) * P].bitcast(FP8X4),
-                                        lhsT_scale=late["w3s"][:].bitcast(U8)[:, b * N + c * P:b * N + (c + 1) * P],
-                                        rhs=rhs.bitcast(FP8X4), rhs_scale=rhs_s,
-                                        start=(b == 0 and u == 0), stop=(b == 1 and u == len(group) - 1))
+                    loss[c, group[0]] = psum.tile([P, 2, HM], F32, name="acc", tag="acc")
+                for u, n in enumerate(group):
+                    nc.tensor.matmul_mx(out=loss[c, group[0]][:, u, :],
+                                        lhsT=late["w3w"][:, b, n * P:(n + 1) * P].bitcast(FP8X4),
+                                        lhsT_scale=late["w3s"][:].bitcast(U8)[:, b * N + n * P:b * N + (n + 1) * P],
+                                        rhs=piece(z_codes, b, c).bitcast(FP8X4), rhs_scale=piece(z_scales, b, c),
+                                        start=(b == 0 and u == 0), stop=(b == 1 and u == 1))
 
-        def finish(m0, m1, group, on_vector):
-            n, c0 = len(group), group[0]
-            acc = loss[m0, c0]
-            res = keep.tile([P, n, m1 - m0], F32, name="res%d_%d" % (m0, c0), align_bytes=64)
+        def finish(c, group, on_vector):
+            n0 = group[0]
+            acc = loss[c, n0]
+            res = keep.tile([P, 2, HM], F32, name="res%d_%d" % (c, n0), align_bytes=64)
             if on_vector:
                 nc.vector.tensor_tensor(res[:], acc[:],
-                                        late["ded"][:, c0:c0 + n].unsqueeze(2).to_broadcast([P, n, m1 - m0]), ALU.max)
+                                        late["ded"][:, n0:n0 + 2].unsqueeze(2).to_broadcast([P, 2, HM]), ALU.max)
             else:
-                over = work.tile([P, n, m1 - m0], F32, name="over", tag="over", bufs=2)
-                for u, c in enumerate(group):
-                    nc.scalar.activation(over[:, u, :], acc[:, u, :], ACT.Relu, bias=late["neg"][:, c:c + 1])
-                for u, c in enumerate(group):
-                    nc.scalar.activation(res[:, u, :], over[:, u, :], ACT.Identity, bias=late["ded"][:, c:c + 1])
-            nc.sync.dma_start(out[c0 * P:(c0 + n) * P, m0:m1].rearrange("(u p) m -> p u m", p=P), res[:])
+                over = work.tile([P, 2, HM], F32, name="over", tag="over", bufs=2)
+                for u, n in enumerate(group):
+                    nc.scalar.activation(over[:, u, :], acc[:, u, :], ACT.Relu, bias=late["neg"][:, n:n + 1])
+                for u, n in enumerate(group):
+                    nc.scalar.activation(res[:, u, :], over[:, u, :], ACT.Identity, bias=late["ded"][:, n:n + 1])
+            nc.sync.dma_start(out[n0 * P:(n0 + 2) * P, c * HM:(c + 1) * HM].rearrange("(u p) m -> p u m", p=P), res[:])
 
-        for s, h in ((0, 0), (1, 0), (0, 1), (1, 1)):
-            rows("back", s, h)
-        cast_w1(0, 0)
-        quant_w1(0, 0)
+        opened = [(s, h) for h in range(2) for s in range(4)]
+        for s, h in opened:
+            one_pass("back", s, h, 0, True)
+        for s, h in opened:
+            one_pass("back", s, h, 1, False)
+        for s, h in opened:
+            empty("back", s, h)
         pick_near(0)
         pick_near(1)
-        window("back", 2)
-        pick_near(2)
+        cast_w1(0, 0)
         cast_w1(1, 0)
+        quant_w1(0, 0)
         quant_w1(1, 0)
         cast_w1(0, 1)
         quant_w1(0, 1)
         cast_w1(1, 1)
         quant_w1(1, 1)
-        for s in range(3, 6):
-            window("back", s)
-            pick_near(s)
+        pick_near(2)
+        pick_near(3)
+        window("back", 4)
+        pick_near(4)
         square_near(0)
-        rows("back", 6, 0)
-        root_one(0)
-        rows("back", 6, 1)
+        square_near(1)
+        window("back", 5)
+        pick_near(5)
+        window("back", 6)
         pick_near(6)
         window("back", 7)
         pick_near(7)
-        square_near(1)
-        damp_one(0)
-        root_one(1)
-        rows("hail", 0, 0)
-        damp_one(1)
-        rows("hail", 0, 1)
+        root_pair(0)
+        window("hail", 0)
+        damp_pair(0)
         window("hail", 1)
         for s in (0, 1):
             pick_field(s)
         for s in (0, 1):
             pick_base(s)
-        cuts = (0, HM, M)
-        chunks = list(zip(cuts[:-1], cuts[1:]))
         for s in range(2, SLICES, 2):
             banks = [(u, h) for u in (s, s + 1) for h in range(2)]
             for u, h in banks:
                 multiply("hail", u, h)
             square_near(s)
             square_near(s + 1)
-            for u, h in reversed(banks[2:]):
+            for u, h in banks[:2]:
                 empty("hail", u, h)
             root_pair(s)
-            for u, h in reversed(banks[:2]):
+            for u, h in banks[2:]:
                 empty("hail", u, h)
             if s + 2 < SLICES:
                 damp_pair(s)
@@ -357,30 +347,30 @@ def tile_list_hail_indemnity_kernel(tc, tab_words, tab_scales, offs, pos1, pos2,
         late["neg"] = keep.tile([P, NT], F32, name="neg_ded")
         nc.scalar.activation(late["neg"][:], late["ded"][:], ACT.Copy, scale=-1.0)
         s6, s7 = SLICES - 2, SLICES - 1
-        for i, (m0, m1) in enumerate(chunks):
-            damp_pair(s6, m0, m1)
-            pick_field(s6, m0, m1)
-            pick_field(s7, m0, m1)
-            if i == 0:
-                pick_base(s6, m0, m1)
-                pick_base(s7, m0, m1)
-                round_z(0, 0, M, False)
-                quant_z(0, 0, M)
-                for c in chunks:
-                    last_pass(0, *c)
-            else:
-                base = turns.tile([P, 2, HM], F32, name="base_last", offset=RAW0)
-                for u in (s6, s7):
-                    nc.scalar.activation(base[:, u % 2, :], windows["back", u][:].indirect(base_list[:, HM // 16:]),
-                                         ACT.Copy)
-                nc.vector.tensor_tensor(negz[1][:, 2:, HM:], base[:], ratio[s6 // 2][:, :, HM:], ALU.subtract)
-                round_z(1, *chunks[i - 1], False)
-                quant_z(1, *chunks[i - 1])
-                last_pass(1, *chunks[i - 1])
-        round_z(1, *chunks[-1], True)
-        quant_z(1, *chunks[-1])
-        last_pass(1, *chunks[-1])
-        for group in bank_groups(*chunks[0]):
-            finish(*chunks[0], group, group[-1] == NT - 1)
-        for group in bank_groups(*chunks[1]):
-            finish(*chunks[1], group, True)
+        damp_pair(s6, 0, HM)
+        for u in (s6, s7):
+            pick_field(u, 0, HM)
+        for u in (s6, s7):
+            pick_base(u, 0, HM)
+        nc.scalar.activation(z_bf[z_sets[0]][:].rearrange("p u (c i) t -> p (u c) t i", i=4),
+                             negz[0][:].rearrange("p t (c i) -> p c t i", i=4), ACT.Copy, scale=-1.0)
+        quant_z(z_sets[0])
+        last_pass(0, 0)
+        last_pass(0, 1)
+        damp_pair(s6, HM, M)
+        for u in (s6, s7):
+            pick_field(u, HM, M)
+        base = turns.tile([P, 2, HM], F32, name="base_last", offset=RAW0)
+        for u in (s6, s7):
+            nc.scalar.activation(base[:, u % 2, :], windows["back", u][:].indirect(base_list[:, HM // 16:]), ACT.Copy)
+        nc.vector.tensor_tensor(negz[1][:, 2:, HM:], base[:], ratio[s6 // 2][:, :, HM:], ALU.subtract)
+        round_z(1, 0, False)
+        quant_z(z_sets[1])
+        last_pass(1, 0)
+        round_z(1, 1, True)
+        quant_z(z_sets[2])
+        last_pass(1, 1)
+        for group in groups:
+            finish(0, group, group[-1] == NT - 1)
+        for group in groups:
+            finish(1, group, True)

@@ -27,10 +27,14 @@ NT = N // P
 HM = M // 2
 TAB_BYTES = 4 * T
 RAW_BYTES = 4 * PACK * KP
-TAB1 = TAB_BYTES
-TAB_ROWS = 2 * TAB_BYTES
-RAW0 = 0
-FIRST_RAW = TAB_ROWS + T
+PLANE1 = TAB_BYTES
+TAB1 = PLANE1 + S + H
+RAW2 = TAB1 + 2048
+RAW3 = RAW2 + RAW_BYTES
+W2_DEALT = RAW3 + RAW_BYTES
+W2_RAW = W2_DEALT + 4 * H
+ROWS = (16, 112)
+EMPTY = ((0, 16), (32, 64), (64, 112))
 
 
 def tile_list_hail_indemnity_kernel(tc, tab_words, tab_scales, offs, pos1, pos2, pos3, w1,
@@ -43,15 +47,15 @@ def tile_list_hail_indemnity_kernel(tc, tab_words, tab_scales, offs, pos1, pos2,
         psum = ctx.enter_context(tc.psum_pool(name="psum", bufs=8))
 
         tab_rows = turns.tile([P, T // 4], I32, name="tab_rows", offset=TAB1 + T, align_bytes=64)
-        nc.vector.memset(tab_rows[32:64, :], 0)
-        nc.vector.memset(tab_rows[64:P, :], 0)
+        for p0, p1 in EMPTY:
+            nc.vector.memset(tab_rows[p0:p1, :], 0)
         half_t = keep.tile([P, GROUPS, PACK], F32, name="half_t")
         nc.gpsimd.dma_start(half_t[:], half.rearrange("(b p t) -> p b t", b=GROUPS, t=PACK))
-        w2s_rows = turns.tile([P, H // 4], I32, name="w2s_rows", offset=TAB_ROWS - H // 2, align_bytes=64)
-        nc.gpsimd.memset(w2s_rows[32:64, :], 0)
-        nc.gpsimd.memset(w2s_rows[64:P, :], 0)
-        planes = keep.tile([P, PASSES, (S + H) // 4], I32, name="planes", align_bytes=64)
-        nc.vector.memset(planes[:], 0)
+        w2s_rows = turns.tile([P, H // 4], I32, name="w2s_rows", offset=TAB1 + S, align_bytes=64)
+        for p0, p1 in EMPTY:
+            nc.gpsimd.memset(w2s_rows[p0:p1, :], 0)
+        planes = [keep.tile([P, (S + H) // 4], I32, name="plane0", align_bytes=64)]
+        nc.vector.memset(planes[0][:], 0)
 
         lists = {}
 
@@ -60,16 +64,18 @@ def tile_list_hail_indemnity_kernel(tc, tab_words, tab_scales, offs, pos1, pos2,
             nc.sync.dma_start(lists[name][:], src)
 
         load_list("offs", offs)
-        nc.sync.dma_start(tab_rows[0:32, :], tab_scales.bitcast(I32).rearrange("a q t -> q a t"))
-        nc.sync.dma_start(w2s_rows[0:32, :], w2_scales.bitcast(I32).rearrange("a q c -> q a c"))
-        w2_raw = turns.tile([P, PASSES, H // 2], I32, name="w2_raw", offset=FIRST_RAW, align_bytes=64)
+        for a in range(PASSES):
+            nc.sync.dma_start(tab_rows[ROWS[a]:ROWS[a] + 16, :], tab_scales[a].bitcast(I32))
+        for a in range(PASSES):
+            nc.sync.dma_start(w2s_rows[ROWS[a]:ROWS[a] + 16, :], w2_scales[a].bitcast(I32))
+        w2_raw = turns.tile([P, PASSES, H // 2], I32, name="w2_raw", offset=W2_RAW, align_bytes=64)
         nc.sync.dma_start(w2_raw[:], w2_words.bitcast(I32).rearrange("a p c -> p a c"))
         load_list("pos2", pos2)
+        tab_w = [turns.tile([P, T], I32, name="tab_w0", offset=0, align_bytes=64)]
+        nc.sync.dma_start(tab_w[0][:], tab_words[0].rearrange("p t i -> p (t i)").bitcast(I32))
         load_list("pos1", pos1)
         load_list("pos3", pos3)
         offs_t, near_list, field_list, base_list = lists["offs"], lists["pos2"], lists["pos1"], lists["pos3"]
-        tab_w = [turns.tile([P, T], I32, name="tab_w0", offset=0, align_bytes=64)]
-        nc.sync.dma_start(tab_w[0][:], tab_words[0].rearrange("p t i -> p (t i)").bitcast(I32))
         inv_root = keep.tile([P, SLICES], F32, name="inv_root")
         nc.scalar.activation(inv_root[:], half_t[:].rearrange("p b t -> p (b t)"), ACT.Abs_reciprocal_sqrt)
         inv_half = keep.tile([P, SLICES], F32, name="inv_half")
@@ -79,23 +85,30 @@ def tile_list_hail_indemnity_kernel(tc, tab_words, tab_scales, offs, pos1, pos2,
         nc.gpsimd.tensor_copy(
             staged[:, S // 4:].bitcast(U8).rearrange("p (g t m n) -> p g m t n", t=PACK, m=P // 16, n=16),
             w2s_rows[:].bitcast(U8).rearrange("p (g m n t) -> p g m t n", t=PACK, m=P // 16, n=16))
-        v_rows = turns.tile([P, S // 4], I32, name="v_rows", offset=TAB1, align_bytes=64)
+        v_rows = turns.tile([P, S // 4], I32, name="v_rows", offset=TAB1 - S // 2, align_bytes=64)
         nc.vector.tensor_copy(v_rows[:].bitcast(U8), tab_rows[:].bitcast(U8).indirect(offs_t[:]))
         nc.vector.tensor_copy(staged[:, :S // 4], v_rows[:])
-        for q in range(4):
-            nc.sync.dma_start(planes[32 * q:32 * q + 4], staged[8 * q:8 * q + 8, :])
+
+        def move_planes(a):
+            for q in range(4):
+                nc.sync.dma_start(planes[a][32 * q:32 * q + 4, :], staged[ROWS[a] + 4 * q:ROWS[a] + 4 * q + 4, :])
+
+        move_planes(0)
         tab_w.append(turns.tile([P, T], I32, name="tab_w1", offset=TAB1, align_bytes=64))
         nc.sync.dma_start(tab_w[1][:], tab_words[1].rearrange("p t i -> p (t i)").bitcast(I32))
-        v_planes = [planes[:, a, :S // 4] for a in range(PASSES)]
-        w2s = [planes[:, a, S // 4:].bitcast(U8) for a in range(PASSES)]
+        planes.append(turns.tile([P, (S + H) // 4], I32, name="plane1", offset=PLANE1, align_bytes=64))
+        nc.vector.memset(planes[1][:], 0)
+        move_planes(1)
+        v_planes = [planes[a][:, :S // 4] for a in range(PASSES)]
+        w2s = [planes[a][:, S // 4:].bitcast(U8) for a in range(PASSES)]
 
-        w2c = turns.tile([P, PASSES * H * 2], U8, name="w2c", offset=TAB_ROWS, align_bytes=64)
+        w2c = turns.tile([P, PASSES * H * 2], U8, name="w2c", offset=W2_DEALT, align_bytes=64)
         nc.vector.tensor_copy(
             w2c[:].bitcast(U16).rearrange("p (g t m n) -> p g m t n", t=PACK, m=P // 8, n=8),
             w2_raw[:].rearrange("p a c -> p (a c)").bitcast(U16).rearrange("p (g m n t) -> p g m t n", t=PACK, m=P // 8, n=8))
 
         v_words = {}
-        whole = turns.tile([P, S], I32, name="v_words0", offset=FIRST_RAW + RAW_BYTES, align_bytes=64)
+        whole = turns.tile([P, S], I32, name="v_words0", offset=W2_RAW + 4 * H, align_bytes=64)
         nc.vector.tensor_copy(whole[:].bitcast(U32), tab_w[0][:].bitcast(U32).indirect(offs_t[:]))
         for h in range(2):
             v_words[0, h] = whole[:, h * BANK:(h + 1) * BANK]
@@ -105,7 +118,7 @@ def tile_list_hail_indemnity_kernel(tc, tab_words, tab_scales, offs, pos1, pos2,
         def load_w1(b):
             for a in range(PASSES):
                 w1_raw[a, b] = turns.tile([P, PACK, KP], F32, name="w1_raw%d%d" % (a, b),
-                                          offset=((FIRST_RAW, RAW0), (RAW_BYTES, TAB1 + RAW_BYTES))[a][b])
+                                          offset=((0, RAW2), (RAW_BYTES, RAW3))[a][b])
                 nc.sync.dma_start(
                     w1_raw[a, b][:],
                     w1[a * KP:(a + 1) * KP, b * KP:(b + 1) * KP].rearrange("(p j) c -> p j c", j=PACK))
@@ -195,7 +208,7 @@ def tile_list_hail_indemnity_kernel(tc, tab_words, tab_scales, offs, pos1, pos2,
             elif s < 5:
                 near[s] = turns.tile([P, M], F32, name="near%d" % s, offset=RAW_BYTES + 4 * M * (s - 2))
             else:
-                near[s] = turns.tile([P, M], F32, name="near%d" % s, offset=RAW0 + 4 * M * (s - 5))
+                near[s] = turns.tile([P, M], F32, name="near%d" % s, offset=RAW2 + 4 * M * (s - 5))
             nc.vector.tensor_copy(near[s][:], windows["back", s][:].indirect(near_list[:]))
 
         def square_near(s):
@@ -210,7 +223,7 @@ def tile_list_hail_indemnity_kernel(tc, tab_words, tab_scales, offs, pos1, pos2,
 
         def pick_field(s, m0=0, m1=M):
             if s == 0:
-                ratio[0] = turns.tile([P, 2, M], F32, name="ratio01", offset=TAB1 + RAW_BYTES)
+                ratio[0] = turns.tile([P, 2, M], F32, name="ratio01", offset=RAW3)
             nc.vector.tensor_tensor(pair_tile(ratio, "ratio", s, 2)[:, s % 2, m0:m1],
                                     windows["hail", s][:].indirect(field_list[:, m0 // 16:m1 // 16]),
                                     damp[s // 2][:, s % 2, m0:m1], ALU.mult)
@@ -249,12 +262,12 @@ def tile_list_hail_indemnity_kernel(tc, tab_words, tab_scales, offs, pos1, pos2,
         late = {}
 
         def load_last():
-            late["ded"] = turns.tile([P, NT], F32, name="ded_t", offset=FIRST_RAW + 7680)
+            late["ded"] = turns.tile([P, NT], F32, name="ded_t", offset=7680)
             with nc.allow_non_contiguous_dma(reason="one deductible a partition"):
                 nc.sync.dma_start(late["ded"][:], ded.rearrange("(c p) -> p c", p=P))
             late["w3s"] = turns.tile([P, PASSES * N // 4], I32, name="w3s", offset=TAB1, align_bytes=64)
             nc.gpsimd.memset(late["w3s"][:], 0)
-            late["w3w"] = turns.tile([P, PASSES, N], I32, name="w3_w", offset=FIRST_RAW, align_bytes=64)
+            late["w3w"] = turns.tile([P, PASSES, N], I32, name="w3_w", offset=0, align_bytes=64)
             nc.sync.dma_start(late["w3w"][:], w3_words.rearrange("a p c i -> p a (c i)").bitcast(I32))
             for q in range(4):
                 nc.sync.dma_start(
@@ -360,7 +373,7 @@ def tile_list_hail_indemnity_kernel(tc, tab_words, tab_scales, offs, pos1, pos2,
         damp_pair(s6, HM, M)
         for u in (s6, s7):
             pick_field(u, HM, M)
-        base = turns.tile([P, 2, HM], F32, name="base_last", offset=RAW0)
+        base = turns.tile([P, 2, HM], F32, name="base_last", offset=RAW2)
         for u in (s6, s7):
             nc.scalar.activation(base[:, u % 2, :], windows["back", u][:].indirect(base_list[:, HM // 16:]), ACT.Copy)
         nc.vector.tensor_tensor(negz[1][:, 2:, HM:], base[:], ratio[s6 // 2][:, :, HM:], ALU.subtract)

@@ -27,14 +27,10 @@ NT = N // P
 HM = M // 2
 TAB_BYTES = 4 * T
 RAW_BYTES = 4 * PACK * KP
-PLANE1 = TAB_BYTES
-TAB1 = PLANE1 + S + H
-RAW2 = TAB1 + 2048
-RAW3 = RAW2 + RAW_BYTES
-W2_DEALT = RAW3 + RAW_BYTES
-W2_RAW = W2_DEALT + 4 * H
-ROWS = (16, 112)
-EMPTY = ((0, 16), (32, 64), (64, 112))
+TAB1 = TAB_BYTES
+TAB_ROWS = 2 * TAB_BYTES
+RAW0 = 0
+FIRST_RAW = TAB_ROWS + T
 
 
 def tile_list_hail_indemnity_kernel(tc, tab_words, tab_scales, offs, pos1, pos2, pos3, w1,
@@ -47,15 +43,15 @@ def tile_list_hail_indemnity_kernel(tc, tab_words, tab_scales, offs, pos1, pos2,
         psum = ctx.enter_context(tc.psum_pool(name="psum", bufs=8))
 
         tab_rows = turns.tile([P, T // 4], I32, name="tab_rows", offset=TAB1 + T, align_bytes=64)
-        for p0, p1 in EMPTY:
-            nc.vector.memset(tab_rows[p0:p1, :], 0)
+        nc.vector.memset(tab_rows[32:64, :], 0)
+        nc.vector.memset(tab_rows[64:P, :], 0)
         half_t = keep.tile([P, GROUPS, PACK], F32, name="half_t")
         nc.gpsimd.dma_start(half_t[:], half.rearrange("(b p t) -> p b t", b=GROUPS, t=PACK))
-        w2s_rows = turns.tile([P, H // 4], I32, name="w2s_rows", offset=TAB1 + S, align_bytes=64)
-        for p0, p1 in EMPTY:
-            nc.gpsimd.memset(w2s_rows[p0:p1, :], 0)
-        planes = [keep.tile([P, (S + H) // 4], I32, name="plane0", align_bytes=64)]
-        nc.vector.memset(planes[0][:], 0)
+        w2s_rows = turns.tile([P, H // 4], I32, name="w2s_rows", offset=TAB_ROWS - H // 2, align_bytes=64)
+        nc.gpsimd.memset(w2s_rows[32:64, :], 0)
+        nc.gpsimd.memset(w2s_rows[64:P, :], 0)
+        planes = keep.tile([P, PASSES, (S + H) // 4], I32, name="planes", align_bytes=64)
+        nc.vector.memset(planes[:], 0)
 
         lists = {}
 
@@ -64,18 +60,16 @@ def tile_list_hail_indemnity_kernel(tc, tab_words, tab_scales, offs, pos1, pos2,
             nc.sync.dma_start(lists[name][:], src)
 
         load_list("offs", offs)
-        for a in range(PASSES):
-            nc.sync.dma_start(tab_rows[ROWS[a]:ROWS[a] + 16, :], tab_scales[a].bitcast(I32))
-        for a in range(PASSES):
-            nc.sync.dma_start(w2s_rows[ROWS[a]:ROWS[a] + 16, :], w2_scales[a].bitcast(I32))
-        w2_raw = turns.tile([P, PASSES, H // 2], I32, name="w2_raw", offset=W2_RAW, align_bytes=64)
+        nc.sync.dma_start(tab_rows[0:32, :], tab_scales.bitcast(I32).rearrange("a q t -> q a t"))
+        nc.sync.dma_start(w2s_rows[0:32, :], w2_scales.bitcast(I32).rearrange("a q c -> q a c"))
+        w2_raw = turns.tile([P, PASSES, H // 2], I32, name="w2_raw", offset=FIRST_RAW, align_bytes=64)
         nc.sync.dma_start(w2_raw[:], w2_words.bitcast(I32).rearrange("a p c -> p a c"))
         load_list("pos2", pos2)
-        tab_w = [turns.tile([P, T], I32, name="tab_w0", offset=0, align_bytes=64)]
-        nc.sync.dma_start(tab_w[0][:], tab_words[0].rearrange("p t i -> p (t i)").bitcast(I32))
         load_list("pos1", pos1)
         load_list("pos3", pos3)
         offs_t, near_list, field_list, base_list = lists["offs"], lists["pos2"], lists["pos1"], lists["pos3"]
+        tab_w = [turns.tile([P, T], I32, name="tab_w0", offset=0, align_bytes=64)]
+        nc.sync.dma_start(tab_w[0][:], tab_words[0].rearrange("p t i -> p (t i)").bitcast(I32))
         inv_root = keep.tile([P, SLICES], F32, name="inv_root")
         nc.scalar.activation(inv_root[:], half_t[:].rearrange("p b t -> p (b t)"), ACT.Abs_reciprocal_sqrt)
         inv_half = keep.tile([P, SLICES], F32, name="inv_half")
@@ -85,30 +79,23 @@ def tile_list_hail_indemnity_kernel(tc, tab_words, tab_scales, offs, pos1, pos2,
         nc.gpsimd.tensor_copy(
             staged[:, S // 4:].bitcast(U8).rearrange("p (g t m n) -> p g m t n", t=PACK, m=P // 16, n=16),
             w2s_rows[:].bitcast(U8).rearrange("p (g m n t) -> p g m t n", t=PACK, m=P // 16, n=16))
-        v_rows = turns.tile([P, S // 4], I32, name="v_rows", offset=TAB1 - S // 2, align_bytes=64)
+        v_rows = turns.tile([P, S // 4], I32, name="v_rows", offset=TAB1, align_bytes=64)
         nc.vector.tensor_copy(v_rows[:].bitcast(U8), tab_rows[:].bitcast(U8).indirect(offs_t[:]))
         nc.vector.tensor_copy(staged[:, :S // 4], v_rows[:])
-
-        def move_planes(a):
-            for q in range(4):
-                nc.sync.dma_start(planes[a][32 * q:32 * q + 4, :], staged[ROWS[a] + 4 * q:ROWS[a] + 4 * q + 4, :])
-
-        move_planes(0)
+        for q in range(4):
+            nc.sync.dma_start(planes[32 * q:32 * q + 4], staged[8 * q:8 * q + 8, :])
         tab_w.append(turns.tile([P, T], I32, name="tab_w1", offset=TAB1, align_bytes=64))
         nc.sync.dma_start(tab_w[1][:], tab_words[1].rearrange("p t i -> p (t i)").bitcast(I32))
-        planes.append(turns.tile([P, (S + H) // 4], I32, name="plane1", offset=PLANE1, align_bytes=64))
-        nc.vector.memset(planes[1][:], 0)
-        move_planes(1)
-        v_planes = [planes[a][:, :S // 4] for a in range(PASSES)]
-        w2s = [planes[a][:, S // 4:].bitcast(U8) for a in range(PASSES)]
+        v_planes = [planes[:, a, :S // 4] for a in range(PASSES)]
+        w2s = [planes[:, a, S // 4:].bitcast(U8) for a in range(PASSES)]
 
-        w2c = turns.tile([P, PASSES * H * 2], U8, name="w2c", offset=W2_DEALT, align_bytes=64)
+        w2c = turns.tile([P, PASSES * H * 2], U8, name="w2c", offset=TAB_ROWS, align_bytes=64)
         nc.vector.tensor_copy(
             w2c[:].bitcast(U16).rearrange("p (g t m n) -> p g m t n", t=PACK, m=P // 8, n=8),
             w2_raw[:].rearrange("p a c -> p (a c)").bitcast(U16).rearrange("p (g m n t) -> p g m t n", t=PACK, m=P // 8, n=8))
 
         v_words = {}
-        whole = turns.tile([P, S], I32, name="v_words0", offset=W2_RAW + 4 * H, align_bytes=64)
+        whole = turns.tile([P, S], I32, name="v_words0", offset=FIRST_RAW + RAW_BYTES, align_bytes=64)
         nc.vector.tensor_copy(whole[:].bitcast(U32), tab_w[0][:].bitcast(U32).indirect(offs_t[:]))
         for h in range(2):
             v_words[0, h] = whole[:, h * BANK:(h + 1) * BANK]
@@ -118,7 +105,7 @@ def tile_list_hail_indemnity_kernel(tc, tab_words, tab_scales, offs, pos1, pos2,
         def load_w1(b):
             for a in range(PASSES):
                 w1_raw[a, b] = turns.tile([P, PACK, KP], F32, name="w1_raw%d%d" % (a, b),
-                                          offset=((0, RAW2), (RAW_BYTES, RAW3))[a][b])
+                                          offset=((FIRST_RAW, RAW0), (RAW_BYTES, TAB1 + RAW_BYTES))[a][b])
                 nc.sync.dma_start(
                     w1_raw[a, b][:],
                     w1[a * KP:(a + 1) * KP, b * KP:(b + 1) * KP].rearrange("(p j) c -> p j c", j=PACK))
@@ -134,22 +121,20 @@ def tile_list_hail_indemnity_kernel(tc, tab_words, tab_scales, offs, pos1, pos2,
         w1_bf, w1_codes, w1_scales = {}, {}, {}
 
         def cast_w1(a, b):
-            first = (a, b) == (0, 0)
-            w1_bf[a, b] = work.tile([P, PACK, P, PACK], BF16, name="w1_bf", tag="w1_first" if first else "w1_bf",
-                                    bufs=1, align_bytes=64)
-            if (a, b) == (1, 0):
-                nc.vector.tensor_copy(w1_bf[a, b][:].rearrange("p t m j -> p m j t"),
-                                      w1_raw[a, b][:].rearrange("p j (m t) -> p m j t", t=PACK))
-                return
-            dst = w1_bf[a, b][:].rearrange("p t m j -> p m t j")
+            if a == 0:
+                w1_bf[b] = work.tile([P, PASSES, PACK, P, PACK], BF16, name="w1_bf", tag="w1_bf", bufs=1, align_bytes=64)
+            dst = w1_bf[b][:, a].rearrange("p t m j -> p m t j")
             src = w1_raw[a, b][:].rearrange("p j (m t) -> p m t j", t=PACK)
             nc.gpsimd.tensor_scalar(dst, src, 1.0, 0.0, ALU.mult, ALU.add)
 
-        def quant_w1(a, b):
-            w1_codes[a, b] = keep.tile([P, KP], U32, name="w1_codes%d%d" % (a, b), align_bytes=64)
-            w1_scales[a, b] = keep.tile([P, KP], U8, name="w1_scales%d%d" % (a, b), align_bytes=64)
-            nc.vector.quantize_mx(out=w1_codes[a, b][:].bitcast(FP8X4), scales=w1_scales[a, b][:],
-                                  in_=w1_bf[a, b][:].rearrange("p t m j -> p (t m j)"))
+        def quant_w1(b):
+            codes = keep.tile([P, PASSES * KP], U32, name="w1_codes%d" % b, align_bytes=64)
+            scales = keep.tile([P, PASSES * KP], U8, name="w1_scales%d" % b, align_bytes=64)
+            nc.vector.quantize_mx(out=codes[:].bitcast(FP8X4), scales=scales[:],
+                                  in_=w1_bf[b][:].rearrange("p a t m j -> p (a t m j)"))
+            for a in range(PASSES):
+                w1_codes[a, b] = codes[:, a * KP:(a + 1) * KP]
+                w1_scales[a, b] = scales[:, a * KP:(a + 1) * KP]
 
         windows, sums = {}, {}
 
@@ -175,11 +160,13 @@ def tile_list_hail_indemnity_kernel(tc, tab_words, tab_scales, offs, pos1, pos2,
 
         def empty(kind, s, h):
             bank = sums[kind, s, h]
+            if (kind, s) == ("back", SLICES - 1) and h == 0:
+                windows[kind, s] = turns.tile([P, S], F32, name="back_last", offset=RAW_BYTES + 12 * M, align_bytes=64)
             if (kind, s) not in windows:
                 windows[kind, s] = work.tile([P, S], F32, name=kind, tag=kind,
-                                             bufs=SLICES if kind == "back" else 4, align_bytes=64)
+                                             bufs=SLICES - 1 if kind == "back" else 4, align_bytes=64)
             dst = windows[kind, s][:, h * BANK:(h + 1) * BANK]
-            if kind == "back" and s in (2, 3) and h == 0:
+            if kind == "back" and (s == SLICES - 1 or s in (2, 3) and h == 0):
                 nc.vector.tensor_copy(dst, bank[:])
             elif kind == "back":
                 nc.scalar.copy(dst, bank[:])
@@ -203,12 +190,10 @@ def tile_list_hail_indemnity_kernel(tc, tab_words, tab_scales, offs, pos1, pos2,
             return store[s // 2]
 
         def pick_near(s):
-            if s < 2:
-                near[s] = keep.tile([P, M], F32, name="near%d" % s)
-            elif s < 5:
-                near[s] = turns.tile([P, M], F32, name="near%d" % s, offset=RAW_BYTES + 4 * M * (s - 2))
+            if s in (4, 5, 6):
+                near[s] = turns.tile([P, M], F32, name="near%d" % s, offset=RAW_BYTES + 4 * M * (s - 4))
             else:
-                near[s] = turns.tile([P, M], F32, name="near%d" % s, offset=RAW2 + 4 * M * (s - 5))
+                near[s] = keep.tile([P, M], F32, name="near%d" % s)
             nc.vector.tensor_copy(near[s][:], windows["back", s][:].indirect(near_list[:]))
 
         def square_near(s):
@@ -223,7 +208,7 @@ def tile_list_hail_indemnity_kernel(tc, tab_words, tab_scales, offs, pos1, pos2,
 
         def pick_field(s, m0=0, m1=M):
             if s == 0:
-                ratio[0] = turns.tile([P, 2, M], F32, name="ratio01", offset=RAW3)
+                ratio[0] = turns.tile([P, 2, M], F32, name="ratio01", offset=TAB1 + RAW_BYTES)
             nc.vector.tensor_tensor(pair_tile(ratio, "ratio", s, 2)[:, s % 2, m0:m1],
                                     windows["hail", s][:].indirect(field_list[:, m0 // 16:m1 // 16]),
                                     damp[s // 2][:, s % 2, m0:m1], ALU.mult)
@@ -236,16 +221,17 @@ def tile_list_hail_indemnity_kernel(tc, tab_words, tab_scales, offs, pos1, pos2,
         z_sets = ((0, 1), (2,), (3,))
         z_bf, z_codes, z_scales = {}, {}, {}
         for pieces in z_sets:
-            bf = keep.tile([P, len(pieces), HM, PACK], BF16, name="z_bf%d" % pieces[0], align_bytes=64)
             codes = keep.tile([P, len(pieces), HM], U32, name="z_codes%d" % pieces[0], align_bytes=64)
             scales = keep.tile([P, len(pieces), HM], U8, name="z_scales%d" % pieces[0], align_bytes=64)
-            z_bf[pieces], z_codes[pieces], z_scales[pieces] = bf, codes, scales
+            z_codes[pieces], z_scales[pieces] = codes, scales
+        z_bf[z_sets[0]] = keep.tile([P, 2, HM, PACK], BF16, name="z_bf0", align_bytes=64)
 
         def piece(store, b, c):
             pieces = [q for q in z_sets if 2 * b + c in q][0]
             return store[pieces][:, pieces.index(2 * b + c)]
 
         def round_z(b, c, on_vector):
+            z_bf[2 * b + c,] = work.tile([P, 1, HM, PACK], BF16, name="z_bf1", tag="z_bf1", bufs=1, align_bytes=64)
             dst = piece(z_bf, b, c).rearrange("p (c i) t -> p c t i", i=4)
             src = negz[b][:, :, c * HM:(c + 1) * HM].rearrange("p t (c i) -> p c t i", i=4)
             if on_vector:
@@ -262,12 +248,12 @@ def tile_list_hail_indemnity_kernel(tc, tab_words, tab_scales, offs, pos1, pos2,
         late = {}
 
         def load_last():
-            late["ded"] = turns.tile([P, NT], F32, name="ded_t", offset=7680)
+            late["ded"] = turns.tile([P, NT], F32, name="ded_t", offset=FIRST_RAW + 7680)
             with nc.allow_non_contiguous_dma(reason="one deductible a partition"):
                 nc.sync.dma_start(late["ded"][:], ded.rearrange("(c p) -> p c", p=P))
-            late["w3s"] = turns.tile([P, PASSES * N // 4], I32, name="w3s", offset=TAB1, align_bytes=64)
+            late["w3s"] = turns.tile([P, PASSES * N // 4], I32, name="w3s", offset=TAB1 + 2048, align_bytes=64)
             nc.gpsimd.memset(late["w3s"][:], 0)
-            late["w3w"] = turns.tile([P, PASSES, N], I32, name="w3_w", offset=0, align_bytes=64)
+            late["w3w"] = turns.tile([P, PASSES, N], I32, name="w3_w", offset=FIRST_RAW, align_bytes=64)
             nc.sync.dma_start(late["w3w"][:], w3_words.rearrange("a p c i -> p a (c i)").bitcast(I32))
             for q in range(4):
                 nc.sync.dma_start(
@@ -309,18 +295,12 @@ def tile_list_hail_indemnity_kernel(tc, tab_words, tab_scales, offs, pos1, pos2,
             one_pass("back", s, h, 1, False)
         for s, h in opened:
             empty("back", s, h)
-        pick_near(0)
-        pick_near(1)
-        cast_w1(0, 0)
-        cast_w1(1, 0)
-        quant_w1(0, 0)
-        quant_w1(1, 0)
-        cast_w1(0, 1)
-        quant_w1(0, 1)
-        cast_w1(1, 1)
-        quant_w1(1, 1)
-        pick_near(2)
-        pick_near(3)
+        for s in range(4):
+            pick_near(s)
+        for b in range(GROUPS):
+            for a in range(PASSES):
+                cast_w1(a, b)
+            quant_w1(b)
         window("back", 4)
         pick_near(4)
         square_near(0)
@@ -373,7 +353,7 @@ def tile_list_hail_indemnity_kernel(tc, tab_words, tab_scales, offs, pos1, pos2,
         damp_pair(s6, HM, M)
         for u in (s6, s7):
             pick_field(u, HM, M)
-        base = turns.tile([P, 2, HM], F32, name="base_last", offset=RAW2)
+        base = turns.tile([P, 2, HM], F32, name="base_last", offset=RAW_BYTES + 8 * M)
         for u in (s6, s7):
             nc.scalar.activation(base[:, u % 2, :], windows["back", u][:].indirect(base_list[:, HM // 16:]), ACT.Copy)
         nc.vector.tensor_tensor(negz[1][:, 2:, HM:], base[:], ratio[s6 // 2][:, :, HM:], ALU.subtract)

@@ -123,8 +123,8 @@ def tile_list_hail_indemnity_kernel(tc, tab_words, tab_scales, offs, pos1, pos2,
         def cast_w1(a, b):
             if a == 0:
                 w1_bf[b] = work.tile([P, PASSES, PACK, P, PACK], BF16, name="w1_bf", tag="w1_bf", bufs=1, align_bytes=64)
-            dst = w1_bf[b][:, a].rearrange("p t m j -> p m t j")
-            src = w1_raw[a, b][:].rearrange("p j (m t) -> p m t j", t=PACK)
+            dst = w1_bf[b][:, a].rearrange("p t m j -> p m j t")
+            src = w1_raw[a, b][:].rearrange("p j (m t) -> p m j t", t=PACK)
             nc.gpsimd.tensor_scalar(dst, src, 1.0, 0.0, ALU.mult, ALU.add)
 
         def quant_w1(b):
@@ -162,9 +162,11 @@ def tile_list_hail_indemnity_kernel(tc, tab_words, tab_scales, offs, pos1, pos2,
             bank = sums[kind, s, h]
             if (kind, s) == ("back", SLICES - 1) and h == 0:
                 windows[kind, s] = turns.tile([P, S], F32, name="back_last", offset=RAW_BYTES + 12 * M, align_bytes=64)
+            if kind == "hail" and s % PACK == 2 and h == 0:
+                windows[kind, s] = turns.tile([P, S], F32, name="hail%d" % s, offset=RAW0, align_bytes=64)
             if (kind, s) not in windows:
                 windows[kind, s] = work.tile([P, S], F32, name=kind, tag=kind,
-                                             bufs=SLICES - 1 if kind == "back" else 4, align_bytes=64)
+                                             bufs=SLICES - 1 if kind == "back" else 3, align_bytes=64)
             dst = windows[kind, s][:, h * BANK:(h + 1) * BANK]
             if kind == "back" and (s == SLICES - 1 or s in (2, 3) and h == 0):
                 nc.vector.tensor_copy(dst, bank[:])
@@ -197,7 +199,9 @@ def tile_list_hail_indemnity_kernel(tc, tab_words, tab_scales, offs, pos1, pos2,
             nc.vector.tensor_copy(near[s][:], windows["back", s][:].indirect(near_list[:]))
 
         def square_near(s):
-            nc.scalar.activation(pair_tile(damp, "damp", s, 2)[:, s % 2, :], near[s][:], ACT.Square,
+            if s % PACK == 2:
+                damp[s // 2] = turns.tile([P, 2, M], F32, name="damp%d" % s, offset=RAW0 + 4 * S)
+            nc.scalar.activation(pair_tile(damp, "damp", s, 1)[:, s % 2, :], near[s][:], ACT.Square,
                                  scale=inv_root[:, s:s + 1])
 
         def root_pair(s):
@@ -218,20 +222,22 @@ def tile_list_hail_indemnity_kernel(tc, tab_words, tab_scales, offs, pos1, pos2,
                                     windows["back", s][:].indirect(base_list[:, m0 // 16:m1 // 16]),
                                     ratio[s // 2][:, s % 2, m0:m1], ALU.subtract)
 
-        z_sets = ((0, 1), (2,), (3,))
+        z_sets = ((0,), (1,), (2,), (3,))
         z_bf, z_codes, z_scales = {}, {}, {}
         for pieces in z_sets:
             codes = keep.tile([P, len(pieces), HM], U32, name="z_codes%d" % pieces[0], align_bytes=64)
             scales = keep.tile([P, len(pieces), HM], U8, name="z_scales%d" % pieces[0], align_bytes=64)
             z_codes[pieces], z_scales[pieces] = codes, scales
-        z_bf[z_sets[0]] = keep.tile([P, 2, HM, PACK], BF16, name="z_bf0", align_bytes=64)
+        for u in range(2):
+            z_bf[u,] = keep.tile([P, 1, HM, PACK], BF16, name="z_bf0%d" % u, align_bytes=64)
 
         def piece(store, b, c):
             pieces = [q for q in z_sets if 2 * b + c in q][0]
             return store[pieces][:, pieces.index(2 * b + c)]
 
         def round_z(b, c, on_vector):
-            z_bf[2 * b + c,] = work.tile([P, 1, HM, PACK], BF16, name="z_bf1", tag="z_bf1", bufs=1, align_bytes=64)
+            if b == 1:
+                z_bf[2 * b + c,] = work.tile([P, 1, HM, PACK], BF16, name="z_bf1", tag="z_bf1", bufs=1, align_bytes=64)
             dst = piece(z_bf, b, c).rearrange("p (c i) t -> p c t i", i=4)
             src = negz[b][:, :, c * HM:(c + 1) * HM].rearrange("p t (c i) -> p c t i", i=4)
             if on_vector:
@@ -307,13 +313,13 @@ def tile_list_hail_indemnity_kernel(tc, tab_words, tab_scales, offs, pos1, pos2,
         square_near(1)
         window("back", 5)
         pick_near(5)
+        root_pair(0)
         window("back", 6)
         pick_near(6)
+        damp_pair(0)
         window("back", 7)
         pick_near(7)
-        root_pair(0)
         window("hail", 0)
-        damp_pair(0)
         window("hail", 1)
         for s in (0, 1):
             pick_field(s)
@@ -321,14 +327,17 @@ def tile_list_hail_indemnity_kernel(tc, tab_words, tab_scales, offs, pos1, pos2,
             pick_base(s)
         for s in range(2, SLICES, 2):
             banks = [(u, h) for u in (s, s + 1) for h in range(2)]
-            for u, h in banks:
+            ahead, between, behind = (banks[2:], banks[:1], banks[1:2]) if s == 2 else ([], banks[:2], banks[2:])
+            for u, h in ahead + between + behind:
                 multiply("hail", u, h)
+            for u, h in ahead:
+                empty("hail", u, h)
             square_near(s)
             square_near(s + 1)
-            for u, h in banks[:2]:
+            for u, h in between:
                 empty("hail", u, h)
             root_pair(s)
-            for u, h in banks[2:]:
+            for u, h in behind:
                 empty("hail", u, h)
             if s + 2 < SLICES:
                 damp_pair(s)
@@ -340,15 +349,16 @@ def tile_list_hail_indemnity_kernel(tc, tab_words, tab_scales, offs, pos1, pos2,
         late["neg"] = keep.tile([P, NT], F32, name="neg_ded")
         nc.scalar.activation(late["neg"][:], late["ded"][:], ACT.Copy, scale=-1.0)
         s6, s7 = SLICES - 2, SLICES - 1
+        round_z(0, 0, False)
+        quant_z(z_sets[0])
+        last_pass(0, 0)
         damp_pair(s6, 0, HM)
         for u in (s6, s7):
             pick_field(u, 0, HM)
         for u in (s6, s7):
             pick_base(u, 0, HM)
-        nc.scalar.activation(z_bf[z_sets[0]][:].rearrange("p u (c i) t -> p (u c) t i", i=4),
-                             negz[0][:].rearrange("p t (c i) -> p c t i", i=4), ACT.Copy, scale=-1.0)
-        quant_z(z_sets[0])
-        last_pass(0, 0)
+        round_z(0, 1, False)
+        quant_z(z_sets[1])
         last_pass(0, 1)
         damp_pair(s6, HM, M)
         for u in (s6, s7):
@@ -358,10 +368,10 @@ def tile_list_hail_indemnity_kernel(tc, tab_words, tab_scales, offs, pos1, pos2,
             nc.scalar.activation(base[:, u % 2, :], windows["back", u][:].indirect(base_list[:, HM // 16:]), ACT.Copy)
         nc.vector.tensor_tensor(negz[1][:, 2:, HM:], base[:], ratio[s6 // 2][:, :, HM:], ALU.subtract)
         round_z(1, 0, False)
-        quant_z(z_sets[1])
+        quant_z(z_sets[2])
         last_pass(1, 0)
         round_z(1, 1, True)
-        quant_z(z_sets[2])
+        quant_z(z_sets[3])
         last_pass(1, 1)
         for group in groups:
             finish(0, group, group[-1] == NT - 1)

@@ -30,7 +30,11 @@ RAW_BYTES = 4 * PACK * KP
 TAB1 = TAB_BYTES
 TAB_ROWS = 2 * TAB_BYTES
 RAW0 = 0
-FIRST_RAW = TAB_ROWS + T
+W2_LATE = TAB_ROWS + 4 * H
+W2_EARLY = W2_LATE + 5 * H // 2
+FIRST_RAW = W2_LATE + 3 * H
+RAW1 = 4096
+HELD = 64
 
 
 def tile_list_hail_indemnity_kernel(tc, tab_words, tab_scales, offs, pos1, pos2, pos3, w1,
@@ -51,7 +55,7 @@ def tile_list_hail_indemnity_kernel(tc, tab_words, tab_scales, offs, pos1, pos2,
         nc.gpsimd.memset(w2s_rows[32:64, :], 0)
         nc.gpsimd.memset(w2s_rows[64:P, :], 0)
         planes = keep.tile([P, PASSES, (S + H) // 4], I32, name="planes", align_bytes=64)
-        nc.vector.memset(planes[:], 0)
+        nc.gpsimd.memset(planes[:], 0)
 
         lists = {}
 
@@ -62,18 +66,18 @@ def tile_list_hail_indemnity_kernel(tc, tab_words, tab_scales, offs, pos1, pos2,
         load_list("offs", offs)
         nc.sync.dma_start(tab_rows[0:32, :], tab_scales.bitcast(I32).rearrange("a q t -> q a t"))
         nc.sync.dma_start(w2s_rows[0:32, :], w2_scales.bitcast(I32).rearrange("a q c -> q a c"))
-        w2_raw = turns.tile([P, PASSES, H // 2], I32, name="w2_raw", offset=FIRST_RAW, align_bytes=64)
-        nc.sync.dma_start(w2_raw[:], w2_words.bitcast(I32).rearrange("a p c -> p a c"))
+        w2_i32 = w2_words.bitcast(I32)
+        w2_early = turns.tile([P, KP // 2], I32, name="w2_early", offset=W2_EARLY, align_bytes=64)
+        nc.sync.dma_start(w2_early[:], w2_i32[0, :, :KP // 2])
         load_list("pos2", pos2)
         load_list("pos1", pos1)
         load_list("pos3", pos3)
         offs_t, near_list, field_list, base_list = lists["offs"], lists["pos2"], lists["pos1"], lists["pos3"]
         tab_w = [turns.tile([P, T], I32, name="tab_w0", offset=0, align_bytes=64)]
         nc.sync.dma_start(tab_w[0][:], tab_words[0].rearrange("p t i -> p (t i)").bitcast(I32))
-        inv_root = keep.tile([P, SLICES], F32, name="inv_root")
-        nc.scalar.activation(inv_root[:], half_t[:].rearrange("p b t -> p (b t)"), ACT.Abs_reciprocal_sqrt)
-        inv_half = keep.tile([P, SLICES], F32, name="inv_half")
-        nc.scalar.activation(inv_half[:], inv_root[:], ACT.Square)
+        half_col = half_t[:].rearrange("p b t -> p (b t)")
+        inv_root = keep.tile([P, 2], F32, name="inv_root")
+        nc.scalar.activation(inv_root[:], half_col[:, :2], ACT.Abs_reciprocal_sqrt)
 
         staged = keep.tile([P, (S + H) // 4], I32, name="staged", align_bytes=64)
         nc.gpsimd.tensor_copy(
@@ -89,10 +93,23 @@ def tile_list_hail_indemnity_kernel(tc, tab_words, tab_scales, offs, pos1, pos2,
         v_planes = [planes[:, a, :S // 4] for a in range(PASSES)]
         w2s = [planes[:, a, S // 4:].bitcast(U8) for a in range(PASSES)]
 
-        w2c = turns.tile([P, PASSES * H * 2], U8, name="w2c", offset=TAB_ROWS, align_bytes=64)
-        nc.vector.tensor_copy(
-            w2c[:].bitcast(U16).rearrange("p (g t m n) -> p g m t n", t=PACK, m=P // 8, n=8),
-            w2_raw[:].rearrange("p a c -> p (a c)").bitcast(U16).rearrange("p (g m n t) -> p g m t n", t=PACK, m=P // 8, n=8))
+        w2c = {}
+
+        def deal_w2(parts, raw, copy):
+            dealt = turns.tile([P, len(parts) * KP * 2], U8, name="w2c%d" % len(w2c), offset=TAB_ROWS + len(w2c) * H,
+                               align_bytes=64)
+            copy(dealt[:].bitcast(U16).rearrange("p (g t m n) -> p g m t n", t=PACK, m=P // 8, n=8),
+                 raw.bitcast(U16).rearrange("p (g m n t) -> p g m t n", t=PACK, m=P // 8, n=8))
+            for i, part in enumerate(parts):
+                w2c[part] = dealt[:, i * 2 * KP:(i + 1) * 2 * KP]
+
+        deal_w2([(0, 0)], w2_early[:], nc.vector.tensor_copy)
+        w2_late = turns.tile([P, 3 * KP // 2], I32, name="w2_late", offset=W2_LATE, align_bytes=64)
+        nc.sync.dma_start(w2_late[:, :KP // 2], w2_i32[1, :, :KP // 2])
+        nc.sync.dma_start(w2_late[:, KP // 2:].rearrange("p (a c) -> p a c", a=PASSES),
+                          w2_i32[:, :, KP // 2:].rearrange("a p c -> p a c"))
+        deal_w2([(1, 0)], w2_late[:, :KP // 2], nc.scalar.copy)
+        deal_w2([(0, 1), (1, 1)], w2_late[:, KP // 2:], nc.scalar.copy)
 
         v_words = {}
         whole = turns.tile([P, S], I32, name="v_words0", offset=FIRST_RAW + RAW_BYTES, align_bytes=64)
@@ -104,11 +121,14 @@ def tile_list_hail_indemnity_kernel(tc, tab_words, tab_scales, offs, pos1, pos2,
 
         def load_w1(b):
             for a in range(PASSES):
-                w1_raw[a, b] = turns.tile([P, PACK, KP], F32, name="w1_raw%d%d" % (a, b),
-                                          offset=((FIRST_RAW, RAW0), (RAW_BYTES, TAB1 + RAW_BYTES))[a][b])
-                nc.sync.dma_start(
-                    w1_raw[a, b][:],
-                    w1[a * KP:(a + 1) * KP, b * KP:(b + 1) * KP].rearrange("(p j) c -> p j c", j=PACK))
+                parts = 2 if (a, b) == (0, 0) else 1
+                width = KP // parts
+                w1_raw[a, b] = turns.tile([P, parts, PACK, width], F32, name="w1_raw%d%d" % (a, b),
+                                          offset=((FIRST_RAW, TAB1), (RAW1, TAB1 + RAW_BYTES))[a][b])
+                for i in range(parts):
+                    c0 = b * KP + i * width
+                    nc.sync.dma_start(w1_raw[a, b][:, i],
+                                      w1[a * KP:(a + 1) * KP, c0:c0 + width].rearrange("(p j) c -> p j c", j=PACK))
 
         load_w1(0)
         for h in range(2):
@@ -123,9 +143,11 @@ def tile_list_hail_indemnity_kernel(tc, tab_words, tab_scales, offs, pos1, pos2,
         def cast_w1(a, b):
             if a == 0:
                 w1_bf[b] = work.tile([P, PASSES, PACK, P, PACK], BF16, name="w1_bf", tag="w1_bf", bufs=1, align_bytes=64)
-            dst = w1_bf[b][:, a].rearrange("p t m j -> p m j t")
-            src = w1_raw[a, b][:].rearrange("p j (m t) -> p m j t", t=PACK)
-            nc.gpsimd.tensor_scalar(dst, src, 1.0, 0.0, ALU.mult, ALU.add)
+            parts = w1_raw[a, b].shape[1]
+            for i in range(parts):
+                dst = w1_bf[b][:, a, :, i * P // parts:(i + 1) * P // parts].rearrange("p t m j -> p m j t")
+                src = w1_raw[a, b][:, i].rearrange("p j (m t) -> p m j t", t=PACK)
+                nc.gpsimd.tensor_scalar(dst, src, 1.0, 0.0, ALU.mult, ALU.add)
 
         def quant_w1(b):
             codes = keep.tile([P, PASSES * KP], U32, name="w1_codes%d" % b, align_bytes=64)
@@ -143,8 +165,7 @@ def tile_list_hail_indemnity_kernel(tc, tab_words, tab_scales, offs, pos1, pos2,
             if first:
                 sums[kind, s, h] = psum.tile([P, BANK], F32, name="acc", tag="acc")
             if kind == "back":
-                c0 = a * H + s * P
-                lhs = w2c[:, 2 * c0:2 * (c0 + P)].bitcast(FP4X4)
+                lhs = w2c[a, b][:, 2 * t * P:2 * (t + 1) * P].bitcast(FP4X4)
                 lhs_s = w2s[a][:, s * P:(s + 1) * P]
             else:
                 lhs = w1_codes[a, b][:, t * P:(t + 1) * P].bitcast(FP8X4)
@@ -161,19 +182,19 @@ def tile_list_hail_indemnity_kernel(tc, tab_words, tab_scales, offs, pos1, pos2,
         def empty(kind, s, h):
             bank = sums[kind, s, h]
             if (kind, s) == ("back", SLICES - 1) and h == 0:
-                windows[kind, s] = turns.tile([P, S], F32, name="back_last", offset=RAW_BYTES + 12 * M, align_bytes=64)
+                windows[kind, s] = turns.tile([P, S], F32, name="back_last", offset=HELD, align_bytes=64)
             if kind == "hail" and s % PACK == 2 and h == 0:
-                windows[kind, s] = turns.tile([P, S], F32, name="hail%d" % s, offset=RAW0, align_bytes=64)
+                windows[kind, s] = turns.tile([P, S], F32, name="hail%d" % s, offset=TAB1, align_bytes=64)
             if (kind, s) not in windows:
                 windows[kind, s] = work.tile([P, S], F32, name=kind, tag=kind,
                                              bufs=SLICES - 1 if kind == "back" else 3, align_bytes=64)
             dst = windows[kind, s][:, h * BANK:(h + 1) * BANK]
-            if kind == "back" and (s == SLICES - 1 or s in (2, 3) and h == 0):
+            if kind == "back" and (s, h) in ((2, 0), (3, 0), (7, 1)):
                 nc.vector.tensor_copy(dst, bank[:])
             elif kind == "back":
                 nc.scalar.copy(dst, bank[:])
             else:
-                nc.scalar.activation(dst, bank[:], ACT.Abs, scale=inv_half[:, s:s + 1])
+                nc.scalar.activation(dst, bank[:], ACT.Abs)
 
         def rows(kind, s, h):
             multiply(kind, s, h)
@@ -192,23 +213,36 @@ def tile_list_hail_indemnity_kernel(tc, tab_words, tab_scales, offs, pos1, pos2,
             return store[s // 2]
 
         def pick_near(s):
-            if s in (4, 5, 6):
-                near[s] = turns.tile([P, M], F32, name="near%d" % s, offset=RAW_BYTES + 4 * M * (s - 4))
-            else:
-                near[s] = keep.tile([P, M], F32, name="near%d" % s)
-            nc.vector.tensor_copy(near[s][:], windows["back", s][:].indirect(near_list[:]))
+            if s in (4, 6):
+                near[s // 2] = turns.tile([P, 2, M], F32, name="near%d" % s, offset=HELD + 4 * S + 4 * M * (s - 4))
+            elif s in (0, 2):
+                near[s // 2] = keep.tile([P, 2, M], F32, name="near%d" % s)
+            nc.vector.tensor_copy(near[s // 2][:, s % 2, :], windows["back", s][:].indirect(near_list[:]))
 
         def square_near(s):
             if s % PACK == 2:
-                damp[s // 2] = turns.tile([P, 2, M], F32, name="damp%d" % s, offset=RAW0 + 4 * S)
-            nc.scalar.activation(pair_tile(damp, "damp", s, 1)[:, s % 2, :], near[s][:], ACT.Square,
-                                 scale=inv_root[:, s:s + 1])
+                damp[s // 2] = turns.tile([P, 2, M], F32, name="damp%d" % s, offset=TAB1 + 4 * S)
+            dst = pair_tile(damp, "damp", s, 1)
+            if s > 0:
+                nc.scalar.activation(dst[:], near[s // 2][:], ACT.Square)
+                return
+            for u in range(2):
+                nc.scalar.activation(dst[:, u, :], near[0][:, u, :], ACT.Square, scale=inv_root[:, u:u + 1])
 
         def root_pair(s):
-            nc.scalar.activation(damp[s // 2][:], damp[s // 2][:], ACT.Abs_reciprocal_sqrt, bias=1.0)
+            if s == 0:
+                nc.scalar.activation(damp[0][:], damp[0][:], ACT.Abs_reciprocal_sqrt, bias=1.0)
+                return
+            for u in range(2):
+                nc.scalar.activation(damp[s // 2][:, u, :], damp[s // 2][:, u, :], ACT.Abs_reciprocal_sqrt,
+                                     bias=half_col[:, s + u:s + u + 1])
 
         def damp_pair(s, m0=0, m1=M):
-            nc.scalar.activation(damp[s // 2][:, :, m0:m1], damp[s // 2][:, :, m0:m1], ACT.Square)
+            if s > 0:
+                nc.scalar.activation(damp[s // 2][:, :, m0:m1], damp[s // 2][:, :, m0:m1], ACT.Square)
+                return
+            for u in range(2):
+                nc.scalar.activation(damp[0][:, u, :], damp[0][:, u, :], ACT.Square, scale=inv_root[:, u:u + 1])
 
         def pick_field(s, m0=0, m1=M):
             if s == 0:
@@ -257,7 +291,7 @@ def tile_list_hail_indemnity_kernel(tc, tab_words, tab_scales, offs, pos1, pos2,
             late["ded"] = turns.tile([P, NT], F32, name="ded_t", offset=FIRST_RAW + 7680)
             with nc.allow_non_contiguous_dma(reason="one deductible a partition"):
                 nc.sync.dma_start(late["ded"][:], ded.rearrange("(c p) -> p c", p=P))
-            late["w3s"] = turns.tile([P, PASSES * N // 4], I32, name="w3s", offset=TAB1 + 2048, align_bytes=64)
+            late["w3s"] = turns.tile([P, PASSES * N // 4], I32, name="w3s", offset=13 * 1024, align_bytes=64)
             nc.gpsimd.memset(late["w3s"][:], 0)
             late["w3w"] = turns.tile([P, PASSES, N], I32, name="w3_w", offset=FIRST_RAW, align_bytes=64)
             nc.sync.dma_start(late["w3w"][:], w3_words.rearrange("a p c i -> p a (c i)").bitcast(I32))
@@ -268,8 +302,8 @@ def tile_list_hail_indemnity_kernel(tc, tab_words, tab_scales, offs, pos1, pos2,
 
         groups = [range(c0, c0 + 2) for c0 in range(0, NT, 2)]
 
-        def last_pass(b, c):
-            for group in groups:
+        def last_pass(b, c, some=groups):
+            for group in some:
                 if b == 0:
                     loss[c, group[0]] = psum.tile([P, 2, HM], F32, name="acc", tag="acc")
                 for u, n in enumerate(group):
@@ -310,13 +344,12 @@ def tile_list_hail_indemnity_kernel(tc, tab_words, tab_scales, offs, pos1, pos2,
         window("back", 4)
         pick_near(4)
         square_near(0)
-        square_near(1)
         window("back", 5)
         pick_near(5)
         root_pair(0)
         window("back", 6)
-        pick_near(6)
         damp_pair(0)
+        pick_near(6)
         window("back", 7)
         pick_near(7)
         window("hail", 0)
@@ -333,7 +366,6 @@ def tile_list_hail_indemnity_kernel(tc, tab_words, tab_scales, offs, pos1, pos2,
             for u, h in ahead:
                 empty("hail", u, h)
             square_near(s)
-            square_near(s + 1)
             for u, h in between:
                 empty("hail", u, h)
             root_pair(s)
@@ -349,31 +381,38 @@ def tile_list_hail_indemnity_kernel(tc, tab_words, tab_scales, offs, pos1, pos2,
         late["neg"] = keep.tile([P, NT], F32, name="neg_ded")
         nc.scalar.activation(late["neg"][:], late["ded"][:], ACT.Copy, scale=-1.0)
         s6, s7 = SLICES - 2, SLICES - 1
-        round_z(0, 0, False)
-        quant_z(z_sets[0])
-        last_pass(0, 0)
         damp_pair(s6, 0, HM)
         for u in (s6, s7):
             pick_field(u, 0, HM)
         for u in (s6, s7):
             pick_base(u, 0, HM)
-        round_z(0, 1, False)
-        quant_z(z_sets[1])
-        last_pass(0, 1)
+        round_z(0, 0, False)
+        quant_z(z_sets[0])
+        last_pass(0, 0)
         damp_pair(s6, HM, M)
         for u in (s6, s7):
             pick_field(u, HM, M)
-        base = turns.tile([P, 2, HM], F32, name="base_last", offset=RAW_BYTES + 8 * M)
-        for u in (s6, s7):
+        base = turns.tile([P, 2, HM], F32, name="base_last", offset=HELD + 4 * S + 8 * M)
+
+        def pick_base_plain(u):
             nc.scalar.activation(base[:, u % 2, :], windows["back", u][:].indirect(base_list[:, HM // 16:]), ACT.Copy)
-        nc.vector.tensor_tensor(negz[1][:, 2:, HM:], base[:], ratio[s6 // 2][:, :, HM:], ALU.subtract)
+
+        pick_base_plain(s6)
         round_z(1, 0, False)
         quant_z(z_sets[2])
         last_pass(1, 0)
+        pick_base_plain(s7)
+        nc.vector.tensor_tensor(negz[1][:, 2:, HM:], base[:], ratio[s6 // 2][:, :, HM:], ALU.subtract)
+        finish(0, groups[0], True)
         round_z(1, 1, True)
+        round_z(0, 1, False)
+        quant_z(z_sets[1])
+        last_pass(0, 1, groups[:2])
         quant_z(z_sets[3])
-        last_pass(1, 1)
-        for group in groups:
-            finish(0, group, group[-1] == NT - 1)
+        last_pass(1, 1, groups[:2])
+        last_pass(0, 1, groups[2:])
+        last_pass(1, 1, groups[2:])
+        for group in groups[1:]:
+            finish(0, group, False)
         for group in groups:
             finish(1, group, True)

from contextlib import ExitStack

import concourse.mybir as mybir

K, T, S, M, H, N = 1024, 4096, 1024, 512, 1024, 768
FLOPS = 2 * K * H * S * 2 + 2 * H * N * M

F32 = mybir.dt.float32
BF16 = mybir.dt.bfloat16
I32 = mybir.dt.int32
U32 = mybir.dt.uint32
U16 = mybir.dt.uint16
U8 = mybir.dt.uint8
FP8X4 = mybir.dt.float8_e4m3fn_x4
FP4X4 = mybir.dt.float4_e2m1fn_x4
ACT = mybir.ActivationFunctionType
ALU = mybir.AluOpType

P = 128
PACK = 4
KP = P * PACK
BANK = 512
PASSES = K // KP
GROUPS = H // KP
SLICES = GROUPS * PACK
NT = N // P
HM = M // 2
TAB_BYTES = 4 * T
RAW_BYTES = 4 * PACK * KP
TAB1 = TAB_BYTES
TAB_ROWS = 2 * TAB_BYTES
RAW0 = 0
W2_LATE = TAB_ROWS + 4 * H
W2_EARLY = W2_LATE + 5 * H // 2
FIRST_RAW = W2_LATE + 3 * H
RAW1 = 4096
HELD = 64


def tile_list_hail_indemnity_kernel(tc, tab_words, tab_scales, offs, pos1, pos2, pos3, w1,
                                                 w2_words, w2_scales, half, w3_words, w3_scales, ded, out):
    nc = tc.nc
    with ExitStack() as ctx:
        keep = ctx.enter_context(tc.tile_pool(name="keep", bufs=1))
        turns = ctx.enter_context(tc.tile_pool(name="turns", bufs=1))
        work = ctx.enter_context(tc.tile_pool(name="work", bufs=2))
        psum = ctx.enter_context(tc.psum_pool(name="psum", bufs=8))

        tab_rows = turns.tile([P, T // 4], I32, name="tab_rows", offset=TAB1 + T, align_bytes=64)
        nc.vector.memset(tab_rows[32:64, :], 0)
        nc.vector.memset(tab_rows[64:P, :], 0)
        half_t = keep.tile([P, GROUPS, PACK], F32, name="half_t")
        nc.gpsimd.dma_start(half_t[:], half.rearrange("(b p t) -> p b t", b=GROUPS, t=PACK))
        w2s_rows = turns.tile([P, H // 4], I32, name="w2s_rows", offset=TAB_ROWS - H // 2, align_bytes=64)
        nc.gpsimd.memset(w2s_rows[32:64, :], 0)
        nc.gpsimd.memset(w2s_rows[64:P, :], 0)
        planes = keep.tile([P, PASSES, (S + H) // 4], I32, name="planes", align_bytes=64)
        nc.gpsimd.memset(planes[:], 0)

        lists = {}

        def load_list(name, src):
            lists[name] = keep.tile([P, src.shape[1]], U16, name=name + "_t")
            nc.sync.dma_start(lists[name][:], src)

        load_list("offs", offs)
        nc.sync.dma_start(tab_rows[0:32, :], tab_scales.bitcast(I32).rearrange("a q t -> q a t"))
        nc.sync.dma_start(w2s_rows[0:32, :], w2_scales.bitcast(I32).rearrange("a q c -> q a c"))
        w2_i32 = w2_words.bitcast(I32)
        w2_early = turns.tile([P, KP // 2], I32, name="w2_early", offset=W2_EARLY, align_bytes=64)
        nc.sync.dma_start(w2_early[:], w2_i32[0, :, :KP // 2])
        load_list("pos2", pos2)
        load_list("pos1", pos1)
        load_list("pos3", pos3)
        offs_t, near_list, field_list, base_list = lists["offs"], lists["pos2"], lists["pos1"], lists["pos3"]
        tab_w = [turns.tile([P, T], I32, name="tab_w0", offset=0, align_bytes=64)]
        nc.sync.dma_start(tab_w[0][:], tab_words[0].rearrange("p t i -> p (t i)").bitcast(I32))
        half_col = half_t[:].rearrange("p b t -> p (b t)")
        inv_root = keep.tile([P, 2], F32, name="inv_root")
        nc.scalar.activation(inv_root[:], half_col[:, :2], ACT.Abs_reciprocal_sqrt)

        staged = keep.tile([P, (S + H) // 4], I32, name="staged", align_bytes=64)
        nc.gpsimd.tensor_copy(
            staged[:, S // 4:].bitcast(U8).rearrange("p (g t m n) -> p g m t n", t=PACK, m=P // 16, n=16),
            w2s_rows[:].bitcast(U8).rearrange("p (g m n t) -> p g m t n", t=PACK, m=P // 16, n=16))
        v_rows = turns.tile([P, S // 4], I32, name="v_rows", offset=TAB1, align_bytes=64)
        nc.vector.tensor_copy(v_rows[:].bitcast(U8), tab_rows[:].bitcast(U8).indirect(offs_t[:]))
        nc.vector.tensor_copy(staged[:, :S // 4], v_rows[:])
        for q in range(4):
            nc.sync.dma_start(planes[32 * q:32 * q + 4], staged[8 * q:8 * q + 8, :])
        tab_w.append(turns.tile([P, T], I32, name="tab_w1", offset=TAB1, align_bytes=64))
        nc.sync.dma_start(tab_w[1][:], tab_words[1].rearrange("p t i -> p (t i)").bitcast(I32))
        v_planes = [planes[:, a, :S // 4] for a in range(PASSES)]
        w2s = [planes[:, a, S // 4:].bitcast(U8) for a in range(PASSES)]

        w2c = {}

        def deal_w2(parts, raw, copy):
            dealt = turns.tile([P, len(parts) * KP * 2], U8, name="w2c%d" % len(w2c), offset=TAB_ROWS + len(w2c) * H,
                               align_bytes=64)
            copy(dealt[:].bitcast(U16).rearrange("p (g t m n) -> p g m t n", t=PACK, m=P // 8, n=8),
                 raw.bitcast(U16).rearrange("p (g m n t) -> p g m t n", t=PACK, m=P // 8, n=8))
            for i, part in enumerate(parts):
                w2c[part] = dealt[:, i * 2 * KP:(i + 1) * 2 * KP]

        deal_w2([(0, 0)], w2_early[:], nc.vector.tensor_copy)
        w2_late = turns.tile([P, 3 * KP // 2], I32, name="w2_late", offset=W2_LATE, align_bytes=64)
        nc.sync.dma_start(w2_late[:, :KP // 2], w2_i32[1, :, :KP // 2])
        nc.sync.dma_start(w2_late[:, KP // 2:].rearrange("p (a c) -> p a c", a=PASSES),
                          w2_i32[:, :, KP // 2:].rearrange("a p c -> p a c"))
        deal_w2([(1, 0)], w2_late[:, :KP // 2], nc.scalar.copy)
        deal_w2([(0, 1), (1, 1)], w2_late[:, KP // 2:], nc.scalar.copy)

        v_words = {}
        whole = turns.tile([P, S], I32, name="v_words0", offset=FIRST_RAW + RAW_BYTES, align_bytes=64)
        nc.vector.tensor_copy(whole[:].bitcast(U32), tab_w[0][:].bitcast(U32).indirect(offs_t[:]))
        for h in range(2):
            v_words[0, h] = whole[:, h * BANK:(h + 1) * BANK]

        w1_raw = {}

        def load_w1(b):
            for a in range(PASSES):
                parts = 2 if (a, b) == (0, 0) else 1
                width = KP // parts
                w1_raw[a, b] = turns.tile([P, parts, PACK, width], F32, name="w1_raw%d%d" % (a, b),
                                          offset=((FIRST_RAW, TAB1), (RAW1, TAB1 + RAW_BYTES))[a][b])
                for i in range(parts):
                    c0 = b * KP + i * width
                    nc.sync.dma_start(w1_raw[a, b][:, i],
                                      w1[a * KP:(a + 1) * KP, c0:c0 + width].rearrange("(p j) c -> p j c", j=PACK))

        load_w1(0)
        for h in range(2):
            part = keep.tile([P, BANK], I32, name="v_words1%d" % h, align_bytes=64)
            nc.vector.tensor_copy(part[:].bitcast(U32),
                                  tab_w[1][:].bitcast(U32).indirect(offs_t[:, h * 32:(h + 1) * 32]))
            v_words[1, h] = part[:]
        load_w1(1)

        w1_bf, w1_codes, w1_scales = {}, {}, {}

        def cast_w1(a, b):
            if a == 0:
                w1_bf[b] = work.tile([P, PASSES, PACK, P, PACK], BF16, name="w1_bf", tag="w1_bf", bufs=1, align_bytes=64)
            parts = w1_raw[a, b].shape[1]
            for i in range(parts):
                dst = w1_bf[b][:, a, :, i * P // parts:(i + 1) * P // parts].rearrange("p t m j -> p m j t")
                src = w1_raw[a, b][:, i].rearrange("p j (m t) -> p m j t", t=PACK)
                nc.gpsimd.tensor_scalar(dst, src, 1.0, 0.0, ALU.mult, ALU.add)

        def quant_w1(b):
            codes = keep.tile([P, PASSES * KP], U32, name="w1_codes%d" % b, align_bytes=64)
            scales = keep.tile([P, PASSES * KP], U8, name="w1_scales%d" % b, align_bytes=64)
            nc.vector.quantize_mx(out=codes[:].bitcast(FP8X4), scales=scales[:],
                                  in_=w1_bf[b][:].rearrange("p a t m j -> p (a t m j)"))
            for a in range(PASSES):
                w1_codes[a, b] = codes[:, a * KP:(a + 1) * KP]
                w1_scales[a, b] = scales[:, a * KP:(a + 1) * KP]

        windows, sums = {}, {}

        def one_pass(kind, s, h, a, first):
            b, t = divmod(s, PACK)
            if first:
                sums[kind, s, h] = psum.tile([P, BANK], F32, name="acc", tag="acc")
            if kind == "back":
                lhs = w2c[a, b][:, 2 * t * P:2 * (t + 1) * P].bitcast(FP4X4)
                lhs_s = w2s[a][:, s * P:(s + 1) * P]
            else:
                lhs = w1_codes[a, b][:, t * P:(t + 1) * P].bitcast(FP8X4)
                lhs_s = w1_scales[a, b][:, t * P:(t + 1) * P]
            nc.tensor.matmul_mx(out=sums[kind, s, h][:], lhsT=lhs, lhsT_scale=lhs_s,
                                rhs=v_words[a, h].bitcast(FP8X4),
                                rhs_scale=v_planes[a].bitcast(U8)[:, h * BANK:(h + 1) * BANK],
                                start=first, stop=not first)

        def multiply(kind, s, h):
            for a in range(PASSES):
                one_pass(kind, s, h, a, a == 0)

        def empty(kind, s, h):
            bank = sums[kind, s, h]
            if (kind, s) == ("back", SLICES - 1) and h == 0:
                windows[kind, s] = turns.tile([P, S], F32, name="back_last", offset=HELD, align_bytes=64)
            if kind == "hail" and s % PACK == 2 and h == 0:
                windows[kind, s] = turns.tile([P, S], F32, name="hail%d" % s, offset=TAB1, align_bytes=64)
            if (kind, s) not in windows:
                windows[kind, s] = work.tile([P, S], F32, name=kind, tag=kind,
                                             bufs=SLICES - 1 if kind == "back" else 3, align_bytes=64)
            dst = windows[kind, s][:, h * BANK:(h + 1) * BANK]
            if kind == "back" and (s, h) in ((2, 0), (3, 0), (7, 1)):
                nc.vector.tensor_copy(dst, bank[:])
            elif kind == "back":
                nc.scalar.copy(dst, bank[:])
            else:
                nc.scalar.activation(dst, bank[:], ACT.Abs)

        def rows(kind, s, h):
            multiply(kind, s, h)
            empty(kind, s, h)

        def window(kind, s):
            for h in range(2):
                rows(kind, s, h)

        negz = [keep.tile([P, PACK, M], F32, name="negz%d" % b, align_bytes=64) for b in range(GROUPS)]
        near, damp, ratio = {}, {}, {}

        def pair_tile(store, name, s, bufs):
            if s // 2 not in store:
                store[s // 2] = work.tile([P, 2, M], F32, name=name, tag=name, bufs=bufs)
            return store[s // 2]

        def pick_near(s):
            if s in (4, 6):
                near[s // 2] = turns.tile([P, 2, M], F32, name="near%d" % s, offset=HELD + 4 * S + 4 * M * (s - 4))
            elif s in (0, 2):
                near[s // 2] = keep.tile([P, 2, M], F32, name="near%d" % s)
            nc.vector.tensor_copy(near[s // 2][:, s % 2, :], windows["back", s][:].indirect(near_list[:]))

        def square_near(s):
            if s % PACK == 2:
                damp[s // 2] = turns.tile([P, 2, M], F32, name="damp%d" % s, offset=TAB1 + 4 * S)
            dst = pair_tile(damp, "damp", s, 1)
            if s > 0:
                nc.scalar.activation(dst[:], near[s // 2][:], ACT.Square)
                return
            for u in range(2):
                nc.scalar.activation(dst[:, u, :], near[0][:, u, :], ACT.Square, scale=inv_root[:, u:u + 1])

        def root_pair(s):
            if s == 0:
                nc.scalar.activation(damp[0][:], damp[0][:], ACT.Abs_reciprocal_sqrt, bias=1.0)
                return
            for u in range(2):
                nc.scalar.activation(damp[s // 2][:, u, :], damp[s // 2][:, u, :], ACT.Abs_reciprocal_sqrt,
                                     bias=half_col[:, s + u:s + u + 1])

        def damp_pair(s, m0=0, m1=M):
            if s > 0:
                nc.scalar.activation(damp[s // 2][:, :, m0:m1], damp[s // 2][:, :, m0:m1], ACT.Square)
                return
            for u in range(2):
                nc.scalar.activation(damp[0][:, u, :], damp[0][:, u, :], ACT.Square, scale=inv_root[:, u:u + 1])

        def pick_field(s, m0=0, m1=M):
            if s == 0:
                ratio[0] = turns.tile([P, 2, M], F32, name="ratio01", offset=TAB1 + RAW_BYTES)
            nc.vector.tensor_tensor(pair_tile(ratio, "ratio", s, 2)[:, s % 2, m0:m1],
                                    windows["hail", s][:].indirect(field_list[:, m0 // 16:m1 // 16]),
                                    damp[s // 2][:, s % 2, m0:m1], ALU.mult)

        def pick_base(s, m0=0, m1=M):
            nc.vector.tensor_tensor(negz[s // PACK][:, s % PACK, m0:m1],
                                    windows["back", s][:].indirect(base_list[:, m0 // 16:m1 // 16]),
                                    ratio[s // 2][:, s % 2, m0:m1], ALU.subtract)

        z_sets = ((0,), (1,), (2,), (3,))
        z_bf, z_codes, z_scales = {}, {}, {}
        for pieces in z_sets:
            codes = keep.tile([P, len(pieces), HM], U32, name="z_codes%d" % pieces[0], align_bytes=64)
            scales = keep.tile([P, len(pieces), HM], U8, name="z_scales%d" % pieces[0], align_bytes=64)
            z_codes[pieces], z_scales[pieces] = codes, scales
        for u in range(2):
            z_bf[u,] = keep.tile([P, 1, HM, PACK], BF16, name="z_bf0%d" % u, align_bytes=64)

        def piece(store, b, c):
            pieces = [q for q in z_sets if 2 * b + c in q][0]
            return store[pieces][:, pieces.index(2 * b + c)]

        def round_z(b, c, on_vector):
            if b == 1:
                z_bf[2 * b + c,] = work.tile([P, 1, HM, PACK], BF16, name="z_bf1", tag="z_bf1", bufs=1, align_bytes=64)
            dst = piece(z_bf, b, c).rearrange("p (c i) t -> p c t i", i=4)
            src = negz[b][:, :, c * HM:(c + 1) * HM].rearrange("p t (c i) -> p c t i", i=4)
            if on_vector:
                nc.vector.tensor_scalar(dst, src, -1.0, None, ALU.mult)
            else:
                nc.scalar.activation(dst, src, ACT.Copy, scale=-1.0)

        def quant_z(pieces):
            nc.vector.quantize_mx(out=z_codes[pieces][:].rearrange("p u m -> p (u m)").bitcast(FP8X4),
                                  scales=z_scales[pieces][:].rearrange("p u m -> p (u m)"),
                                  in_=z_bf[pieces][:].rearrange("p u m t -> p (u m t)"))

        loss = {}
        late = {}

        def load_last():
            late["ded"] = turns.tile([P, NT], F32, name="ded_t", offset=FIRST_RAW + 7680)
            with nc.allow_non_contiguous_dma(reason="one deductible a partition"):
                nc.sync.dma_start(late["ded"][:], ded.rearrange("(c p) -> p c", p=P))
            late["w3s"] = turns.tile([P, PASSES * N // 4], I32, name="w3s", offset=13 * 1024, align_bytes=64)
            nc.gpsimd.memset(late["w3s"][:], 0)
            late["w3w"] = turns.tile([P, PASSES, N], I32, name="w3_w", offset=FIRST_RAW, align_bytes=64)
            nc.sync.dma_start(late["w3w"][:], w3_words.rearrange("a p c i -> p a (c i)").bitcast(I32))
            for q in range(4):
                nc.sync.dma_start(
                    late["w3s"][32 * q:32 * q + 4, :].rearrange("r (a c) -> r a c", a=PASSES),
                    w3_scales.bitcast(I32)[:, 4 * q:4 * q + 4, :].rearrange("a r c -> r a c"))

        groups = [range(c0, c0 + 2) for c0 in range(0, NT, 2)]

        def last_pass(b, c, some=groups):
            for group in some:
                if b == 0:
                    loss[c, group[0]] = psum.tile([P, 2, HM], F32, name="acc", tag="acc")
                for u, n in enumerate(group):
                    nc.tensor.matmul_mx(out=loss[c, group[0]][:, u, :],
                                        lhsT=late["w3w"][:, b, n * P:(n + 1) * P].bitcast(FP8X4),
                                        lhsT_scale=late["w3s"][:].bitcast(U8)[:, b * N + n * P:b * N + (n + 1) * P],
                                        rhs=piece(z_codes, b, c).bitcast(FP8X4), rhs_scale=piece(z_scales, b, c),
                                        start=(b == 0 and u == 0), stop=(b == 1 and u == 1))

        def finish(c, group, on_vector):
            n0 = group[0]
            acc = loss[c, n0]
            res = keep.tile([P, 2, HM], F32, name="res%d_%d" % (c, n0), align_bytes=64)
            if on_vector:
                nc.vector.tensor_tensor(res[:], acc[:],
                                        late["ded"][:, n0:n0 + 2].unsqueeze(2).to_broadcast([P, 2, HM]), ALU.max)
            else:
                over = work.tile([P, 2, HM], F32, name="over", tag="over", bufs=2)
                for u, n in enumerate(group):
                    nc.scalar.activation(over[:, u, :], acc[:, u, :], ACT.Relu, bias=late["neg"][:, n:n + 1])
                for u, n in enumerate(group):
                    nc.scalar.activation(res[:, u, :], over[:, u, :], ACT.Identity, bias=late["ded"][:, n:n + 1])
            nc.sync.dma_start(out[n0 * P:(n0 + 2) * P, c * HM:(c + 1) * HM].rearrange("(u p) m -> p u m", p=P), res[:])

        opened = [(s, h) for h in range(2) for s in range(4)]
        for s, h in opened:
            one_pass("back", s, h, 0, True)
        for s, h in opened:
            one_pass("back", s, h, 1, False)
        for s, h in opened:
            empty("back", s, h)
        for s in range(4):
            pick_near(s)
        for b in range(GROUPS):
            for a in range(PASSES):
                cast_w1(a, b)
            quant_w1(b)
        window("back", 4)
        pick_near(4)
        square_near(0)
        window("back", 5)
        pick_near(5)
        root_pair(0)
        window("back", 6)
        damp_pair(0)
        pick_near(6)
        window("back", 7)
        pick_near(7)
        window("hail", 0)
        window("hail", 1)
        for s in (0, 1):
            pick_field(s)
        for s in (0, 1):
            pick_base(s)
        for s in range(2, SLICES, 2):
            banks = [(u, h) for u in (s, s + 1) for h in range(2)]
            ahead, between, behind = (banks[2:], banks[:1], banks[1:2]) if s == 2 else ([], banks[:2], banks[2:])
            for u, h in ahead + between + behind:
                multiply("hail", u, h)
            for u, h in ahead:
                empty("hail", u, h)
            square_near(s)
            for u, h in between:
                empty("hail", u, h)
            root_pair(s)
            for u, h in behind:
                empty("hail", u, h)
            if s + 2 < SLICES:
                damp_pair(s)
                for u in (s, s + 1):
                    pick_field(u)
                for u in (s, s + 1):
                    pick_base(u)
        load_last()
        late["neg"] = keep.tile([P, NT], F32, name="neg_ded")
        nc.scalar.activation(late["neg"][:], late["ded"][:], ACT.Copy, scale=-1.0)
        s6, s7 = SLICES - 2, SLICES - 1
        damp_pair(s6, 0, HM)
        for u in (s6, s7):
            pick_field(u, 0, HM)
        for u in (s6, s7):
            pick_base(u, 0, HM)
        round_z(0, 0, False)
        quant_z(z_sets[0])
        last_pass(0, 0)
        damp_pair(s6, HM, M)
        for u in (s6, s7):
            pick_field(u, HM, M)
        base = turns.tile([P, 2, HM], F32, name="base_last", offset=HELD + 4 * S + 8 * M)

        def pick_base_plain(u):
            nc.scalar.activation(base[:, u % 2, :], windows["back", u][:].indirect(base_list[:, HM // 16:]), ACT.Copy)

        pick_base_plain(s6)
        round_z(1, 0, False)
        quant_z(z_sets[2])
        last_pass(1, 0)
        pick_base_plain(s7)
        nc.vector.tensor_tensor(negz[1][:, 2:, HM:], base[:], ratio[s6 // 2][:, :, HM:], ALU.subtract)
        finish(0, groups[0], True)
        round_z(1, 1, True)
        round_z(0, 1, False)
        quant_z(z_sets[1])
        last_pass(0, 1, groups[:2])
        quant_z(z_sets[3])
        last_pass(1, 1, groups[:2])
        last_pass(0, 1, groups[2:])
        last_pass(1, 1, groups[2:])
        for group in groups[1:]:
            finish(0, group, False)
        for group in groups:
            finish(1, group, True)
